import numpy as np, ml_dtypes
CORES = [8,136,40,168]
N = 4
BF = ml_dtypes.bfloat16
W, L, CAP, T, D = 4096, 256, 2, 5, 3
def place(s, p):
    return ((((s & 4095) * (2 * p + 1)) >> 3) + 37 * s + 613 * p) & (W - 1)
def cells(lf, p):
    return place((32768 + lf)[..., None] >> np.arange(16), p[..., None])
def page(w, z):
    return np.add.reduce(w[..., 0:1] * z, axis=-2) & 255
def pack(x, c, z, lf, w, th):
    return {"x0": x.reshape(N, 128, W).astype(np.float32).astype(BF), "c0": c.reshape(N, 8, W).astype(np.float32).astype(BF), "z0": z.reshape(N, 128, L).astype(np.float32).astype(BF),
            "leaf": np.ascontiguousarray(lf).astype(np.int32), "wt": np.ascontiguousarray(w.reshape(N, 128, 2)).astype(np.int32), "th": np.ascontiguousarray(th.reshape(N, 8, 1)).astype(np.int32)}
def parts(rng):
    x = rng.integers(0, 16, (N, 8, 16, W)); c = rng.integers(0, CAP, (N, 8, W))
    pool = rng.integers(0, 16, (N, 8, 16, 64)); z = np.take_along_axis(pool, rng.integers(0, 64, (N, 8, 1, L)), 3)
    z = np.where(rng.random((N, 8, 1, L)) < 0.5, z, rng.integers(0, 16, (N, 8, 16, L)))
    few = rng.integers(0, 32768, (N, 8, 16)); lf = np.take_along_axis(few, rng.integers(0, 16, (N, 8, L)), 2)
    lf = np.where(rng.random((N, 8, L)) < 0.25, lf, rng.integers(0, 32768, (N, 8, L)))
    return x, c, z, lf, rng.integers(1, 256, (N, 8, 16, 2)), rng.integers(50, 81, (N, 8))
def setup_inputs(rng):
    return pack(*parts(rng))
def setup_inputs_spread(rng):
    def uneven(n):
        v = np.minimum((np.exp2(4 * rng.random((N, 8, 1, n))) * rng.random((N, 8, 16, n))).astype(np.int64), 15)
        return np.where(rng.random((N, 8, 1, n)) < 0.5, v, 15 - v)
    c = np.where(rng.random((N, 8, W)) < rng.random((N, 8, 1)), CAP - 1, rng.integers(0, CAP, (N, 8, W)))
    lf = np.minimum(np.exp2(15 * rng.random((N, 8, L))).astype(np.int64), 32767)
    w = np.minimum(np.maximum(np.exp2(8 * rng.random((N, 8, 16, 2))).astype(np.int64), 1), 255)
    return pack(uneven(W), c, uneven(L), lf, w, rng.integers(0, 121, (N, 8)))
def setup_inputs_ends(rng):
    def ends(n):
        one = rng.integers(0, 2, (N, 8, 1, n)); el = rng.integers(0, 2, (N, 8, 16, n))
        return np.where(rng.random((N, 8, 1, n)) < 0.5, one, el) * 15
    x = ends(W); z = ends(L); c = (CAP - 1) * rng.integers(0, 2, (N, 8, W)); lf = 32767 * rng.integers(0, 2, (N, 8, L))
    w = 1 + 254 * rng.integers(0, 2, (N, 8, 16, 2)); w[:, 1::3] = 255; w[:, 0, 0] = 1; w[:, 0, 15] = 255
    th = 120 * ((np.arange(8)[None, :] + rng.integers(0, 2, (N, 1))) & 1)
    for q in range(N):
        for g in range(8):
            if g % 3 == 1:
                z[q, g][:, [1, L - 2]] = 15; lf[q, g, [1, L - 2]] = 32767
                x[q, g][:, cells(np.array([32767]), np.array([(16 * 15 * 255) & 255]))[0]] = 0
            z[q, g][:, [2, L - 3]] = 0; lf[q, g, [2, L - 3]] = 0
            order = rng.permutation(16)
            for m in (16, 0) + tuple(range(1, 16)):
                v = 15 * (order < m).astype(np.int64); p = int(np.dot(w[q, g, :, 0], v)) & 255
                k = np.flatnonzero(place(32768 + np.arange(32768), p) == W - 1)
                if k.size:
                    lone = int(rng.choice(k))
                    z[q, g][:, [0, L - 1]] = v[:, None]; lf[q, g, [0, L - 1]] = lone
                    x[q, g][:, W - 1] = v if (q + g) % 2 == 0 else 15 - v
                    above = int(place((32768 + lone) >> 1, p))
                    if (q + g) % 2 == 1 and above != W - 1:
                        x[q, g][:, above] = v; c[q, g, W - 1] = CAP - 1
                    break
    return pack(x, c, z, lf, w, th)
def near(z, n):
    i = np.arange(16)[:, None]; d = (n >> 4)[None, :] + (i < (n & 15)[None, :])
    return np.where(z < 8, z + d, z - d)
def setup_inputs_corners(rng):
    x, c, z, lf, w, th = parts(rng)
    th = rng.choice(np.array([0, 1, 20, 40, 120]), (N, 8)); kind = (np.arange(8)[None, :] + rng.integers(0, 3, (N, 1))) % 3
    c = np.where(kind[:, :, None] == 0, 0, np.where(kind[:, :, None] == 1, CAP - 1, c))
    lf = np.where(rng.random((N, 8, L)) < 0.5, rng.choice(np.array([0, 1, 16383, 16384, 32766, 32767]), (N, 8, L)), lf); lf[:, :, 0] = 0; lf[:, :, L - 1] = 32767
    wk = rng.integers(0, 4, (N, 8, 1, 2)); w = np.where(wk == 0, 1, np.where(wk == 1, 255, w))
    zk = rng.random((N, 8, 1, L)); z = np.where(zk < 0.05, 0, np.where(zk > 0.95, 15, z))
    for q in range(N):
        for g in range(8):
            h = cells(lf[q, g], page(w[q, g], z[q, g]))
            lv = rng.choice(np.array([0, 1, 7, 14]), L); n = np.maximum(th[q, g] + rng.integers(-1, 2, L), 0)
            x[q, g][:, h[np.arange(L), lv]] = near(z[q, g], n)
            e = np.array([th[q, g], th[q, g] + 1])
            x[q, g][:, h[[0, L - 1], 0]] = near(z[q, g][:, [0, L - 1]], e)
    return pack(x, c, z, lf, w, th)
def setup_inputs_crowd(rng):
    x, c, z, lf, w, th = parts(rng)
    for q in range(N):
        if q % 3 < 2:
            x[q] = rng.integers(0, 4, (8, 16, W)); z[q] = rng.integers(12, 16, (8, 16, L)); th[q] = rng.integers(0, 61, 8)
        lone = 0 if q & 1 else L - 1
        for g in range(8):
            if g % 4 == 0: ix = np.full(L, int(rng.integers(0, L)))
            elif g % 4 == 1: ix = np.full(L, lone ^ 1); ix[lone] = lone
            elif g % 4 == 2: ix = rng.integers(0, 4, L)
            else: ix = np.arange(L)
            z[q, g] = z[q, g][:, ix]; lf[q, g] = lf[q, g][ix]
            if q % 3 == 1 and g == 1:
                pg = page(w[q, g], z[q, g]); other = cells(lf[q, g, [lone ^ 1]], pg[[lone ^ 1]])[0]
                some = rng.permutation(32768)[:256]; hs = place(32768 + some, pg[lone])
                k = int(np.argmax(~np.isin(hs, other)))
                lf[q, g, lone] = some[k]; x[q, g][:, hs[k]] = z[q, g][:, lone]
    return pack(x, c, z, lf, w, th)
def setup_inputs_full(rng):
    x, c, z, lf, w, th = parts(rng); th = rng.integers(0, 9, (N, 8)); c[:, [0, 1, 4, 5]] = CAP - 1
    for q in range(N):
        for g in range(8):
            a, b = rng.permutation(16)[:2]; w[q, g, a, 0] = 1; w[q, g, b, 0] = 16
            zz = rng.integers(0, 16, (16, L)); zz[[a, b]] = 0
            pg = np.full(L, int(rng.integers(0, 256))) if g % 4 == 3 else rng.permutation(256)[:L]
            left = (pg - page(w[q, g], zz)) & 255; zz[a] = left & 15; zz[b] = left >> 4; z[q, g] = zz
            cand = rng.integers(0, 32768, (L, 24)); lv = rng.integers(1, 16, (L, 24))
            if g % 2 == 0: lv[:, :16] = 15
            h = cells(cand, pg[:, None]).tolist(); lv = lv.tolist(); taken = set(); hits = set(); at = []; who = []
            for l in range(L):
                for m in range(24):
                    v = lv[l][m]; way = h[l][m]
                    if way[v - 1] not in taken and (v == 15 or (way[v] not in hits and way[v] not in way[:v])): break
                lf[q, g, l] = cand[l, m]; taken.add(way[v - 1])
                if v < 15: hits.add(way[v]); at.append(way[v]); who.append(l)
            if at: x[q, g][:, np.array(at)] = near(zz[:, np.array(who)], rng.integers(0, int(th[q, g]) + 1, len(at)))
    return pack(x, c, z, lf, w, th)
def check_inputs(d):
    bad = []
    for k, lo, hi in (("x0", 0, 15), ("c0", 0, CAP - 1), ("z0", 0, 15), ("leaf", 0, 32767), ("wt", 1, 255), ("th", 0, 120)):
        a = np.asarray(d[k]).astype(np.float64)
        if not (np.min(a) >= lo and np.max(a) <= hi): bad.append("range of " + k)
        elif np.any(a != np.floor(a)): bad.append("whole numbers in " + k)
    return bad
def reference(x0, c0, z0, leaf, wt, th):
    X = x0.astype(np.float32).astype(np.int64).reshape(N, 8, 16, W); C = c0.astype(np.float32).astype(np.int64).reshape(N, 8, W)
    z = z0.astype(np.float32).astype(np.int64).reshape(N, 8, 16, L); lf = leaf.astype(np.int64)
    w = wt.astype(np.int64).reshape(N, 8, 16, 2); lim = th.astype(np.int64).reshape(N, 8, 1, 1); A = np.zeros(N, np.int64); zs = []
    for t in range(T):
        home = (np.arange(N) - D * t) % N
        zq = z[home]; lq = lf[home]
        h = cells(lq, page(w, zq))
        xk = np.take_along_axis(X, h.reshape(N, 8, 1, L * 16), 3).reshape(N, 8, 16, L, 16)
        dist = np.add.reduce(np.abs(xk - zq[..., None]), axis=2)
        hit = dist <= lim + (A & 15).reshape(N, 1, 1, 1); hit[..., 15] = True
        j = np.argmax(hit, axis=-1)
        y = np.take_along_axis(xk, j[:, :, None, :, None], 4)[..., 0]
        for q in range(N):
            for g in range(8):
                m = np.flatnonzero(j[q, g] > 0); named = h[q, g, m, j[q, g, m] - 1]
                cell, first = np.unique(named, return_index=True); who = m[first]
                C[q, g, cell] += 1; full = C[q, g, cell] == CAP
                X[q, g][:, cell[full]] = y[q, g][:, who[full]]; C[q, g, cell[full]] = 0
                cell, first = np.unique(h[q, g, :, 15], return_index=True)
                X[q, g][:, cell] = (xk[q, g][:, first, 15] + zq[q, g][:, first]) >> 1
        A = np.add.reduce((j == 15).astype(np.int64).reshape(N, 8 * L), axis=1)
        zq = np.abs(zq - y); z = np.zeros_like(zq); z[home] = zq; zs.append(z)
        if t < T - 1: lf[home] = (8 * lq + np.add.reduce(w[..., 1:2] * zq, axis=2)) & 32767
    return {"zs": np.concatenate(zs, axis=3).reshape(N, 128, T * L).astype(np.float32).astype(BF), "xs": np.add.reduce(w[..., 0:1] * X, axis=2).astype(np.float32), "cs": C.astype(np.float32)}

@@ -1,0 +1,537 @@
+from concourse.mybir import AluOpType, AxisListType, ActivationFunctionType
+
+ALU = AluOpType
+ACT = ActivationFunctionType
+W, L, STEPS, D = 4096, 256, 5, 3
+XW = 16 + W + L
+BIG = float(2 ** 46)
+MAGIC = 1.5 * 2 ** 23
+SILU_ONE = 1.2784645427610738
+S_GATH = [(0, 64), (64, 128), (128, 192)]
+V_GATH = [(192, 256)]
+CHUNKS = [(192, 256), (0, 64), (64, 128), (128, 192)]
+ROOT = (0, 3, 16)
+SU_FIRST = True
+C_S, C_V = 1280, 1600
+
+SCRATCH = {
+    "X": ("sbuf", [128, XW], "float32"), "C": ("sbuf", [128, XW], "float32"),
+    "xk": ("sbuf", [128, W], "bfloat16"), "mx": ("sbuf", [128, W], "bfloat16"), "xb": ("sbuf", [128, W], "bfloat16"),
+    "E": ("sbuf", [128, 16, 256], "bfloat16"),
+    "zin": ("sbuf", [128, 5 * L], "bfloat16"), "zout": ("sbuf", [128, 5 * L], "bfloat16"),
+    "zhome": ("sbuf", [128, 2 * L], "bfloat16"),
+    "fin": ("sbuf", [128, 4 * L], "float32"), "fout": ("sbuf", [128, 4 * L], "float32"),
+    "LI": ("sbuf", [128, 264], "int32"), "LF": ("sbuf", [128, 264], "float32"),
+    "wi": ("sbuf", [128, 2], "int32"), "wf": ("sbuf", [128, 2], "float32"),
+    "Bm": ("sbuf", [128, 128], "bfloat16"), "Bin": ("sbuf", [128, 128], "bfloat16"),
+    "pI": ("sbuf", [128, 4], "int32"), "col": ("sbuf", [128, 32], "float32"),
+    "im": ("sbuf", [128, 144], "bfloat16"), "ig": ("sbuf", [128, 128], "bfloat16"),
+    "ic": ("sbuf", [128, L], "bfloat16"),
+    "ib": ("sbuf", [128, 16], "float32"),
+    "ones": ("sbuf", [128, L], "bfloat16"),
+    "cA": ("sbuf", [128, 128], "bfloat16"), "cB": ("sbuf", [128, 128], "bfloat16"), "cC": ("sbuf", [128, 128], "bfloat16"),
+    "half": ("sbuf", [128, 16], "float32"), "PW": ("sbuf", [128, 16], "float32"),
+    "dm": ("sbuf", [128, 16], "float32"), "dm2": ("sbuf", [128, 16], "float32"),
+    "S2": ("sbuf", [128, 144], "bfloat16"), "Sn": ("sbuf", [128, 144], "bfloat16"),
+    "SA": ("sbuf", [128, 144], "bfloat16"),
+    "L8": ("sbuf", [128, 128], "float32"), "BO32": ("sbuf", [128, 128], "float32"),
+    "sel14": ("sbuf", [128, 128], "float32"),
+    "Cm0": ("sbuf", [128, L], "bfloat16"), "R": ("sbuf", [128, L], "bfloat16"), "Y0": ("sbuf", [128, 16], "bfloat16"),
+    "SJ": ("sbuf", [128, 144], "bfloat16"), "SK": ("sbuf", [128, 144], "bfloat16"),
+    "DX": ("sbuf", [128, 16], "float32"), "DR": ("sbuf", [128, 16], "float32"),
+    "w1": ("sbuf", [128, L], "int32"), "w2": ("sbuf", [128, L], "int32"), "mI": ("sbuf", [128, L], "int32"),
+    "vf": ("sbuf", [128, L], "float32"), "uI": ("sbuf", [128, L], "int32"), "h32": ("sbuf", [128, L], "int32"),
+    "h16": ("sbuf", [128, L], "uint16"),
+    "r32": ("sbuf", [128, L], "float32"), "rb": ("sbuf", [128, L], "float16"), "pb": ("sbuf", [128, L], "bfloat16"),
+    "N512": ("sbuf", [128, 128], "float16"), "E2": ("sbuf", [128, 16, 256], "bfloat16"),
+    "R2": ("sbuf", [128, L], "bfloat16"), "nT": ("sbuf", [128, 16], "float32"),
+    "sU": ("sbuf", [128, L], "float32"), "tf": ("sbuf", [128, L], "float32"), "pT": ("sbuf", [128, 16], "float32"),
+    "sN": ("sbuf", [128, L], "float32"), "sV": ("sbuf", [128, L], "float32"),
+    "hit": ("sbuf", [128, L], "bfloat16"), "oh": ("sbuf", [128, L], "bfloat16"), "msk": ("sbuf", [128, L], "float32"),
+    "dz": ("sbuf", [128, L], "bfloat16"), "nrep": ("sbuf", [128, L], "uint16"), "avg": ("sbuf", [128, L], "bfloat16"),
+    "tb": ("sbuf", [128, L], "bfloat16"), "yf": ("sbuf", [128, L], "float32"), "af": ("sbuf", [128, L], "float32"),
+    "ti": ("sbuf", [128, 32], "int32"), "tt": ("sbuf", [128, 112], "float32"),
+    "oY": ("sbuf", [128, 16], "uint16"), "oN": ("sbuf", [128, 16], "uint16"), "oX": ("sbuf", [128, 16], "uint16"),
+    "oC": ("sbuf", [128, 16], "uint16"), "oR": ("sbuf", [128, 16], "uint16"),
+    "acc": ("sbuf", [128, 4], "float32"), "ai": ("sbuf", [128, 4], "int32"),
+    "xo": ("sbuf", [128, L], "float32"),
+}
+for _n in ("I", "H", "BO", "BOn", "BO4", "BO16", "Cs", "W4", "A2", "TE", "TE0", "dg1"):
+    SCRATCH[_n] = ("sbuf", [128, 128], "bfloat16")
+for _b in range(8):
+    SCRATCH["b%d" % _b] = ("psum", [128, 512], "float32")
+
+SEMAPHORES = (["qv", "qs", "qp", "qg", "sent", "out", "lo", "barr", "lz", "lw", "ll", "lt", "lc"]
+              + ["lx%d" % i for i in range(4)]
+              + ["zarr%d" % t for t in range(1, 5)] + ["farr%d" % t for t in range(1, 5)] + ["harr1", "harr2"])
+
+
+def weave(*lists):
+    for i in range(max(len(x) for x in lists)):
+        for x in lists:
+            if i < len(x):
+                x[i]()
+
+
+def rank_program(g, core, T, topo):
+    rank = T.rank_of(core)
+    if rank is None:
+        return
+    N = len(T.cores)
+    Q = {"v": g.vector, "s": g.scalar, "p": g.tensor, "g": g, "y": g.sync}
+    ops = []
+    last_w, readers, bank = {}, {}, {}
+
+    def add(q, fn, r=(), w=(), ps=(), sem=None, inc=16, strict=False):
+        i = len(ops)
+        deps = set()
+        for x in r:
+            if x in last_w:
+                deps.add(last_w[x])
+        for x in w:
+            for j in readers.get(x, []) + ([last_w[x]] if x in last_w else []):
+                if strict or ops[j]["q"] != q or ops[j]["sem"] is not None or sem is not None:
+                    deps.add(j)
+        for b in ps:
+            for qq, j in bank.get(b, {}).items():
+                if qq != q:
+                    deps.add(j)
+            bank.setdefault(b, {})[q] = i
+        for x in r:
+            readers.setdefault(x, []).append(i)
+        for x in w:
+            last_w[x] = i
+            readers[x] = []
+        ops.append({"q": q, "fn": fn, "deps": deps, "sem": sem, "inc": inc})
+        return i
+
+    def arrival(name, sem, n):
+        add(None, None, w=[name], sem=sem, inc=n)
+
+    def ts(out, in0, s1, s2, o0, o1=None, r=(), w=(), ps=(), **k):
+        if o1 is None:
+            add("v", lambda: g.vector.tensor_scalar(out, in0, s1, None, o0), r, w, ps, **k)
+        else:
+            add("v", lambda: g.vector.tensor_scalar(out, in0, s1, s2, o0, o1), r, w, ps, **k)
+
+    def tt(out, a, b, op, r=(), w=(), ps=(), **k):
+        add("v", lambda: g.vector.tensor_tensor(out, a, b, op), r, w, ps, **k)
+
+    def cp(out, a, r=(), w=(), ps=()):
+        add("v", lambda: g.vector.tensor_copy(out, a), r, w, ps)
+
+    def ms(out, c, w):
+        add("v", lambda: g.vector.memset(out, c), (), w)
+
+    def act(out, a, f=ACT.Identity, bias=0.0, scale=1.0, r=(), w=(), ps=(), acc=None):
+        if acc is None:
+            add("s", lambda: g.scalar.activation(out, a, f, bias=bias, scale=scale), r, w, ps)
+        else:
+            add("s", lambda: g.scalar.activation(out, a, f, bias=bias, scale=scale, accum_out=acc), r, w, ps)
+
+    def mm(b, out, lhsT, rhs, start, stop, r=()):
+        add("p", lambda: g.tensor.matmul(out, lhsT, rhs, start, stop), r, (), [b])
+
+    def scan(out, b, w):
+        add("v", lambda: g.vector.tensor_tensor_scan(out[:], T.R[:], T[b][:, 0:L], 0.0, ALU.add, ALU.max),
+            ["R"], [w], [b])
+
+    def iota(out, pat, base, cm, w, small=True):
+        if small:
+            add("g", lambda: g.iota(out, pat, base, cm, allow_small_or_imprecise_dtypes=True), (), [w])
+        else:
+            add("g", lambda: g.iota(out, pat, base, cm), (), [w])
+
+    nsent = [0]
+
+    def send(dst_rank, out, in_, sem, r):
+        dst = T.cores[dst_rank]
+        rid, pid = topo.addr(dst, core)
+        m = topo.mask(core, dst)
+        nsent[0] += len(topo.engines(core, dst))
+        add("g", lambda: g.remote_dma(out, in_, T.sem[sem], T.sem.sent, pid, rid, m), r, (), sem="-")
+
+    nxt, prv = (rank + D) % N, (rank - D) % N
+    n_in = len(topo.engines(T.cores[prv], core))
+    cols = {}
+
+    def c(name):
+        if name not in cols:
+            cols[name] = len(cols)
+        return T.col[:, cols[name]:cols[name] + 1]
+
+    add("y", lambda: g.sync.dma_start(T.wi[:], T.wt[:]), (), ["wi"], sem="lw")
+    add("y", lambda: g.sync.dma_start(T.zin[:, 0:L], T.z0[:]), (), ["zin0"], sem="lz")
+    ms(T.LI[:], 0, ["LI", "LIt"])
+    add("s", lambda: g.scalar.dma_start(T.LI[0:128:16, 0:L], T.leaf[:]), (), ["LI"], sem="ll")
+    PW4 = W // 4
+    for i in range(4):
+        add("y", lambda i=i: g.sync.dma_start(T.xb[:, i * PW4:(i + 1) * PW4], T.x0[:, i * PW4:(i + 1) * PW4]),
+            (), ["xb%d" % i], sem="lx%d" % i)
+    iota(T.pI[:, 0:1], [[0, 1]], 0, 1, "pI", small=False)
+    iota(T.ig[:], [[1, 8], [0, 16]], 0, 0, "ig")
+    iota(T.ic[:], [[0, 16], [1, 16]], 0, 0, "ic")
+    iota(T.im[:], [[1, 144]], 0, 0, "im")
+    add("g", lambda: g.dma_start(T.LI[0:128:16, L:L + 1], T.th[:], allow_slow_non_contiguous=True), (), ["LIt"], sem="lt")
+    iota(T.ib[:], [[16, 16]], W, 0, "ib")
+
+    ms(T.ones[:], 1.0, ["ones"])
+    ms(T.half[:], 0.5, ["half"])
+    act(T.C[:, 0:L], T.ones[:], ACT.Silu, scale=0.0, r=["ones"], w=["C0"])
+    ts(T.pI[:, 1:2], T.pI[:, 0:1], 15, None, ALU.bitwise_and, r=["pI"], w=["kI"])
+    ts(T.pI[:, 2:3], T.pI[:, 0:1], 4, None, ALU.arith_shift_right, r=["pI"], w=["gI"])
+    add("v", lambda: g.vector.tensor_tensor_scan(T.PW[:], T.half[:], T.ones[:, 0:16], 2.0, ALU.mult, ALU.min),
+        ["half", "ones"], ["PW"])
+    cp(c("p"), T.pI[:, 0:1], ["pI"], ["p"])
+    cp(c("k"), T.pI[:, 1:2], ["kI"], ["k"])
+    cp(c("g"), T.pI[:, 2:3], ["gI"], ["g"])
+    ms(T.cA[0:32, :], 512.0 * 1536, ["cA"])
+    ms(T.cB[0:32, :], 33.0, ["cB"])
+    ms(T.cC[0:32, :], 32.0, ["cC"])
+    ts(T.BO[:], T.ig[:], c("g"), None, ALU.is_equal, r=["ig", "g"], w=["BO"])
+    ts(c("k0"), c("k"), 0.0, 8.0, ALU.is_equal, ALU.mult, r=["k"], w=["k0"])
+    ts(c("k0s"), c("k"), 0.0, 0.25, ALU.is_equal, ALU.mult, r=["k"], w=["k0s"])
+    ts(c("k14"), c("k"), 14.0, None, ALU.is_equal, r=["k"], w=["k14"])
+    ts(c("e15"), c("k"), 15.0, 0.25, ALU.is_equal, ALU.mult, r=["k"], w=["e15"])
+    ts(c("g15"), c("g"), 16.0, 15.0, ALU.mult, ALU.add, r=["g"], w=["g15"])
+    ts(T.dm[:], T.ic[:, 0:16], c("k"), None, ALU.is_equal, r=["ic", "k"], w=["dm"])
+    ts(T.Cm0[:], T.ic[:], c("k"), -BIG, ALU.not_equal, ALU.mult, r=["ic", "k"], w=["Cm0"])
+    ts(T.R[:], T.ic[:], 0.0, -2 * BIG, ALU.is_equal, ALU.mult, r=["ic"], w=["R"])
+    tt(T.dm2[:], T.dm[:], T.PW[:], ALU.mult, ["dm", "PW"], ["dm2"])
+    ts(T.I[:], T.im[:, 0:128], c("p"), None, ALU.is_equal, r=["im", "p"], w=["I"])
+    add("v", lambda: g.vector.tensor_reduce(c("pw"), T.dm2[:], AxisListType.X, ALU.add), ["dm2"], ["pw"])
+    ms(T.C[:, C_S:C_V], 0.0, ["C1"])
+    ts(c("sb"), c("pw"), 0.125, None, ALU.max, r=["pw"], w=["sb"])
+    ts(T.wf[:], T.wi[:], 2.0, None, ALU.mult, r=["wi"], w=["wf"])
+    ts(T.dg1[:], T.I[:], c("sb"), None, ALU.mult, r=["I", "sb"], w=["dg1"])
+    ts(T.A2[:], T.ig[:], c("g"), T.wf[:, 0:1], ALU.is_equal, ALU.mult, r=["ig", "g", "wf"], w=["A2"])
+    mm("b7", T.b7[:, 0:128], T.BO[:], T.dg1[:], True, True, ["BO", "dg1"])
+    act(T.BOn[:], T.BO[:], scale=-1.0, r=["BO"], w=["BOn"])
+    act(T.BO4[:], T.BO[:], scale=32768.0, r=["BO"], w=["BO4"])
+    act(T.BO16[:], T.BO[:], scale=16.0, r=["BO"], w=["BO16"])
+    ts(T.N512[:], T.I[:], -512.0, None, ALU.mult, r=["I"], w=["N512"])
+    act(T.BO32[:], T.BO[:], r=["BO"], w=["BO32"])
+    act(T.H[:], T.I[:], scale=0.5, r=["I"], w=["H"])
+    act(T.sel14[:], T.ones[:, 0:128], scale=c("k14"), r=["ones", "k14"], w=["sel14"])
+    act(T.Cs[:], T.BO4[:], scale=c("k0s"), r=["BO4", "k0s"], w=["Cs"])
+    ts(c("t8"), c("pw"), 8.0, 1.0, ALU.mult, ALU.min, r=["pw"], w=["t8"])
+    ts(c("t2"), c("pw"), 32772.0, -0.5, ALU.mult, ALU.add, r=["pw"], w=["t2"])
+    ts(T.LF[:, 0:L], T.LI[:, 0:L], 0.125, None, ALU.mult, r=["LI"], w=["LF"])
+    ts(T.L8[:], T.b7[:, 0:128], c("k0"), None, ALU.mult, r=["k0"], w=["L8"], ps=["b7"])
+    ts(T.Bm[:], T.b7[:, 0:128], T.wf[:, 1:2], 0.5, ALU.mult, ALU.mult, r=["wf"], w=["Bm"], ps=["b7"])
+    ts(c("t3"), c("k"), 4.0, c("t2"), ALU.is_ge, ALU.mult, r=["k", "t2"], w=["t3"])
+    ts(c("c1"), c("sb"), 0.5, -0.5, ALU.mult, ALU.add, r=["sb"], w=["c1"])
+    ts(c("sc3"), c("k"), 15.0, c("t8"), ALU.is_lt, ALU.mult, r=["k", "t8"], w=["sc3"])
+    ts(c("c2"), c("t3"), c("e15"), 2452.0, ALU.add, ALU.add, r=["t3", "e15"], w=["c2"])
+    act(T.R2[:], T.Cm0[:], bias=8192.0 - 2.0 ** 20, scale=-2.0 ** 20 / BIG, r=["Cm0"], w=["R2"])
+    send(nxt, T.Bin[:], T.Bm[:], "barr", ["Bm"])
+    arrival("Bin", "barr", n_in)
+    add("g", lambda: g.affine_select(T.TE0[:], T.BOn[:], [[1, 128]], ALU.is_ge, 0.0, 1, -1), ["BOn"], ["TE0"])
+    add("g", lambda: g.affine_select(T.W4[:], T.BO4[:], [[1, 128]], ALU.is_gt, 0.0, 0, -1), ["BO4"], ["W4"])
+    add("g", lambda: g.affine_select(T.TE[:], T.TE0[:], [[1, 128]], ALU.not_equal, 1.0, 1, -1), ["TE0"], ["TE"])
+    for a in range(L, C_S, L):
+        act(T.C[:, a:a + L], T.ones[:], scale=0.0, r=["ones"], w=["C0"])
+
+    def load_counters():
+        iota(T.C[:, C_V:16 + W], [[0, 16 + W - C_V]], 0, 0, "C3")
+        add("g", lambda: g.dma_start(T.C[0:128:16, 16:16 + W], T.c0[:]), (), ["C0", "C1", "C3", "C"], sem="lc")
+
+    def widen(q, a, b):
+        i = a // PW4
+        if q == "s":
+            act(T.X[:, 16 + a:16 + b], T.xb[:, a:b], bias=32.0, r=["xb%d" % i], w=["X%d" % a])
+        else:
+            ts(T.X[:, 16 + a:16 + b], T.xb[:, a:b], 32.0, None, ALU.add, r=["xb%d" % i], w=["X%d" % a])
+        return "X%d" % a
+
+    def late_constants():
+        ts(T.S2[:], T.im[:], c("g15"), 2.0, ALU.is_equal, ALU.mult, r=["im", "g15"], w=["S2"])
+        ts(T.Sn[:], T.im[:], c("g15"), -1.0, ALU.is_equal, ALU.mult, r=["im", "g15"], w=["Sn"])
+        ts(c("kp1"), c("k"), 1.0, None, ALU.add, r=["k"], w=["kp1"])
+        ts(c("hold"), c("k"), -8192.0, 15 * 8192.0, ALU.mult, ALU.add, r=["k"], w=["hold"])
+        ts(T.SA[:], T.im[:], c("g15"), T.wf[:, 0:1], ALU.is_equal, ALU.mult, r=["im", "g15", "wf"], w=["SA"])
+        ts(c("big15"), c("e15"), 4096.0, 512.5, ALU.mult, ALU.add, r=["e15"], w=["big15"])
+        ts(c("kh"), c("k"), -0.5, None, ALU.mult, r=["k"], w=["kh"])
+        ts(T.DR[:], T.ib[:], c("k"), None, ALU.add, r=["ib", "k"], w=["DR"])
+        ts(T.DX[:], T.ib[:], c("k"), 16.0, ALU.add, ALU.add, r=["ib", "k"], w=["DX"])
+        ts(T.SJ[:], T.im[:], c("g15"), c("kp1"), ALU.is_equal, ALU.mult, r=["im", "g15", "kp1"], w=["SJ"])
+        ts(T.SK[:], T.im[:], c("g15"), 0.0625, ALU.is_equal, ALU.mult, r=["im", "g15"], w=["SK"])
+        ts(T.Y0[:], T.DR[:], -float(W), 16.0, ALU.add, ALU.mult, r=["DR"], w=["Y0"])
+
+    def later_constants():
+        cp(T.LF[:, L:L + 2], T.LI[:, L:L + 2], ["LIt"], ["LFt"])
+        mm("b7", T.b7[:, 2:4], T.A2[:], T.ones[:, 0:2], True, True, ["A2", "ones"])
+        mm("b7", T.b7[:, 0:2], T.BO32[:], T.LF[:, L:L + 2], True, True, ["BO32", "LFt"])
+
+    def gap_constants():
+        ts(c("th"), T.b7[:, 0:1], c("big15"), None, ALU.add, r=["big15"], w=["th"], ps=["b7"])
+        ts(c("asum"), T.b7[:, 2:3], -16.0, None, ALU.mult, w=["asum"], ps=["b7"])
+
+    def firsts(keys, kname, scal, sname, b, en, extra=None):
+        E = T[en]
+
+        def sums(j):
+            if j == 0:
+                mm(b, T[b][:, 0:L], T.I[:], T.Cm0[:], True, False, ["I", "Cm0"])
+            if j < 15:
+                mm(b, T[b][:, 16 * j + 16:L], T.BO4[:], E[:, j, 16:L - 16 * j], False, False, ["BO4", en + "%d" % j])
+            if j == 14 and extra is not None:
+                extra()
+            if j == 15:
+                mm(b, T[b][:, 0:L], T.W4[:], E[:, :, 0:16], False, True, ["W4"] + [en + "%d" % i for i in range(16)])
+
+        def one(j, now=True):
+            ts(E[:, j, 0:L - 16 * j], keys[:, 16 * j:L], scal[:, j:j + 1], None, ALU.is_equal,
+               r=[kname, sname], w=[en + "%d" % j])
+            if now:
+                sums(j)
+            return lambda: sums(j)
+        return [lambda now=True, j=j: one(j, now) for j in range(16)]
+
+    Xc = T.X[:, 16:16 + W]
+    H2 = [(0, L // 2), (L // 2, L)]
+    Xn = []
+
+    def pages(t):
+        z, zn = T.zin[:, t * L:(t + 1) * L], "zin%d" % t
+        mm("b3", T.b3[:, 0:L], T.cA[0:1, :], T.ones[0:1, :], True, False, ["cA", "ones"])
+        mm("b3", T.b3[:, 0:L], T.cB[0:9, :], T.ones[0:9, :], False, False, ["cB", "ones"])
+        if t > 0:
+            arrival("fin%d" % t, "farr%d" % t, n_in)
+            arrival(zn, "zarr%d" % t, n_in)
+            mm("b4", T.b4[:, 0:L], T.L8[:], T.fin[:, (t - 1) * L:t * L], True, False, ["L8", "fin%d" % t])
+        mm("b2", T.b2[:, 0:L], T.A2[:], z, True, True, ["A2", zn])
+        if t > 0:
+            mm("b4", T.b4[:, 0:L], T.Bin[:], z, False, True, ["Bin", zn])
+        mm("b3", T.b3[:, 0:L], T.A2[:], z, False, False, ["A2", zn])
+        if t == 0:
+            mm("b4", T.b4[:, 0:L], T.L8[:], T.LF[:, 0:L], True, True, ["L8", "LF"])
+
+    def rounds():
+        ts(T.rb[:], T.b2[:, 0:L], 2.0 ** -9, 1536.0 - 255.0 / 512, ALU.mult, ALU.add, w=["rb"], ps=["b2"])
+        mm("b3", T.b3[:, 0:L], T.N512[:], T.rb[:], False, True, ["N512", "rb"])
+
+    pages(0)
+    for t in range(STEPS):
+        z, zn = T.zin[:, t * L:(t + 1) * L], "zin%d" % t
+        zo, zon = T.zout[:, t * L:(t + 1) * L], "zout%d" % t
+        last = t == STEPS - 1
+        rounds()
+        mm("b0", T.b0[:, 0:L], T.cC[0:1, :], T.ones[0:1, :], True, False, ["cC", "ones"])
+        mm("b0", T.b0[:, 0:L], T.I[:], z, False, True, ["I", zn])
+        mm("b1", T.b1[:, 0:L], T.BOn[:], z, True, False, ["BOn", zn])
+        fo = None if last else T.fout[:, t * L:(t + 1) * L]
+
+        def chain(a, b):
+            n = "_%d" % a
+            return [
+                lambda: ts(T.w1[:, a:b], T.b4[:, a:b], c("c1"), None, ALU.add, r=["c1"], w=["w1" + n], ps=["b4"]),
+                lambda: ts(T.w2[:, a:b], T.w1[:, a:b], 4095, None, ALU.bitwise_and, r=["w1" + n], w=["w2" + n]),
+                lambda: ts(T.mI[:, a:b], T.w2[:, a:b], c("sc3"), c("c2"), ALU.mult, ALU.add,
+                           r=["w2" + n, "sc3", "c2"], w=["mI" + n]),
+                lambda: tt(T.vf[:, a:b], T.mI[:, a:b], T.b3[:, a:b], ALU.mult, ["mI" + n], ["vf" + n], ["b3"]),
+                lambda: ts(T.uI[:, a:b], T.vf[:, a:b], 0.125, 3177.0625, ALU.mult, ALU.add, r=["vf" + n], w=["uI" + n]),
+                lambda: ts(T.h32[:, a:b], T.uI[:, a:b], 4095, None, ALU.bitwise_and, r=["uI" + n], w=["h32" + n]),
+                lambda: cp(T.h16[:, a:b], T.h32[:, a:b], ["h32" + n], ["h16" + n]),
+            ]
+        ch = [chain(a, b) for a, b in H2]
+        weave(*[x[:4] for x in ch])
+        if t == 0:
+            Xn = [widen("s", 0, PW4), widen("s", PW4, 2 * PW4)]
+        weave(*[x[4:] for x in ch])
+        h16n, h32n = ["h16_%d" % a for a, b in H2], ["h32_%d" % a for a, b in H2]
+
+        def leaves():
+            if t == 2:
+                cp(fo, T.w2[:], ["w2_%d" % a for a, b in H2], ["fout%d" % t])
+            else:
+                act(fo, T.b4[:, 0:L], w=["fout%d" % t], ps=["b4"])
+            send(nxt, T.fin[:, t * L:(t + 1) * L], fo, "farr%d" % (t + 1), ["fout%d" % t])
+        if t == 0:
+            leaves()
+            load_counters()
+        if t in (2, 3):
+            arrival("zhome%d" % t, "harr%d" % (t - 1), len(topo.engines(T.cores[(rank + D * (t - 1)) % N], core)))
+            add("y", lambda t=t: g.sync.dma_start(T.zs[:, (t - 1) * L:t * L], T.zhome[:, (t - 2) * L:(t - 1) * L]),
+                ["zhome%d" % t], (), sem="out")
+        if last:
+            add("y", lambda z=z: g.sync.dma_start(T.zs[:, 3 * L:4 * L], z), [zn], (), sem="out")
+        if t == 0:
+            late_constants()
+            Xn += [widen("v", 2 * PW4, 3 * PW4), widen("s", 3 * PW4, 3 * PW4 + 640), widen("v", 3 * PW4 + 640, W)]
+        def hn(a, b):
+            return ["h16_%d" % aa for aa, bb in H2 if aa < b and bb > a]
+        for i, (a, b) in enumerate(S_GATH):
+            add("s", lambda a=a, b=b: g.scalar.activation(T.xk[:, 16 * a:16 * b], Xc.indirect(T.h16[:, a:b]), ACT.Copy),
+                Xn + hn(a, b), ["xk%d" % a])
+            if i == 0:
+                act(T.pb[:], T.b3[:, 0:L], bias=-148.5, scale=0.5, w=["pb"], ps=["b3"])
+        if t in (1, 3):
+            leaves()
+        if t == 2:
+            leaves()
+        for a, b in V_GATH:
+            add("v", lambda a=a, b=b: g.vector.tensor_copy(T.xk[:, 16 * a:16 * b], Xc.indirect(T.h16[:, a:b])),
+                Xn + hn(a, b), ["xk%d" % a])
+        if t == 0:
+            later_constants()
+        allxk = ["xk%d" % a for a, b in S_GATH + V_GATH]
+        rootf = firsts(T.pb, "pb", T.pT, "pT", "b7", "E2")
+        for ci, (a, b) in enumerate(CHUNKS):
+            need = ["xk%d" % aa for aa, bb in S_GATH + V_GATH if aa < b and bb > a]
+
+            def level(k, a=a, b=b, ci=ci, need=need):
+                mm("b1", T.b1[:, a:b], T.Sn[:, 15 - k:143 - k], T.xk[:, 16 * a + k:16 * b:16], False, False, ["Sn"] + need)
+                tt(T.mx[:, k * L + a:k * L + b], T.xk[:, 16 * a + k:16 * b:16], T.b0[:, a:b], ALU.max,
+                   need, ["mx%d_%d" % (ci, k)], ["b0"])
+                mm("b1", T.b1[:, a:b], T.S2[:, 15 - k:143 - k], T.mx[:, k * L + a:k * L + b], False,
+                   ci == len(CHUNKS) - 1 and k == 14, ["S2", "mx%d_%d" % (ci, k)])
+            side = []
+            if ci == 0 and t == 0:
+                side = [gap_constants]
+            weave([lambda k=k: level(k) for k in range(15)], side)
+            if ci == 0:
+                for jj in range(16):
+                    mm("b2", T.b2[:, 0:16], T.SK[:, 15 - jj:143 - jj], T.pb[:, jj:L:16], jj == 0, jj == 15, ["SK", "pb"])
+            if ci == len(CHUNKS) - 2:
+                cp(T.pT[:], T.b2[:, 0:16], (), ["pT"], ["b2"])
+                late = [f(False) for f in rootf[:ROOT[0]]]
+        M, Mn = (c("th"), "th") if t == 0 else (c("M"), "M")
+        act(T.hit[:], T.b1[:, 0:L], ACT.Sign, bias=M, scale=-1.0, r=[Mn], w=["hit"], ps=["b1"])
+        mm("b6", T.b6[:, 0:L], T.H[:], T.xk[:, 15:W:16], True, False, ["H"] + allxk)
+        mm("b6", T.b6[:, 0:L], T.H[:], z, False, True, ["H", zn])
+        mm("b4", T.b4[:, L:L + 16], T.I[:], T.Y0[:], True, False, ["I", "Y0"])
+        ts(T.ti[:, 0:16], T.pT[:], 613.25, 36.625, ALU.mult, ALU.add, r=["pT"], w=["ti0"])
+        late += [f(False) for f in rootf[ROOT[0]:8]]
+        ts(T.ti[:, 16:32], T.ti[:, 0:16], 4095, None, ALU.bitwise_and, r=["ti0"], w=["ti1"])
+        late += [f(False) for f in rootf[max(8, ROOT[0]):]]
+        mm("b2", T.b2[:, 0:L], T.TE[:], T.hit[:], True, True, ["TE", "hit"])
+        weave(late[:ROOT[1]])
+        act(T.oh[:], T.b2[:, 0:L], ACT.Relu, bias=c("kh"), scale=0.5, r=["kh"], w=["oh"], ps=["b2"])
+        act(T.b0[:, 0:L], T.b2[:, 0:L], ACT.Relu, bias=c("kh"), scale=0.5, r=["kh"], w=["acc"], ps=["b2", "b0"],
+            acc=None if last else T.acc[:, 0:1])
+        act(T.avg[:], T.b6[:, 0:L], bias=111.75, w=["avg"], ps=["b6"])
+        for j in range(16):
+            mm("b4", T.b4[:, L:L + 16], T.SJ[:, 15 - j:143 - j], T.oh[:, j:L:16], False, j == 15, ["SJ", "oh"])
+        tt(T.msk[:], T.h32[:], T.b0[:, 0:L], ALU.mult, h32n, ["msk"], ["b0"])
+        mm("b5", T.b5[:, 0:L], T.BO16[:], T.oh[:], True, False, ["BO16", "oh"])
+        mm("b5", T.b5[:, 0:L], T.BO32[:], T.msk[:], False, True, ["BO32", "msk"])
+        weave(late[ROOT[1]:ROOT[2]])
+        if not last:
+            mm("b6", T.b6[:, L:L + 1], T.sel14[:], T.acc[:, 0:1], True, True, ["sel14", "acc"])
+        cp(T.oY[:], T.b4[:, L:L + 16], (), ["oY"], ["b4"])
+        tt(T.dz[:], T.xk[:, 0:W].indirect(T.oY[:]), z, ALU.subtract, allxk + ["oY", zn], ["dz"])
+        act(T.af[:], T.avg[:], bias=-96.0, r=["avg"], w=["af"])
+        act(zo, T.dz[:], ACT.Abs, bias=-32.0, r=["dz"], w=[zon])
+        if not last:
+            send(nxt, T.zin[:, (t + 1) * L:(t + 2) * L], zo, "zarr%d" % (t + 1), [zon])
+        if t in (1, 2):
+            send((rank - D * t) % N, T.zhome[:, (t - 1) * L:t * L], zo, "harr%d" % t, [zon])
+        if t == 0 or last:
+            add("y", lambda t=t, zo=zo: g.sync.dma_start(T.zs[:, t * L:(t + 1) * L], zo), [zon], (), sem="out")
+        add("v", lambda: g.vector.tensor_tensor_scan(T.sN[:], T.R2[:], T.b5[:, 0:L], 0.0, ALU.add, ALU.max),
+            ["R2"], ["sN"], ["b5"])
+        cp(T.nrep[:], T.b5[:, 0:L], (), ["nrep"], ["b5"])
+        ts(T.nT[:], T.sN[:, 15:L:16], c("hold"), None, ALU.subtract, r=["sN", "hold"], w=["nT"])
+        ts(T.oN[:], T.sN[:, 15:L:16], c("hold"), None, ALU.subtract, r=["sN", "hold"], w=["oN"])
+        if t > 0:
+            add("s", lambda: g.scalar.activation(T.C[:, 0:XW].indirect(T.oC[:]), T.tf[:], ACT.Silu), ["oC", "tf"], ["C"])
+        add("s", lambda: g.scalar.activation(T.tb[:], T.C[:, 0:16 + W].indirect(T.oN[:]), ACT.Relu, bias=1.0, scale=-2.0),
+            ["C", "oN"], ["tb"])
+        add("s", lambda: g.scalar.activation(T.yf[:], T.xk[:, 0:W].indirect(T.oY[:]), ACT.Copy), allxk + ["oY"], ["yf"])
+        if not last:
+            act(T.tf[:], T.tb[:], scale=SILU_ONE, r=["tb"], w=["tf"])
+        weave(firsts(T.nrep, "nrep", T.nT, "nT", "b1", "E",
+                     lambda: mm("b1", T.b1[:, 0:L], T.Cs[:], T.tb[:], False, False, ["Cs", "tb"])))
+        weave(late[ROOT[2]:])
+        if not last:
+            pages(t + 1)
+        bound = [] if last else [
+            lambda: cp(T.ai[:, 0:1], T.b6[:, L:L + 1], (), ["ai0"], ["b6"]),
+            lambda: ts(T.ai[:, 1:2], T.ai[:, 0:1], 15, None, ALU.bitwise_and, r=["ai0"], w=["ai1"]),
+            lambda: ts(c("M"), T.ai[:, 1:2], c("th"), None, ALU.add, r=["ai1", "th"], w=["M"])]
+        if SU_FIRST:
+            scan(T.sU, "b7", "sU")
+        else:
+            weave(bound[:2])
+        scan(T.sV, "b1", "sV")
+        root = [lambda: tt(T.tt[:, 0:16], T.sU[:, 15:L:16], T.DR[:], ALU.min, ["sU", "DR"], ["tt0"]),
+                lambda: tt(T.tt[:, 16:32], T.tt[:, 0:16], T.ti[:, 16:32], ALU.max, ["tt0", "ti1"], ["tt1"]),
+                lambda: cp(T.oR[:], T.tt[:, 16:32], ["tt1"], ["oR"])]
+        named = [lambda: tt(T.tt[:, 32:48], T.sV[:, 15:L:16], T.DX[:], ALU.min, ["sV", "DX"], ["tt2"]),
+                 lambda: tt(T.tt[:, 48:64], T.tt[:, 32:48], T.nT[:], ALU.max, ["tt2", "nT"], ["tt3"]),
+                 lambda: cp(T.oX[:], T.tt[:, 48:64], ["tt3"], ["oX"])]
+        count = [lambda: ts(T.tt[:, 64:80], T.sV[:, 15:L:16], -16384.0, None, ALU.add, r=["sV"], w=["tt4"]),
+                 lambda: tt(T.tt[:, 80:96], T.tt[:, 64:80], T.DX[:], ALU.min, ["tt4", "DX"], ["tt5"]),
+                 lambda: tt(T.tt[:, 96:112], T.tt[:, 80:96], T.nT[:], ALU.max, ["tt5", "nT"], ["tt6"]),
+                 lambda: cp(T.oC[:], T.tt[:, 96:112], ["tt6"], ["oC"])]
+        if SU_FIRST:
+            weave(root[:1])
+            weave(named, root[1:])
+            weave(count, bound)
+        else:
+            weave(named, count[:2])
+            scan(T.sU, "b7", "sU")
+            weave(count[2:3])
+            weave(root, count[3:] + bound[2:])
+        add("s", lambda Xn=Xn: g.scalar.activation(T.X[:, 0:XW].indirect(T.oX[:]), T.yf[:], ACT.Silu), ["oX", "yf"], Xn)
+        add("s", lambda: g.scalar.activation(T.X[:, 16:XW].indirect(T.oR[:]), T.af[:], ACT.Silu), ["oR", "af"], ["X"] + Xn,
+            strict=True)
+        Xn = ["X"]
+
+    add("v", lambda: g.vector.tensor_copy(T.C[:, 0:XW].indirect(T.oC[:]), T.tb[:]), ["oC", "tb"], ["C"])
+    add("y", lambda: g.sync.dma_start(T.r32[:], T.C[0:128:16, 16:16 + W]), ["C"], ["r32"], sem="lo")
+    for j2 in range(8):
+        a, b = j2 * 512, (j2 + 1) * 512
+        if j2 % 2:
+            act(T.xb[:, a:b], T.X[:, 16 + a:16 + b], r=["X"], w=["xe%d" % j2])
+        else:
+            cp(T.xb[:, a:b], T.X[:, 16 + a:16 + b], ["X"], ["xe%d" % j2])
+        for j in (2 * j2, 2 * j2 + 1):
+            mm("b6", T.b6[:, 0:L], T.SA[:, 15 - j:143 - j], T.xb[:, j * L:(j + 1) * L], j == 0, j == 15, ["SA", "xe%d" % j2])
+    ts(T.tf[:], T.r32[:], 0.5, None, ALU.is_gt, r=["r32"], w=["tf"])
+    add("s", lambda: g.scalar.dma_start(T.cs[:], T.tf[:]), ["tf"], (), sem="out")
+    ts(T.xo[:], T.b6[:, 0:L], 0.5, c("asum"), ALU.mult, ALU.add, r=["asum"], w=["xo"], ps=["b6"])
+    add("y", lambda: g.sync.dma_start(T.xs[:], T.xo[:]), ["xo"], (), sem="out")
+
+    needed = set()
+    for o in ops:
+        best = {}
+        for j in o["deps"]:
+            if ops[j]["sem"] is None:
+                best[ops[j]["q"]] = max(best.get(ops[j]["q"], -1), j)
+        needed.update(best.values())
+    count, total = {}, {}
+    for i, o in enumerate(ops):
+        s = o["sem"] if o["sem"] is not None else "q" + o["q"]
+        if o["sem"] is not None or i in needed:
+            total[s] = total.get(s, 0) + (o["inc"] if o["sem"] is not None else 1)
+        count[i] = (s, total.get(s, 0))
+    seen, most = {}, {}
+    for i, o in enumerate(ops):
+        q = o["q"]
+        if q is None:
+            continue
+        want = {}
+        for j in o["deps"]:
+            if ops[j]["sem"] is None and j not in needed:
+                continue
+            s, n = count[j]
+            want[s] = max(want.get(s, 0), n)
+        for s in sorted(want):
+            if want[s] > seen.get((q, s), 0):
+                Q[q].wait_ge(T.sem[s], want[s])
+                seen[(q, s)] = want[s]
+                most[s] = max(most.get(s, 0), want[s])
+        ins = o["fn"]()
+        if o["sem"] == "-":
+            continue
+        if o["sem"] is not None:
+            ins.then_inc(T.sem[o["sem"]], o["inc"])
+        elif i in needed:
+            ins.then_inc(T.sem["q" + q], 1)
+    g.wait_ge(T.sem.sent, nsent[0])
+    for s in sorted(total):
+        if s not in ("-", "out") and most.get(s, 0) < total[s]:
+            g.wait_ge(T.sem[s], total[s])
+    g.wait_ge(T.sem.out, total["out"])

@@ -3,74 +3,137 @@ from concourse.mybir import AluOpType, AxisListType, ActivationFunctionType
 ALU = AluOpType
 ACT = ActivationFunctionType
 W, L, STEPS, D = 4096, 256, 5, 3
-XW = 16 + W + L
-BIG = float(2 ** 46)
+HL = L // 2
+BASE = 272
+CW = BASE + W
+TURN = 3177
+ONE = 41 / 32
+AWAY = 41 * 107
+XW = 8768
+BIG = float(2 ** 30)
 MAGIC = 1.5 * 2 ** 23
-SILU_ONE = 1.2784645427610738
-S_GATH = [(0, 64), (64, 128), (128, 192)]
-V_GATH = [(192, 256)]
-CHUNKS = [(192, 256), (0, 64), (64, 128), (128, 192)]
-ROOT = (0, 3, 16)
-SU_FIRST = True
-C_S, C_V = 1280, 1600
+V_GATH = 32
+S_CHUNK = 32
+C_S = 2304
+STRICT = False
+CYC, PE_CYC, GATH, SCAT, WAKE, LOOK = 0.92, 0.46, 1.25, 3.0, 220.0, 150.0
+DMA_LAT, REMOTE_LAT, DMA_RATE = 2000.0, 2300.0, 250.0
+ROUNDS = 1
+PERIOD = 11.5
+DUE = {"paths0": -3.0, "leaves": 1.0, "gather": 0.0, "chunk": 0.7, "near": (1.0, 2.3, 3.9, 5.3), "z1": 3.0, "z0": 5.5,
+       "named1": 6.0, "named0": 5.6, "roots": 6.5, "means": 6.4, "write": 7.0, "paths1": 5.4, "counters": 10.0,
+       "bound": 9.0, "home": 8.0, "sums": 12.0}
 
 SCRATCH = {
-    "X": ("sbuf", [128, XW], "float32"), "C": ("sbuf", [128, XW], "float32"),
+    "X": ("sbuf", [128, XW], "float32"), "C": ("sbuf", [128, CW], "float32"), "C2": ("sbuf", [128, CW], "float32"),
+    "Cb": ("sbuf", [128, W], "bfloat16"),
     "xk": ("sbuf", [128, W], "bfloat16"), "mx": ("sbuf", [128, W], "bfloat16"), "xb": ("sbuf", [128, W], "bfloat16"),
-    "E": ("sbuf", [128, 16, 256], "bfloat16"),
+    "E": ("sbuf", [128, 16, HL], "bfloat16"), "E2": ("sbuf", [128, 16, HL], "bfloat16"),
     "zin": ("sbuf", [128, 5 * L], "bfloat16"), "zout": ("sbuf", [128, 5 * L], "bfloat16"),
     "zhome": ("sbuf", [128, 2 * L], "bfloat16"),
-    "fin": ("sbuf", [128, 4 * L], "float32"), "fout": ("sbuf", [128, 4 * L], "float32"),
-    "LI": ("sbuf", [128, 264], "int32"), "LF": ("sbuf", [128, 264], "float32"),
+    "fin": ("sbuf", [128, 5 * L], "float32"), "mI": ("sbuf", [128, 5 * L], "float32"),
+    "LI": ("sbuf", [128, 264], "int32"), "thf": ("sbuf", [128, 2], "float32"),
     "wi": ("sbuf", [128, 2], "int32"), "wf": ("sbuf", [128, 2], "float32"),
-    "Bm": ("sbuf", [128, 128], "bfloat16"), "Bin": ("sbuf", [128, 128], "bfloat16"),
-    "pI": ("sbuf", [128, 4], "int32"), "col": ("sbuf", [128, 32], "float32"),
+    "pI": ("sbuf", [128, 4], "int32"), "col": ("sbuf", [128, 40], "float32"),
     "im": ("sbuf", [128, 144], "bfloat16"), "ig": ("sbuf", [128, 128], "bfloat16"),
-    "ic": ("sbuf", [128, L], "bfloat16"),
-    "ib": ("sbuf", [128, 16], "float32"),
-    "ones": ("sbuf", [128, L], "bfloat16"),
-    "cA": ("sbuf", [128, 128], "bfloat16"), "cB": ("sbuf", [128, 128], "bfloat16"), "cC": ("sbuf", [128, 128], "bfloat16"),
-    "half": ("sbuf", [128, 16], "float32"), "PW": ("sbuf", [128, 16], "float32"),
-    "dm": ("sbuf", [128, 16], "float32"), "dm2": ("sbuf", [128, 16], "float32"),
-    "S2": ("sbuf", [128, 144], "bfloat16"), "Sn": ("sbuf", [128, 144], "bfloat16"),
-    "SA": ("sbuf", [128, 144], "bfloat16"),
-    "L8": ("sbuf", [128, 128], "float32"), "BO32": ("sbuf", [128, 128], "float32"),
-    "sel14": ("sbuf", [128, 128], "float32"),
-    "Cm0": ("sbuf", [128, L], "bfloat16"), "R": ("sbuf", [128, L], "bfloat16"), "Y0": ("sbuf", [128, 16], "bfloat16"),
-    "SJ": ("sbuf", [128, 144], "bfloat16"), "SK": ("sbuf", [128, 144], "bfloat16"),
-    "DX": ("sbuf", [128, 16], "float32"), "DR": ("sbuf", [128, 16], "float32"),
-    "w1": ("sbuf", [128, L], "int32"), "w2": ("sbuf", [128, L], "int32"), "mI": ("sbuf", [128, L], "int32"),
+    "ic": ("sbuf", [128, L], "bfloat16"), "ib": ("sbuf", [128, 16], "float32"),
+    "ones": ("sbuf", [128, L], "bfloat16"), "onef": ("sbuf", [128, HL], "float32"),
+    "dm": ("sbuf", [128, 32], "float32"),
+    "Cm0": ("sbuf", [128, L], "bfloat16"), "Cm1": ("sbuf", [128, L], "bfloat16"), "RF": ("sbuf", [128, L], "bfloat16"),
+    "R2": ("sbuf", [128, L], "bfloat16"), "Y0": ("sbuf", [128, 8], "bfloat16"),
+    "qq": ("sbuf", [128, L], "bfloat16"), "rb": ("sbuf", [128, L], "float16"), "pb": ("sbuf", [128, L], "bfloat16"),
     "vf": ("sbuf", [128, L], "float32"), "uI": ("sbuf", [128, L], "int32"), "h32": ("sbuf", [128, L], "int32"),
-    "h16": ("sbuf", [128, L], "uint16"),
-    "r32": ("sbuf", [128, L], "float32"), "rb": ("sbuf", [128, L], "float16"), "pb": ("sbuf", [128, L], "bfloat16"),
-    "N512": ("sbuf", [128, 128], "float16"), "E2": ("sbuf", [128, 16, 256], "bfloat16"),
-    "R2": ("sbuf", [128, L], "bfloat16"), "nT": ("sbuf", [128, 16], "float32"),
-    "sU": ("sbuf", [128, L], "float32"), "tf": ("sbuf", [128, L], "float32"), "pT": ("sbuf", [128, 16], "float32"),
-    "sN": ("sbuf", [128, L], "float32"), "sV": ("sbuf", [128, L], "float32"),
-    "hit": ("sbuf", [128, L], "bfloat16"), "oh": ("sbuf", [128, L], "bfloat16"), "msk": ("sbuf", [128, L], "float32"),
-    "dz": ("sbuf", [128, L], "bfloat16"), "nrep": ("sbuf", [128, L], "uint16"), "avg": ("sbuf", [128, L], "bfloat16"),
-    "tb": ("sbuf", [128, L], "bfloat16"), "yf": ("sbuf", [128, L], "float32"), "af": ("sbuf", [128, L], "float32"),
-    "ti": ("sbuf", [128, 32], "int32"), "tt": ("sbuf", [128, 112], "float32"),
+    "h16": ("sbuf", [128, L], "uint16"), "hf": ("sbuf", [128, L], "float16"), "msk": ("sbuf", [128, L], "float16"),
+    "hit": ("sbuf", [128, L], "bfloat16"), "oh": ("sbuf", [128, L], "bfloat16"),
+    "dz": ("sbuf", [128, L], "bfloat16"), "nrep": ("sbuf", [128, L], "uint16"),
+    "sN": ("sbuf", [128, L], "float32"), "sV": ("sbuf", [128, L], "float32"), "sU": ("sbuf", [128, L], "float32"),
+    "tf": ("sbuf", [128, L], "float32"), "yf": ("sbuf", [128, L], "float32"), "af": ("sbuf", [128, L], "float32"),
+    "pT": ("sbuf", [128, 16], "float32"), "tt": ("sbuf", [128, 32], "float32"),
     "oY": ("sbuf", [128, 16], "uint16"), "oN": ("sbuf", [128, 16], "uint16"), "oX": ("sbuf", [128, 16], "uint16"),
     "oC": ("sbuf", [128, 16], "uint16"), "oR": ("sbuf", [128, 16], "uint16"),
     "acc": ("sbuf", [128, 4], "float32"), "ai": ("sbuf", [128, 4], "int32"),
     "xo": ("sbuf", [128, L], "float32"),
 }
-for _n in ("I", "H", "BO", "BOn", "BO4", "BO16", "Cs", "W4", "A2", "TE", "TE0", "dg1"):
+for _n in ("S2", "Sn", "SA", "SJ", "SK"):
+    SCRATCH[_n] = ("sbuf", [128, 144], "bfloat16")
+for _n in ("I", "H", "BO", "BOn", "BOm", "BOb", "Wm", "A2", "TE", "TE0", "dg1", "QM", "Bm", "Bin", "c128", "tiny"):
     SCRATCH[_n] = ("sbuf", [128, 128], "bfloat16")
+for _n in ("N64", "BOh", "R15", "c809", "c1025"):
+    SCRATCH[_n] = ("sbuf", [128, 128], "float16")
+for _n in ("L8", "DG", "Cs", "Cs1", "sel14", "BO32", "I32"):
+    SCRATCH[_n] = ("sbuf", [128, 128], "float32")
 for _b in range(8):
     SCRATCH["b%d" % _b] = ("psum", [128, 512], "float32")
 
-SEMAPHORES = (["qv", "qs", "qp", "qg", "sent", "out", "lo", "barr", "lz", "lw", "ll", "lt", "lc"]
-              + ["lx%d" % i for i in range(4)]
-              + ["zarr%d" % t for t in range(1, 5)] + ["farr%d" % t for t in range(1, 5)] + ["harr1", "harr2"])
+SEMAPHORES = (["qv", "qs", "qp", "qg", "sent", "out", "barr", "lz", "lw", "ll", "lt", "lc", "lx", "lX", "lb", "l2"]
+              + ["zarr%d_%d" % (t, h) for t in range(1, 5) for h in range(2)] + ["farr%d" % t for t in range(1, 5)]
+              + ["harr1", "harr2"])
+
+ORDER = []
 
 
-def weave(*lists):
-    for i in range(max(len(x) for x in lists)):
-        for x in lists:
-            if i < len(x):
-                x[i]()
+def elems(ap):
+    n = 1
+    for s in ap.shape[1:]:
+        n *= s
+    return n
+
+
+def list_schedule(ops, edges, release, rank):
+    n = len(ops)
+    left = [0] * n
+    for e in edges:
+        for u, _ in e:
+            left[u] += 1
+    ready_at, start = list(release), [0.0] * n
+    ready, free, order = {}, {}, []
+    for i in range(n):
+        if left[i] == 0:
+            ready.setdefault(ops[i]["q"], []).append(i)
+    while len(order) < n:
+        best = None
+        for q, r in ready.items():
+            if r:
+                t = max(free.get(q, 0.0), min(ready_at[i] for i in r))
+                i = max((i for i in r if ready_at[i] <= t + LOOK), key=lambda i: rank[i])
+                t = max(t, ready_at[i])
+                if best is None or t < best[0]:
+                    best = (t, i)
+        t, i = best
+        ready[ops[i]["q"]].remove(i)
+        free[ops[i]["q"]] = t + ops[i]["cost"]
+        start[i] = t
+        order.append(i)
+        for u, gap in edges[i]:
+            ready_at[u] = max(ready_at[u], t + gap)
+            left[u] -= 1
+            if left[u] == 0:
+                ready.setdefault(ops[u]["q"], []).append(u)
+    return order, start
+
+
+def put_in_order(ops):
+    n = len(ops)
+    ahead, back = [[] for _ in ops], [[] for _ in ops]
+    for u, o in enumerate(ops):
+        for i in o["deps"] | o["after"]:
+            gap = ops[i]["lat"] + (WAKE if o["q"] else 0.0) if i in o["deps"] else ops[i]["cost"]
+            ahead[i].append((u, gap))
+            back[u].append((i, gap + o["cost"] - ops[i]["cost"]))
+    due = [o["due"] for o in ops]
+    for i in range(n - 1, -1, -1):
+        if due[i] is None:
+            due[i] = min([1e9] + [due[u] - gap for u, gap in ahead[i]])
+    rank, best = [(-due[i], -i) for i in range(n)], None
+    for _ in range(ROUNDS):
+        order, start = list_schedule(ops, ahead, [0.0] * n, rank)
+        end = max(start[i] + ops[i]["lat"] for i in range(n))
+        if best is None or end < best[0]:
+            best = (end, order)
+        rank = [(start[i] + ops[i]["cost"], i) for i in range(n)]
+        _, late = list_schedule(ops, back, [o["lat"] - o["cost"] for o in ops], rank)
+        rank = [(late[i] + ops[i]["cost"], -i) for i in range(n)]
+    return best[1]
 
 
 def rank_program(g, core, T, topo):
@@ -80,76 +143,100 @@ def rank_program(g, core, T, topo):
     N = len(T.cores)
     Q = {"v": g.vector, "s": g.scalar, "p": g.tensor, "g": g, "y": g.sync}
     ops = []
-    last_w, readers, bank = {}, {}, {}
+    last_w, readers, bank, sends = {}, {}, {}, {}
+    due = [None]
 
-    def add(q, fn, r=(), w=(), ps=(), sem=None, inc=16, strict=False):
+    def stage(t, at):
+        due[0] = 1000.0 * (t * PERIOD + at)
+
+    def add(q, fn, r=(), w=(), ps=(), cost=60.0, lat=None, sem=None, inc=16, strict=False):
         i = len(ops)
-        deps = set()
+        deps, after = set(), set()
         for x in r:
-            if x in last_w:
-                deps.add(last_w[x])
+            deps.update(last_w.get(x, []))
         for x in w:
-            for j in readers.get(x, []) + ([last_w[x]] if x in last_w else []):
-                if strict or ops[j]["q"] != q or ops[j]["sem"] is not None or sem is not None:
-                    deps.add(j)
+            for j in readers.get(x, []) + last_w.get(x, []):
+                (after if x == "in turn" else deps).add(j)
         for b in ps:
             for qq, j in bank.get(b, {}).items():
-                if qq != q:
-                    deps.add(j)
+                (after if qq == q else deps).add(j)
             bank.setdefault(b, {})[q] = i
         for x in r:
             readers.setdefault(x, []).append(i)
         for x in w:
-            last_w[x] = i
+            last_w[x] = [i]
             readers[x] = []
-        ops.append({"q": q, "fn": fn, "deps": deps, "sem": sem, "inc": inc})
+        ops.append({"q": q, "fn": fn, "deps": deps, "after": after - deps, "sem": sem, "inc": inc, "cost": cost,
+                    "lat": cost if lat is None else lat, "due": due[0]})
         return i
 
     def arrival(name, sem, n):
-        add(None, None, w=[name], sem=sem, inc=n)
+        i = add(None, None, w=[name], sem=sem, inc=n, cost=0.0)
+        ops[i]["deps"].add(sends[sem])
 
-    def ts(out, in0, s1, s2, o0, o1=None, r=(), w=(), ps=(), **k):
+    def vcost(n, fast=False):
+        return max(64, n / 2 if fast else n) * CYC
+
+    def ts(out, in0, s1, s2, o0, o1=None, r=(), w=(), ps=(), fast=False):
         if o1 is None:
-            add("v", lambda: g.vector.tensor_scalar(out, in0, s1, None, o0), r, w, ps, **k)
+            add("v", lambda: g.vector.tensor_scalar(out, in0, s1, None, o0), r, w, ps, vcost(elems(out), fast))
         else:
-            add("v", lambda: g.vector.tensor_scalar(out, in0, s1, s2, o0, o1), r, w, ps, **k)
+            add("v", lambda: g.vector.tensor_scalar(out, in0, s1, s2, o0, o1), r, w, ps, vcost(elems(out), fast))
 
-    def tt(out, a, b, op, r=(), w=(), ps=(), **k):
-        add("v", lambda: g.vector.tensor_tensor(out, a, b, op), r, w, ps, **k)
+    def tt(out, a, b, op, r=(), w=(), ps=()):
+        add("v", lambda: g.vector.tensor_tensor(out, a, b, op), r, w, ps, vcost(elems(out)))
 
     def cp(out, a, r=(), w=(), ps=()):
-        add("v", lambda: g.vector.tensor_copy(out, a), r, w, ps)
+        add("v", lambda: g.vector.tensor_copy(out, a), r, w, ps, vcost(elems(out)))
 
     def ms(out, c, w):
-        add("v", lambda: g.vector.memset(out, c), (), w)
+        add("v", lambda: g.vector.memset(out, c), (), w, (), vcost(elems(out), True))
 
-    def act(out, a, f=ACT.Identity, bias=0.0, scale=1.0, r=(), w=(), ps=(), acc=None):
+    def scan(out, d0, d1, init, o0, r, w, ps):
+        add("v", lambda: g.vector.tensor_tensor_scan(out, d0, d1, init, o0, ALU.max), r, w, ps, vcost(elems(out)))
+
+    def act(out, a, f=ACT.Identity, bias=0.0, scale=1.0, r=(), w=(), ps=(), acc=None, cost=None):
+        cost = vcost(elems(out)) if cost is None else cost
         if acc is None:
-            add("s", lambda: g.scalar.activation(out, a, f, bias=bias, scale=scale), r, w, ps)
+            add("s", lambda: g.scalar.activation(out, a, f, bias=bias, scale=scale), r, w, ps, cost)
         else:
-            add("s", lambda: g.scalar.activation(out, a, f, bias=bias, scale=scale, accum_out=acc), r, w, ps)
+            add("s", lambda: g.scalar.activation(out, a, f, bias=bias, scale=scale, accum_out=acc), r, w, ps, cost + 20)
 
-    def mm(b, out, lhsT, rhs, start, stop, r=()):
-        add("p", lambda: g.tensor.matmul(out, lhsT, rhs, start, stop), r, (), [b])
+    def scatter(win, off, src, n, r, w):
+        add("s", lambda: g.scalar.activation(win.indirect(off), src, ACT.Silu), r, w, (), 65 + n * SCAT, strict=STRICT)
 
-    def scan(out, b, w):
-        add("v", lambda: g.vector.tensor_tensor_scan(out[:], T.R[:], T[b][:, 0:L], 0.0, ALU.add, ALU.max),
-            ["R"], [w], [b])
+    def mm(b, out, lhsT, rhs, start, stop, r=(), f32=False):
+        add("p", lambda: g.tensor.matmul(out, lhsT, rhs, start, stop), r, (), [b],
+            max(64, elems(out)) * PE_CYC * (4 if f32 else 1))
+
+    def dma(q, out, in_, r, w, sem, size=0, **k):
+        return add(q, lambda: Q[q].dma_start(out, in_, **k), r, w, (), 600.0 if q == "g" else 60.0,
+                   DMA_LAT + size / DMA_RATE, sem)
+
+    def turned(q, win, base, src, r, name, sem, size, before=()):
+        rows = slice(0, 128, 128 // src.shape[0])
+        i = dma(q, win[rows, base + W - TURN:base + W], src[:, 0:TURN], r, list(before) + [name + "a"], sem, size)
+        j = dma(q, win[rows, base:base + W - TURN], src[:, TURN:W], r, [name], sem, size)
+        ops[j]["deps"] |= ops[i]["deps"]
+        ops[j]["after"].add(i)
+        last_w[name] = [i, j]
 
     def iota(out, pat, base, cm, w, small=True):
         if small:
-            add("g", lambda: g.iota(out, pat, base, cm, allow_small_or_imprecise_dtypes=True), (), [w])
+            add("g", lambda: g.iota(out, pat, base, cm, allow_small_or_imprecise_dtypes=True), (), [w], (),
+                130 + 2 * elems(out) * CYC)
         else:
-            add("g", lambda: g.iota(out, pat, base, cm), (), [w])
+            add("g", lambda: g.iota(out, pat, base, cm), (), [w], (), 130.0)
 
     nsent = [0]
 
-    def send(dst_rank, out, in_, sem, r):
+    def send(dst_rank, out, in_, sem, r, size):
         dst = T.cores[dst_rank]
         rid, pid = topo.addr(dst, core)
         m = topo.mask(core, dst)
         nsent[0] += len(topo.engines(core, dst))
-        add("g", lambda: g.remote_dma(out, in_, T.sem[sem], T.sem.sent, pid, rid, m), r, (), sem="-")
+        sends[sem] = add("g", lambda: g.remote_dma(out, in_, T.sem[sem], T.sem.sent, pid, rid, m), r, (), (), 600.0,
+                         REMOTE_LAT + size / 60, "-")
 
     nxt, prv = (rank + D) % N, (rank - D) % N
     n_in = len(topo.engines(T.cores[prv], core))
@@ -160,355 +247,365 @@ def rank_program(g, core, T, topo):
             cols[name] = len(cols)
         return T.col[:, cols[name]:cols[name] + 1]
 
-    add("y", lambda: g.sync.dma_start(T.wi[:], T.wt[:]), (), ["wi"], sem="lw")
-    add("y", lambda: g.sync.dma_start(T.zin[:, 0:L], T.z0[:]), (), ["zin0"], sem="lz")
+    def cc(name, src, s1, s2, o0, o1=None):
+        r = [src] + [x for x in (s1, s2) if isinstance(x, str)]
+        s1, s2 = [c(x) if isinstance(x, str) else x for x in (s1, s2)]
+        ts(c(name), c(src), s1, s2, o0, o1, r=r, w=[name])
+
+    def mat(name, src, s1, s2, o0, o1=None):
+        r = [src] + [x for x in (s1, s2) if isinstance(x, str)]
+        s1, s2 = [c(x) if isinstance(x, str) else x for x in (s1, s2)]
+        ts(T[name][:], T[src][:, 0:T[name].shape[1]], s1, s2, o0, o1, r=r, w=[name], fast=True)
+
+    dma("y", T.wi[:], T.wt[:], (), ["wi"], "lw")
+    dma("y", T.zin[:, 0:L], T.z0[:], (), ["zin0_0", "zin0_1"], "lz")
     ms(T.LI[:], 0, ["LI", "LIt"])
-    add("s", lambda: g.scalar.dma_start(T.LI[0:128:16, 0:L], T.leaf[:]), (), ["LI"], sem="ll")
-    PW4 = W // 4
-    for i in range(4):
-        add("y", lambda i=i: g.sync.dma_start(T.xb[:, i * PW4:(i + 1) * PW4], T.x0[:, i * PW4:(i + 1) * PW4]),
-            (), ["xb%d" % i], sem="lx%d" % i)
+    dma("s", T.LI[0:128:16, 0:L], T.leaf[:], (), ["LI"], "ll")
+    turned("y", T.xb, 0, T.x0, (), "xb", "lx", 128 * W * 2)
     iota(T.pI[:, 0:1], [[0, 1]], 0, 1, "pI", small=False)
     iota(T.ig[:], [[1, 8], [0, 16]], 0, 0, "ig")
-    iota(T.ic[:], [[0, 16], [1, 16]], 0, 0, "ic")
     iota(T.im[:], [[1, 144]], 0, 0, "im")
-    add("g", lambda: g.dma_start(T.LI[0:128:16, L:L + 1], T.th[:], allow_slow_non_contiguous=True), (), ["LIt"], sem="lt")
-    iota(T.ib[:], [[16, 16]], W, 0, "ib")
-
+    iota(T.ic[:], [[0, 16], [1, 16]], 0, 0, "ic")
+    iota(T.ib[:], [[16, 16]], 0, 0, "ib")
+    dma("g", T.LI[0:128:16, L:L + 1], T.th[:], (), ["LIt"], "lt", allow_slow_non_contiguous=True)
     ms(T.ones[:], 1.0, ["ones"])
-    ms(T.half[:], 0.5, ["half"])
-    act(T.C[:, 0:L], T.ones[:], ACT.Silu, scale=0.0, r=["ones"], w=["C0"])
+    ms(T.onef[:], 1.0, ["onef"])
+    ms(T.c128[0:32, :], 128.0, ["c128"])
+    ms(T.tiny[0:32, :], 2.0 ** -17, ["tiny"])
+    ts(T.c809[0:32, :], T.ones[0:32, 0:128], 809.0, None, ALU.mult, r=["ones"], w=["c809"], fast=True)
+    ts(T.c1025[0:32, :], T.ones[0:32, 0:128], 1025.0 / 8, None, ALU.mult, r=["ones"], w=["c1025"], fast=True)
+    act(T.C[:, 0:L], T.ones[:], ACT.Silu, scale=0.0, r=["ones"], w=["C0"], cost=1500.0)
+    for a in range(L, C_S, L):
+        act(T.C[:, a:a + L], T.ones[:], scale=0.0, r=["ones"], w=["C%d" % a])
+    for a in range(C_S, CW, 516):
+        iota(T.C[:, a:a + 516], [[0, 516]], 0, 0, "C%d" % a)
+    turned("g", T.C, BASE, T.c0, (), "C", "lc", 8 * W * 4,
+           ["C%d" % a for a in list(range(0, C_S, L)) + list(range(C_S, CW, 516))])
+    turned("g", T.X, BASE, T.x0, ["xb"], "X", "lX", 128 * W * 4)
+
     ts(T.pI[:, 1:2], T.pI[:, 0:1], 15, None, ALU.bitwise_and, r=["pI"], w=["kI"])
     ts(T.pI[:, 2:3], T.pI[:, 0:1], 4, None, ALU.arith_shift_right, r=["pI"], w=["gI"])
-    add("v", lambda: g.vector.tensor_tensor_scan(T.PW[:], T.half[:], T.ones[:, 0:16], 2.0, ALU.mult, ALU.min),
-        ["half", "ones"], ["PW"])
     cp(c("p"), T.pI[:, 0:1], ["pI"], ["p"])
     cp(c("k"), T.pI[:, 1:2], ["kI"], ["k"])
     cp(c("g"), T.pI[:, 2:3], ["gI"], ["g"])
-    ms(T.cA[0:32, :], 512.0 * 1536, ["cA"])
-    ms(T.cB[0:32, :], 33.0, ["cB"])
-    ms(T.cC[0:32, :], 32.0, ["cC"])
-    ts(T.BO[:], T.ig[:], c("g"), None, ALU.is_equal, r=["ig", "g"], w=["BO"])
-    ts(c("k0"), c("k"), 0.0, 8.0, ALU.is_equal, ALU.mult, r=["k"], w=["k0"])
-    ts(c("k0s"), c("k"), 0.0, 0.25, ALU.is_equal, ALU.mult, r=["k"], w=["k0s"])
-    ts(c("k14"), c("k"), 14.0, None, ALU.is_equal, r=["k"], w=["k14"])
-    ts(c("e15"), c("k"), 15.0, 0.25, ALU.is_equal, ALU.mult, r=["k"], w=["e15"])
-    ts(c("g15"), c("g"), 16.0, 15.0, ALU.mult, ALU.add, r=["g"], w=["g15"])
-    ts(T.dm[:], T.ic[:, 0:16], c("k"), None, ALU.is_equal, r=["ic", "k"], w=["dm"])
-    ts(T.Cm0[:], T.ic[:], c("k"), -BIG, ALU.not_equal, ALU.mult, r=["ic", "k"], w=["Cm0"])
-    ts(T.R[:], T.ic[:], 0.0, -2 * BIG, ALU.is_equal, ALU.mult, r=["ic"], w=["R"])
-    tt(T.dm2[:], T.dm[:], T.PW[:], ALU.mult, ["dm", "PW"], ["dm2"])
-    ts(T.I[:], T.im[:, 0:128], c("p"), None, ALU.is_equal, r=["im", "p"], w=["I"])
-    add("v", lambda: g.vector.tensor_reduce(c("pw"), T.dm2[:], AxisListType.X, ALU.add), ["dm2"], ["pw"])
-    ms(T.C[:, C_S:C_V], 0.0, ["C1"])
-    ts(c("sb"), c("pw"), 0.125, None, ALU.max, r=["pw"], w=["sb"])
-    ts(T.wf[:], T.wi[:], 2.0, None, ALU.mult, r=["wi"], w=["wf"])
-    ts(T.dg1[:], T.I[:], c("sb"), None, ALU.mult, r=["I", "sb"], w=["dg1"])
-    ts(T.A2[:], T.ig[:], c("g"), T.wf[:, 0:1], ALU.is_equal, ALU.mult, r=["ig", "g", "wf"], w=["A2"])
+    ts(T.dm[:, 0:16], T.im[:, 0:16], c("k"), 0.5, ALU.is_ge, ALU.max, r=["im", "k"], w=["dm0"])
+    add("v", lambda: g.vector.tensor_reduce(c("pw"), T.dm[:, 0:16], AxisListType.X, ALU.mult), ["dm0"], ["pw"])
+    mat("BO", "ig", "g", None, ALU.is_equal)
+    mat("I", "im", "p", None, ALU.is_equal)
+    ts(T.wf[:], T.wi[:], 0.25, None, ALU.mult, r=["wi"], w=["wf"])
+    ts(T.A2[:], T.ig[:], c("g"), T.wf[:, 0:1], ALU.is_equal, ALU.mult, r=["ig", "g", "wf"], w=["A2"], fast=True)
+    mat("dg1", "im", "p", "pw", ALU.is_equal, ALU.mult)
     mm("b7", T.b7[:, 0:128], T.BO[:], T.dg1[:], True, True, ["BO", "dg1"])
+    cc("k0", "k", 0.0, 8.0, ALU.is_equal, ALU.mult)
+    ts(T.L8[:], T.b7[:, 0:128], c("k0"), None, ALU.mult, r=["k0"], w=["L8"], ps=["b7"])
+    ts(T.Bm[:], T.b7[:, 0:128], T.wf[:, 1:2], 4.0, ALU.mult, ALU.mult, r=["wf"], w=["Bm"], ps=["b7"])
+    ts(T.fin[:, 0:L], T.LI[:, 0:L], 0.125, 2452.0, ALU.mult, ALU.add, r=["LI"], w=["fin0"])
+    cc("ck", "pw", -19615.5, -0.5, ALU.mult, ALU.add)
+    mat("DG", "im", "p", "ck", ALU.is_equal, ALU.mult)
+    cc("nT", "pw", -32768.0, -4096.0, ALU.mult, ALU.max)
+    cc("bq", "nT", 128.5, -0.5, ALU.mult, ALU.add)
+    cc("k4", "k", 4.0, "pw", ALU.is_ge, ALU.mult)
+    cc("mg0", "nT", -129.0, MAGIC, ALU.mult, ALU.add)
+    cc("mg", "k4", 32768.0, "mg0", ALU.mult, ALU.add)
+    mat("N64", "I", -64.0, None, ALU.mult)
+    send(nxt, T.Bin[:], T.Bm[:], "barr", ["Bm"], 128 * 256)
+    arrival("Bin", "barr", n_in)
+
+    cc("g15", "g", 16.0, 15.0, ALU.mult, ALU.add)
+    mat("S2", "im", "g15", 2.0, ALU.is_equal, ALU.mult)
+    mat("Sn", "im", "g15", -1.0, ALU.is_equal, ALU.mult)
+    cc("kp1", "k", 1.0, None, ALU.add)
+    mat("SJ", "im", "g15", "kp1", ALU.is_equal, ALU.mult)
+    mat("SK", "im", "g15", 0.0625, ALU.is_equal, ALU.mult)
+    ts(T.SA[:], T.im[:], c("g15"), T.wf[:, 0:1], ALU.is_equal, ALU.mult, r=["im", "g15", "wf"], w=["SA"], fast=True)
+    mat("Cm0", "ic", "k", -BIG, ALU.not_equal, ALU.mult)
+    cc("e15", "k", 15.0, None, ALU.is_equal)
+    cc("k14", "k", 14.0, None, ALU.is_equal)
+    cc("hold", "k", -8192.0, 15 * 8192.0, ALU.mult, ALU.add)
+    cc("big15", "e15", 4096.0, 2048.5, ALU.mult, ALU.add)
+    cc("kh", "k", -0.5, None, ALU.mult)
+    cc("top", "k", -1.0, 256.0, ALU.mult, ALU.add)
+    mat("BOh", "BO", 1.0, None, ALU.mult)
+    mat("R15", "BO", "e15", None, ALU.mult)
+    ms(T.RF[:], BIG, ["RF0"])
+    ts(T.RF[:, 0:L:16], T.ib[:], -1.0, c("top"), ALU.mult, ALU.add, r=["ib", "top", "RF0"], w=["RF"])
+    ts(T.Y0[:], T.ib[:, 0:8], c("k"), 16.0, ALU.add, ALU.mult, r=["ib", "k"], w=["Y0"])
     act(T.BOn[:], T.BO[:], scale=-1.0, r=["BO"], w=["BOn"])
-    act(T.BO4[:], T.BO[:], scale=32768.0, r=["BO"], w=["BO4"])
-    act(T.BO16[:], T.BO[:], scale=16.0, r=["BO"], w=["BO16"])
-    ts(T.N512[:], T.I[:], -512.0, None, ALU.mult, r=["I"], w=["N512"])
+    act(T.BOm[:], T.BO[:], scale=-32768.0, r=["BO"], w=["BOm"])
+    act(T.BOb[:], T.BO[:], scale=2048.0 + BASE, r=["BO"], w=["BOb"])
     act(T.BO32[:], T.BO[:], r=["BO"], w=["BO32"])
+    act(T.I32[:], T.I[:], r=["I"], w=["I32"])
     act(T.H[:], T.I[:], scale=0.5, r=["I"], w=["H"])
     act(T.sel14[:], T.ones[:, 0:128], scale=c("k14"), r=["ones", "k14"], w=["sel14"])
-    act(T.Cs[:], T.BO4[:], scale=c("k0s"), r=["BO4", "k0s"], w=["Cs"])
-    ts(c("t8"), c("pw"), 8.0, 1.0, ALU.mult, ALU.min, r=["pw"], w=["t8"])
-    ts(c("t2"), c("pw"), 32772.0, -0.5, ALU.mult, ALU.add, r=["pw"], w=["t2"])
-    ts(T.LF[:, 0:L], T.LI[:, 0:L], 0.125, None, ALU.mult, r=["LI"], w=["LF"])
-    ts(T.L8[:], T.b7[:, 0:128], c("k0"), None, ALU.mult, r=["k0"], w=["L8"], ps=["b7"])
-    ts(T.Bm[:], T.b7[:, 0:128], T.wf[:, 1:2], 0.5, ALU.mult, ALU.mult, r=["wf"], w=["Bm"], ps=["b7"])
-    ts(c("t3"), c("k"), 4.0, c("t2"), ALU.is_ge, ALU.mult, r=["k", "t2"], w=["t3"])
-    ts(c("c1"), c("sb"), 0.5, -0.5, ALU.mult, ALU.add, r=["sb"], w=["c1"])
-    ts(c("sc3"), c("k"), 15.0, c("t8"), ALU.is_lt, ALU.mult, r=["k", "t8"], w=["sc3"])
-    ts(c("c2"), c("t3"), c("e15"), 2452.0, ALU.add, ALU.add, r=["t3", "e15"], w=["c2"])
+    cc("k0a", "k0", AWAY / ONE / 8, None, ALU.mult)
+    cc("k0b", "k0", AWAY / 8, None, ALU.mult)
+    act(T.Cs[:], T.BO[:], scale=c("k0a"), r=["BO", "k0a"], w=["Cs"])
+    act(T.Cs1[:], T.BO[:], scale=c("k0b"), r=["BO", "k0b"], w=["Cs1"])
     act(T.R2[:], T.Cm0[:], bias=8192.0 - 2.0 ** 20, scale=-2.0 ** 20 / BIG, r=["Cm0"], w=["R2"])
-    send(nxt, T.Bin[:], T.Bm[:], "barr", ["Bm"])
-    arrival("Bin", "barr", n_in)
-    add("g", lambda: g.affine_select(T.TE0[:], T.BOn[:], [[1, 128]], ALU.is_ge, 0.0, 1, -1), ["BOn"], ["TE0"])
-    add("g", lambda: g.affine_select(T.W4[:], T.BO4[:], [[1, 128]], ALU.is_gt, 0.0, 0, -1), ["BO4"], ["W4"])
-    add("g", lambda: g.affine_select(T.TE[:], T.TE0[:], [[1, 128]], ALU.not_equal, 1.0, 1, -1), ["TE0"], ["TE"])
-    for a in range(L, C_S, L):
-        act(T.C[:, a:a + L], T.ones[:], scale=0.0, r=["ones"], w=["C0"])
+    act(T.Cm1[:], T.Cm0[:], bias=2048.0 + BASE, r=["Cm0"], w=["Cm1"])
+    asel = 170 + 256 * CYC
+    add("g", lambda: g.affine_select(T.TE0[:], T.BOn[:], [[1, 128]], ALU.is_ge, 0.0, 1, -1), ["BOn"], ["TE0"], (), asel)
+    add("g", lambda: g.affine_select(T.TE[:], T.TE0[:], [[1, 128]], ALU.not_equal, 1.0, 1, -1), ["TE0"], ["TE"], (), asel)
+    add("g", lambda: g.affine_select(T.Wm[:], T.BOm[:], [[1, 128]], ALU.is_gt, 0.0, 0, -1), ["BOm"], ["Wm"], (), asel)
+    cp(T.thf[:], T.LI[:, L:L + 2], ["LIt"], ["thf"])
+    mm("b7", T.b7[:, 2:4], T.A2[:], T.ones[:, 0:2], True, True, ["A2", "ones"])
+    mm("b7", T.b7[:, 0:2], T.BO32[:], T.thf[:], True, True, ["BO32", "thf"], True)
+    ts(c("th"), T.b7[:, 0:1], c("big15"), None, ALU.add, r=["big15"], w=["th"], ps=["b7"])
+    ts(c("asum"), T.b7[:, 2:3], -512.0, None, ALU.mult, w=["asum"], ps=["b7"])
 
-    def load_counters():
-        iota(T.C[:, C_V:16 + W], [[0, 16 + W - C_V]], 0, 0, "C3")
-        add("g", lambda: g.dma_start(T.C[0:128:16, 16:16 + W], T.c0[:]), (), ["C0", "C1", "C3", "C"], sem="lc")
+    ZB, DB = ["b1", "b0"], ["b3", "b2"]
+    q0, q1, q2, q3 = [slice(i * HL, (i + 1) * HL) for i in range(4)]
 
-    def widen(q, a, b):
-        i = a // PW4
-        if q == "s":
-            act(T.X[:, 16 + a:16 + b], T.xb[:, a:b], bias=32.0, r=["xb%d" % i], w=["X%d" % a])
-        else:
-            ts(T.X[:, 16 + a:16 + b], T.xb[:, a:b], 32.0, None, ALU.add, r=["xb%d" % i], w=["X%d" % a])
-        return "X%d" % a
+    def half(h):
+        return slice(h * HL, (h + 1) * HL), slice(h * 8, (h + 1) * 8), "_%d" % h
 
-    def late_constants():
-        ts(T.S2[:], T.im[:], c("g15"), 2.0, ALU.is_equal, ALU.mult, r=["im", "g15"], w=["S2"])
-        ts(T.Sn[:], T.im[:], c("g15"), -1.0, ALU.is_equal, ALU.mult, r=["im", "g15"], w=["Sn"])
-        ts(c("kp1"), c("k"), 1.0, None, ALU.add, r=["k"], w=["kp1"])
-        ts(c("hold"), c("k"), -8192.0, 15 * 8192.0, ALU.mult, ALU.add, r=["k"], w=["hold"])
-        ts(T.SA[:], T.im[:], c("g15"), T.wf[:, 0:1], ALU.is_equal, ALU.mult, r=["im", "g15", "wf"], w=["SA"])
-        ts(c("big15"), c("e15"), 4096.0, 512.5, ALU.mult, ALU.add, r=["e15"], w=["big15"])
-        ts(c("kh"), c("k"), -0.5, None, ALU.mult, r=["k"], w=["kh"])
-        ts(T.DR[:], T.ib[:], c("k"), None, ALU.add, r=["ib", "k"], w=["DR"])
-        ts(T.DX[:], T.ib[:], c("k"), 16.0, ALU.add, ALU.add, r=["ib", "k"], w=["DX"])
-        ts(T.SJ[:], T.im[:], c("g15"), c("kp1"), ALU.is_equal, ALU.mult, r=["im", "g15", "kp1"], w=["SJ"])
-        ts(T.SK[:], T.im[:], c("g15"), 0.0625, ALU.is_equal, ALU.mult, r=["im", "g15"], w=["SK"])
-        ts(T.Y0[:], T.DR[:], -float(W), 16.0, ALU.add, ALU.mult, r=["DR"], w=["Y0"])
+    def both(x):
+        return [x + "_0", x + "_1"]
 
-    def later_constants():
-        cp(T.LF[:, L:L + 2], T.LI[:, L:L + 2], ["LIt"], ["LFt"])
-        mm("b7", T.b7[:, 2:4], T.A2[:], T.ones[:, 0:2], True, True, ["A2", "ones"])
-        mm("b7", T.b7[:, 0:2], T.BO32[:], T.LF[:, L:L + 2], True, True, ["BO32", "LFt"])
+    def paths(t, h):
+        s, _, n = half(h)
+        st = slice(t * L + h * HL, t * L + (h + 1) * HL)
+        z, zn, zb = T.zin[:, st], "zin%d_%d" % (t, h), ZB[h]
+        if t > 0:
+            if h == 1:
+                arrival("fin%d" % t, "farr%d" % t, n_in)
+            arrival(zn, "zarr%d_%d" % (t, h), n_in)
+        mm("b5", T.b5[:, q0], T.DG[:], T.onef[:], True, False, ["DG", "onef"], True)
+        mm("b5", T.b5[:, q0], T.L8[:], T.fin[:, st], False, t == 0, ["L8", "fin%d" % t], True)
+        mm("b4", T.b4[:, q0], T.c809[0:1, :], T.c1025[0:1, :], True, False, ["c809", "c1025"])
+        if t > 0:
+            mm("b5", T.b5[:, q0], T.Bin[:], z, False, True, ["Bin", zn])
+        mm(zb, T[zb][:, q2], T.A2[:], z, True, True, ["A2", zn])
+        mm("b4", T.b4[:, q0], T.A2[:], z, False, False, ["A2", zn])
+        act(T.qq[:, s], T.b5[:, q0], bias=c("bq"), scale=-1.0, r=["bq"], w=["qq" + n], ps=["b5"])
+        ts(T.rb[:, s], T[zb][:, q2], 2.0 ** -6, 1619.0 - 255.0 / 512, ALU.mult, ALU.add, w=["rb" + n], ps=[zb])
+        tt(T.vf[:, s], T.qq[:, s], T.b5[:, q0], ALU.add, ["qq" + n], ["vf" + n], ["b5"])
+        mm("b4", T.b4[:, q0], T.N64[:], T.rb[:, s], False, False, ["N64", "rb" + n])
+        mm("b4", T.b4[:, q0], T.tiny[0:1, :], T.ones[0:1, 0:HL], False, True, ["tiny", "ones"])
+        mn = "mI%d_%d" % (t, h)
+        ts(T.mI[:, st], T.vf[:, s], c("mg"), MAGIC - 2452.0, ALU.add, ALU.subtract, r=["mg", "vf" + n], w=[mn])
+        tt(T.uI[:, s], T.mI[:, st], T.b4[:, q0], ALU.mult, [mn], ["uI" + n], ["b4"])
+        ts(T.h32[:, s], T.uI[:, s], 4095, None, ALU.bitwise_and, r=["uI" + n], w=["h32" + n])
+        cp(T.h16[:, s], T.h32[:, s], ["h32" + n], ["h16" + n])
+        mm(zb, T[zb][:, q0], T.c128[0:1, :], T.ones[0:1, 0:HL], True, False, ["c128", "ones"])
+        mm(zb, T[zb][:, q0], T.I[:], z, False, True, ["I", zn])
+        act(T.pb[:, s], T.b4[:, q0], bias=-148.5, scale=4.0, w=["pb" + n], ps=["b4"])
+        ts(T.hf[:, s], T.h16[:, s], -2048.0, None, ALU.add, r=["h16" + n], w=["hf" + n], fast=True)
 
-    def gap_constants():
-        ts(c("th"), T.b7[:, 0:1], c("big15"), None, ALU.add, r=["big15"], w=["th"], ps=["b7"])
-        ts(c("asum"), T.b7[:, 2:3], -16.0, None, ALU.mult, w=["asum"], ps=["b7"])
+    def records(t, h):
+        _, _, n = half(h)
+        win, wn = (T.xb[:, 0:W], ["xb"]) if t == 0 else (T.X[:, BASE:CW], ["X"])
+        zb, db = ZB[h], DB[h]
+        cuts = list(range(h * HL + (V_GATH if h else 0), (h + 1) * HL, S_CHUNK)) + [(h + 1) * HL]
+        parts = [(a, b) for a, b in zip(cuts, cuts[1:])]
+        if h and V_GATH:
+            a, b = HL, HL + V_GATH
+            stage(t, DUE["gather"])
+            add("v", lambda a=a, b=b: g.vector.tensor_scalar(T.xk[:, 16 * a:16 * b], win.indirect(T.h16[:, a:b]), 128.0,
+                                                             None, ALU.add),
+                wn + ["h16" + n], ["xk%d" % a], (), 50 + 16 * (b - a) * GATH)
+        for a, b in parts:
+            stage(t, DUE["gather"] + DUE["chunk"] * ((a - HL) % L - V_GATH) / S_CHUNK)
+            act(T.xk[:, 16 * a:16 * b], win.indirect(T.h16[:, a:b]), bias=128.0, r=wn + ["h16" + n],
+                w=["xk%d" % a, "in turn"], cost=65 + 16 * (b - a) * GATH)
+        if h and V_GATH:
+            parts.append((HL, HL + V_GATH))
+        for a in (h * HL, h * HL + 64):
+            stage(t, DUE["near"][(a - HL) % L // 64])
+            if a == h * HL:
+                mm(db, T[db][:, q0], T.BOn[:], T.zin[:, t * L + h * HL:t * L + (h + 1) * HL], True, False,
+                   ["BOn", "zin%d_%d" % (t, h)])
+            b, o = a + 64, slice(a - h * HL, a - h * HL + 64)
+            need = ["xk%d" % aa for aa, bb in parts if aa < b and bb > a]
+            for k in range(15):
+                mm(db, T[db][:, o], T.Sn[:, 15 - k:143 - k], T.xk[:, 16 * a + k:16 * b:16], False, False, ["Sn"] + need)
+            for k in range(15):
+                x, m = T.xk[:, 16 * a + k:16 * b:16], T.mx[:, k * L + a:k * L + b]
+                tt(m, x, T[zb][:, o], ALU.max, need, ["mx%d_%d" % (a, k)], [zb])
+                mm(db, T[db][:, o], T.S2[:, 15 - k:143 - k], m, False, a > h * HL and k == 14, ["S2", "mx%d_%d" % (a, k)])
+        return ["xk%d" % a for a, b in parts]
 
-    def firsts(keys, kname, scal, sname, b, en, extra=None):
+    def matches(h, keys, kn, shift, scal, sn, en, b, out, stop):
         E = T[en]
-
-        def sums(j):
-            if j == 0:
-                mm(b, T[b][:, 0:L], T.I[:], T.Cm0[:], True, False, ["I", "Cm0"])
-            if j < 15:
-                mm(b, T[b][:, 16 * j + 16:L], T.BO4[:], E[:, j, 16:L - 16 * j], False, False, ["BO4", en + "%d" % j])
-            if j == 14 and extra is not None:
-                extra()
-            if j == 15:
-                mm(b, T[b][:, 0:L], T.W4[:], E[:, :, 0:16], False, True, ["W4"] + [en + "%d" % i for i in range(16)])
-
-        def one(j, now=True):
-            ts(E[:, j, 0:L - 16 * j], keys[:, 16 * j:L], scal[:, j:j + 1], None, ALU.is_equal,
-               r=[kname, sname], w=[en + "%d" % j])
-            if now:
-                sums(j)
-            return lambda: sums(j)
-        return [lambda now=True, j=j: one(j, now) for j in range(16)]
-
-    Xc = T.X[:, 16:16 + W]
-    H2 = [(0, L // 2), (L // 2, L)]
-    Xn = []
-
-    def pages(t):
-        z, zn = T.zin[:, t * L:(t + 1) * L], "zin%d" % t
-        mm("b3", T.b3[:, 0:L], T.cA[0:1, :], T.ones[0:1, :], True, False, ["cA", "ones"])
-        mm("b3", T.b3[:, 0:L], T.cB[0:9, :], T.ones[0:9, :], False, False, ["cB", "ones"])
-        if t > 0:
-            arrival("fin%d" % t, "farr%d" % t, n_in)
-            arrival(zn, "zarr%d" % t, n_in)
-            mm("b4", T.b4[:, 0:L], T.L8[:], T.fin[:, (t - 1) * L:t * L], True, False, ["L8", "fin%d" % t])
-        mm("b2", T.b2[:, 0:L], T.A2[:], z, True, True, ["A2", zn])
-        if t > 0:
-            mm("b4", T.b4[:, 0:L], T.Bin[:], z, False, True, ["Bin", zn])
-        mm("b3", T.b3[:, 0:L], T.A2[:], z, False, False, ["A2", zn])
-        if t == 0:
-            mm("b4", T.b4[:, 0:L], T.L8[:], T.LF[:, 0:L], True, True, ["L8", "LF"])
-
-    def rounds():
-        ts(T.rb[:], T.b2[:, 0:L], 2.0 ** -9, 1536.0 - 255.0 / 512, ALU.mult, ALU.add, w=["rb"], ps=["b2"])
-        mm("b3", T.b3[:, 0:L], T.N512[:], T.rb[:], False, True, ["N512", "rb"])
-
-    pages(0)
-    for t in range(STEPS):
-        z, zn = T.zin[:, t * L:(t + 1) * L], "zin%d" % t
-        zo, zon = T.zout[:, t * L:(t + 1) * L], "zout%d" % t
-        last = t == STEPS - 1
-        rounds()
-        mm("b0", T.b0[:, 0:L], T.cC[0:1, :], T.ones[0:1, :], True, False, ["cC", "ones"])
-        mm("b0", T.b0[:, 0:L], T.I[:], z, False, True, ["I", zn])
-        mm("b1", T.b1[:, 0:L], T.BOn[:], z, True, False, ["BOn", zn])
-        fo = None if last else T.fout[:, t * L:(t + 1) * L]
-
-        def chain(a, b):
-            n = "_%d" % a
-            return [
-                lambda: ts(T.w1[:, a:b], T.b4[:, a:b], c("c1"), None, ALU.add, r=["c1"], w=["w1" + n], ps=["b4"]),
-                lambda: ts(T.w2[:, a:b], T.w1[:, a:b], 4095, None, ALU.bitwise_and, r=["w1" + n], w=["w2" + n]),
-                lambda: ts(T.mI[:, a:b], T.w2[:, a:b], c("sc3"), c("c2"), ALU.mult, ALU.add,
-                           r=["w2" + n, "sc3", "c2"], w=["mI" + n]),
-                lambda: tt(T.vf[:, a:b], T.mI[:, a:b], T.b3[:, a:b], ALU.mult, ["mI" + n], ["vf" + n], ["b3"]),
-                lambda: ts(T.uI[:, a:b], T.vf[:, a:b], 0.125, 3177.0625, ALU.mult, ALU.add, r=["vf" + n], w=["uI" + n]),
-                lambda: ts(T.h32[:, a:b], T.uI[:, a:b], 4095, None, ALU.bitwise_and, r=["uI" + n], w=["h32" + n]),
-                lambda: cp(T.h16[:, a:b], T.h32[:, a:b], ["h32" + n], ["h16" + n]),
-            ]
-        ch = [chain(a, b) for a, b in H2]
-        weave(*[x[:4] for x in ch])
-        if t == 0:
-            Xn = [widen("s", 0, PW4), widen("s", PW4, 2 * PW4)]
-        weave(*[x[4:] for x in ch])
-        h16n, h32n = ["h16_%d" % a for a, b in H2], ["h32_%d" % a for a, b in H2]
-
-        def leaves():
-            if t == 2:
-                cp(fo, T.w2[:], ["w2_%d" % a for a, b in H2], ["fout%d" % t])
+        for j in range(8):
+            e, src, n = E[:, 8 * h + j, 0:HL - 16 * j], keys[:, h * HL + 16 * j:(h + 1) * HL], en + "%d" % (8 * h + j)
+            if shift is None:
+                ts(e, src, scal(8 * h + j), None, ALU.is_equal, r=[kn, sn], w=[n], fast=True)
             else:
-                act(fo, T.b4[:, 0:L], w=["fout%d" % t], ps=["b4"])
-            send(nxt, T.fin[:, t * L:(t + 1) * L], fo, "farr%d" % (t + 1), ["fout%d" % t])
-        if t == 0:
-            leaves()
-            load_counters()
-        if t in (2, 3):
-            arrival("zhome%d" % t, "harr%d" % (t - 1), len(topo.engines(T.cores[(rank + D * (t - 1)) % N], core)))
-            add("y", lambda t=t: g.sync.dma_start(T.zs[:, (t - 1) * L:t * L], T.zhome[:, (t - 2) * L:(t - 1) * L]),
-                ["zhome%d" % t], (), sem="out")
-        if last:
-            add("y", lambda z=z: g.sync.dma_start(T.zs[:, 3 * L:4 * L], z), [zn], (), sem="out")
-        if t == 0:
-            late_constants()
-            Xn += [widen("v", 2 * PW4, 3 * PW4), widen("s", 3 * PW4, 3 * PW4 + 640), widen("v", 3 * PW4 + 640, W)]
-        def hn(a, b):
-            return ["h16_%d" % aa for aa, bb in H2 if aa < b and bb > a]
-        for i, (a, b) in enumerate(S_GATH):
-            add("s", lambda a=a, b=b: g.scalar.activation(T.xk[:, 16 * a:16 * b], Xc.indirect(T.h16[:, a:b]), ACT.Copy),
-                Xn + hn(a, b), ["xk%d" % a])
-            if i == 0:
-                act(T.pb[:], T.b3[:, 0:L], bias=-148.5, scale=0.5, w=["pb"], ps=["b3"])
-        if t in (1, 3):
-            leaves()
-        if t == 2:
-            leaves()
-        for a, b in V_GATH:
-            add("v", lambda a=a, b=b: g.vector.tensor_copy(T.xk[:, 16 * a:16 * b], Xc.indirect(T.h16[:, a:b])),
-                Xn + hn(a, b), ["xk%d" % a])
-        if t == 0:
-            later_constants()
-        allxk = ["xk%d" % a for a, b in S_GATH + V_GATH]
-        rootf = firsts(T.pb, "pb", T.pT, "pT", "b7", "E2")
-        for ci, (a, b) in enumerate(CHUNKS):
-            need = ["xk%d" % aa for aa, bb in S_GATH + V_GATH if aa < b and bb > a]
+                ts(e, src, c(shift), scal(8 * h + j), ALU.add, ALU.is_equal, r=[kn, sn, shift], w=[n], fast=True)
+            if j < 7:
+                mm(b, T[b][:, out + 16 * j + 16:out + HL], T.BOm[:], E[:, 8 * h + j, 16:HL - 16 * j], False, False,
+                   ["BOm", n])
+        mm(b, T[b][:, out:out + HL], T.Wm[:], E[:, 8 * h:8 * h + 8, 0:16], False, stop,
+           ["Wm"] + [en + "%d" % (8 * h + j) for j in range(8)])
 
-            def level(k, a=a, b=b, ci=ci, need=need):
-                mm("b1", T.b1[:, a:b], T.Sn[:, 15 - k:143 - k], T.xk[:, 16 * a + k:16 * b:16], False, False, ["Sn"] + need)
-                tt(T.mx[:, k * L + a:k * L + b], T.xk[:, 16 * a + k:16 * b:16], T.b0[:, a:b], ALU.max,
-                   need, ["mx%d_%d" % (ci, k)], ["b0"])
-                mm("b1", T.b1[:, a:b], T.S2[:, 15 - k:143 - k], T.mx[:, k * L + a:k * L + b], False,
-                   ci == len(CHUNKS) - 1 and k == 14, ["S2", "mx%d_%d" % (ci, k)])
-            side = []
-            if ci == 0 and t == 0:
-                side = [gap_constants]
-            weave([lambda k=k: level(k) for k in range(15)], side)
-            if ci == 0:
-                for jj in range(16):
-                    mm("b2", T.b2[:, 0:16], T.SK[:, 15 - jj:143 - jj], T.pb[:, jj:L:16], jj == 0, jj == 15, ["SK", "pb"])
-            if ci == len(CHUNKS) - 2:
-                cp(T.pT[:], T.b2[:, 0:16], (), ["pT"], ["b2"])
-                late = [f(False) for f in rootf[:ROOT[0]]]
-        M, Mn = (c("th"), "th") if t == 0 else (c("M"), "M")
-        act(T.hit[:], T.b1[:, 0:L], ACT.Sign, bias=M, scale=-1.0, r=[Mn], w=["hit"], ps=["b1"])
-        mm("b6", T.b6[:, 0:L], T.H[:], T.xk[:, 15:W:16], True, False, ["H"] + allxk)
-        mm("b6", T.b6[:, 0:L], T.H[:], z, False, True, ["H", zn])
-        mm("b4", T.b4[:, L:L + 16], T.I[:], T.Y0[:], True, False, ["I", "Y0"])
-        ts(T.ti[:, 0:16], T.pT[:], 613.25, 36.625, ALU.mult, ALU.add, r=["pT"], w=["ti0"])
-        late += [f(False) for f in rootf[ROOT[0]:8]]
-        ts(T.ti[:, 16:32], T.ti[:, 0:16], 4095, None, ALU.bitwise_and, r=["ti0"], w=["ti1"])
-        late += [f(False) for f in rootf[max(8, ROOT[0]):]]
-        mm("b2", T.b2[:, 0:L], T.TE[:], T.hit[:], True, True, ["TE", "hit"])
-        weave(late[:ROOT[1]])
-        act(T.oh[:], T.b2[:, 0:L], ACT.Relu, bias=c("kh"), scale=0.5, r=["kh"], w=["oh"], ps=["b2"])
-        act(T.b0[:, 0:L], T.b2[:, 0:L], ACT.Relu, bias=c("kh"), scale=0.5, r=["kh"], w=["acc"], ps=["b2", "b0"],
-            acc=None if last else T.acc[:, 0:1])
-        act(T.avg[:], T.b6[:, 0:L], bias=111.75, w=["avg"], ps=["b6"])
+    def answers(t, h, xk):
+        s, s8, n = half(h)
+        last = t == STEPS - 1
+        st = slice(t * L + h * HL, t * L + (h + 1) * HL)
+        zb, db = ZB[h], DB[h]
+        M = "th" if t == 0 else "M"
+        stage(t, DUE["z%d" % h])
+        act(T.hit[:, s], T[db][:, q0], ACT.Sign, bias=c(M), scale=-1.0, r=[M], w=["hit" + n], ps=[db])
+        mm(db, T[db][:, q1], T.TE[:], T.hit[:, s], True, True, ["TE", "hit" + n])
+
+        def under(where):
+            if where == "psum":
+                act(T[zb][:, q1], T[db][:, q1], ACT.Relu, bias=c("kh"), scale=0.5, r=["kh"], ps=[db, zb])
+            else:
+                act(T.oh[:, s], T[db][:, q1], ACT.Relu, bias=c("kh"), scale=0.5, r=["kh"], w=["oh" + n, "acc" + n],
+                    ps=[db], acc=None if last else T.acc[:, h:h + 1])
+        for where in (("sbuf", "psum") if h else ("psum", "sbuf")):
+            under(where)
+        mm("b6", T.b6[:, s8], T.I[:], T.Y0[:], True, False, ["I", "Y0"])
         for j in range(16):
-            mm("b4", T.b4[:, L:L + 16], T.SJ[:, 15 - j:143 - j], T.oh[:, j:L:16], False, j == 15, ["SJ", "oh"])
-        tt(T.msk[:], T.h32[:], T.b0[:, 0:L], ALU.mult, h32n, ["msk"], ["b0"])
-        mm("b5", T.b5[:, 0:L], T.BO16[:], T.oh[:], True, False, ["BO16", "oh"])
-        mm("b5", T.b5[:, 0:L], T.BO32[:], T.msk[:], False, True, ["BO32", "msk"])
-        weave(late[ROOT[1]:ROOT[2]])
+            mm("b6", T.b6[:, s8], T.SJ[:, 15 - j:143 - j], T.oh[:, h * HL + j:(h + 1) * HL:16], False, j == 15,
+               ["SJ", "oh" + n])
+        cp(T.oY[:, s8], T.b6[:, s8], (), ["oY" + n], ["b6"])
+        win = T.xk[:, 16 * HL * h:16 * HL * (h + 1)]
+        add("v", lambda: g.vector.tensor_tensor(T.dz[:, s], win.indirect(T.oY[:, s8]), T.zin[:, st], ALU.subtract),
+            xk + ["oY" + n, "zin%d_%d" % (t, h)], ["dz" + n], (), 50 + HL * GATH)
+        zon = "zout%d_%d" % (t, h)
+        act(T.zout[:, st], T.dz[:, s], ACT.Abs, bias=-128.0, r=["dz" + n], w=[zon])
         if not last:
-            mm("b6", T.b6[:, L:L + 1], T.sel14[:], T.acc[:, 0:1], True, True, ["sel14", "acc"])
-        cp(T.oY[:], T.b4[:, L:L + 16], (), ["oY"], ["b4"])
-        tt(T.dz[:], T.xk[:, 0:W].indirect(T.oY[:]), z, ALU.subtract, allxk + ["oY", zn], ["dz"])
-        act(T.af[:], T.avg[:], bias=-96.0, r=["avg"], w=["af"])
-        act(zo, T.dz[:], ACT.Abs, bias=-32.0, r=["dz"], w=[zon])
+            send(nxt, T.zin[:, st.start + L:st.stop + L], T.zout[:, st], "zarr%d_%d" % (t + 1, h), [zon], 128 * 256)
+        stage(t, DUE["named%d" % h] - (0.2 if h == 0 else 0))
+        tt(T.msk[:, s], T.hf[:, s], T[zb][:, q1], ALU.mult, ["hf" + n], ["msk" + n], [zb])
+        mm(db, T[db][:, q2], T.BOb[:], T.oh[:, s], True, False, ["BOb", "oh" + n])
+        mm(db, T[db][:, q2], T.BOh[:], T.msk[:, s], False, True, ["BOh", "msk" + n])
+        stage(t, DUE["named%d" % h])
+        scan(T.sN[:, s], T.R2[:, s], T[db][:, q2], 0.0, ALU.add, ["R2"], ["sN" + n], [db])
+        cp(T.nrep[:, s], T[db][:, q2], (), ["nrep" + n], [db])
+        ts(T.oN[:, s8], T.sN[:, h * HL + 15:(h + 1) * HL:16], c("hold"), None, ALU.subtract, r=["sN" + n, "hold"],
+           w=["oN" + n])
+        act(T.tf[:, s], T.C[:, 0:CW].indirect(T.oN[:, s8]), ACT.Relu, bias=1.0 if last else ONE, scale=-2.0,
+            r=["C", "oN" + n], w=["tf" + n], cost=65 + HL * GATH)
+        act(T.yf[:, s], win.indirect(T.oY[:, s8]), bias=-127.75, r=xk + ["oY" + n], w=["yf" + n], cost=65 + HL * GATH)
+        mm(db, T[db][:, q3], T.I[:], T.Cm0[:, s], True, False, ["I", "Cm0"])
+        mm(db, T[db][:, q3], T.BOb[:], T.oh[:, s], False, False, ["BOb", "oh" + n])
+        mm(db, T[db][:, q3], T.BOh[:], T.msk[:, s], False, False, ["BOh", "msk" + n])
+        matches(h, T.nrep, "nrep" + n, "hold", lambda j: T.sN[:, 16 * j + 15:16 * j + 16], "sN" + n, "E", db, 3 * HL, False)
+        cs = "Cs1" if last else "Cs"
+        mm(db, T[db][:, q3], T[cs][:], T.tf[:, s], False, True, [cs, "tf" + n], True)
+        scan(T.sV[:, s], T.RF[:, s], T[db][:, q3], BIG, ALU.min, ["RF"], ["sV" + n], [db])
+        cp(T.oX[:, s8], T.sV[:, h * HL + 15:(h + 1) * HL:16], ["sV" + n], ["oX" + n])
+
+    def roots(t):
+        stage(t, DUE["roots"])
+        for j in range(16):
+            mm("b7", T.b7[:, L:L + 16], T.SK[:, 15 - j:143 - j], T.pb[:, j:L:16], j == 0, j == 15, ["SK"] + both("pb"))
+        cp(T.pT[:], T.b7[:, L:L + 16], (), ["pT"], ["b7"])
+        mm("b7", T.b7[:, 0:L], T.I[:], T.Cm1[:], True, False, ["I", "Cm1"])
+        mm("b7", T.b7[:, 0:L], T.R15[:], T.hf[:], False, False, ["R15"] + both("hf"))
+        for h in (1, 0):
+            matches(h, T.pb, "pb_%d" % h, None, lambda j: T.pT[:, j:j + 1], "pT", "E2", "b7", h * HL, h == 0)
+        scan(T.sU[:], T.RF[:], T.b7[:, 0:L], BIG, ALU.min, ["RF"], ["sU"], ["b7"])
+        cp(T.oR[:], T.sU[:, 15:L:16], ["sU"], ["oR"])
+
+    def means(t, xk):
+        stage(t, DUE["means"])
+        mm("b6", T.b6[:, L:2 * L], T.H[:], T.xk[:, 15:W:16], True, False, ["H"] + xk)
+        mm("b6", T.b6[:, L:2 * L], T.H[:], T.zin[:, t * L:(t + 1) * L], False, True, ["H"] + both("zin%d" % t))
+        act(T.af[:], T.b6[:, L:2 * L], bias=-64.1, w=["af"], ps=["b6"])
+
+    stage(-1, DUE["paths1"])
+    paths(0, 1)
+    for t in range(STEPS):
+        last = t == STEPS - 1
+        zt = slice(t * L, (t + 1) * L)
+        stage(t, DUE["paths0"])
+        paths(t, 0)
         if not last:
-            send(nxt, T.zin[:, (t + 1) * L:(t + 2) * L], zo, "zarr%d" % (t + 1), [zon])
+            stage(t, DUE["leaves"])
+            send(nxt, T.fin[:, (t + 1) * L:(t + 2) * L], T.mI[:, zt], "farr%d" % (t + 1), both("mI%d" % t), 128 * 1024)
+        xk1 = records(t, 1)
+        answers(t, 1, xk1)
+        xk0 = records(t, 0)
+        answers(t, 0, xk0)
+        means(t, xk0 + xk1)
+        roots(t)
+        stage(t, DUE["home"])
         if t in (1, 2):
-            send((rank - D * t) % N, T.zhome[:, (t - 1) * L:t * L], zo, "harr%d" % t, [zon])
+            send((rank - D * t) % N, T.zhome[:, (t - 1) * L:t * L], T.zout[:, zt], "harr%d" % t, both("zout%d" % t), 128 * 512)
+            arrival("zhome%d" % t, "harr%d" % t, len(topo.engines(T.cores[(rank + D * t) % N], core)))
+            dma("y", T.zs[:, zt], T.zhome[:, (t - 1) * L:t * L], ["zhome%d" % t], (), "out")
         if t == 0 or last:
-            add("y", lambda t=t, zo=zo: g.sync.dma_start(T.zs[:, t * L:(t + 1) * L], zo), [zon], (), sem="out")
-        add("v", lambda: g.vector.tensor_tensor_scan(T.sN[:], T.R2[:], T.b5[:, 0:L], 0.0, ALU.add, ALU.max),
-            ["R2"], ["sN"], ["b5"])
-        cp(T.nrep[:], T.b5[:, 0:L], (), ["nrep"], ["b5"])
-        ts(T.nT[:], T.sN[:, 15:L:16], c("hold"), None, ALU.subtract, r=["sN", "hold"], w=["nT"])
-        ts(T.oN[:], T.sN[:, 15:L:16], c("hold"), None, ALU.subtract, r=["sN", "hold"], w=["oN"])
-        if t > 0:
-            add("s", lambda: g.scalar.activation(T.C[:, 0:XW].indirect(T.oC[:]), T.tf[:], ACT.Silu), ["oC", "tf"], ["C"])
-        add("s", lambda: g.scalar.activation(T.tb[:], T.C[:, 0:16 + W].indirect(T.oN[:]), ACT.Relu, bias=1.0, scale=-2.0),
-            ["C", "oN"], ["tb"])
-        add("s", lambda: g.scalar.activation(T.yf[:], T.xk[:, 0:W].indirect(T.oY[:]), ACT.Copy), allxk + ["oY"], ["yf"])
-        if not last:
-            act(T.tf[:], T.tb[:], scale=SILU_ONE, r=["tb"], w=["tf"])
-        weave(firsts(T.nrep, "nrep", T.nT, "nT", "b1", "E",
-                     lambda: mm("b1", T.b1[:, 0:L], T.Cs[:], T.tb[:], False, False, ["Cs", "tb"])))
-        weave(late[ROOT[2]:])
-        if not last:
-            pages(t + 1)
-        bound = [] if last else [
-            lambda: cp(T.ai[:, 0:1], T.b6[:, L:L + 1], (), ["ai0"], ["b6"]),
-            lambda: ts(T.ai[:, 1:2], T.ai[:, 0:1], 15, None, ALU.bitwise_and, r=["ai0"], w=["ai1"]),
-            lambda: ts(c("M"), T.ai[:, 1:2], c("th"), None, ALU.add, r=["ai1", "th"], w=["M"])]
-        if SU_FIRST:
-            scan(T.sU, "b7", "sU")
+            dma("y", T.zs[:, zt], T.zout[:, zt], both("zout%d" % t), (), "out")
+        if last:
+            dma("y", T.zs[:, 3 * L:4 * L], T.zin[:, zt], both("zin%d" % t), (), "out")
         else:
-            weave(bound[:2])
-        scan(T.sV, "b1", "sV")
-        root = [lambda: tt(T.tt[:, 0:16], T.sU[:, 15:L:16], T.DR[:], ALU.min, ["sU", "DR"], ["tt0"]),
-                lambda: tt(T.tt[:, 16:32], T.tt[:, 0:16], T.ti[:, 16:32], ALU.max, ["tt0", "ti1"], ["tt1"]),
-                lambda: cp(T.oR[:], T.tt[:, 16:32], ["tt1"], ["oR"])]
-        named = [lambda: tt(T.tt[:, 32:48], T.sV[:, 15:L:16], T.DX[:], ALU.min, ["sV", "DX"], ["tt2"]),
-                 lambda: tt(T.tt[:, 48:64], T.tt[:, 32:48], T.nT[:], ALU.max, ["tt2", "nT"], ["tt3"]),
-                 lambda: cp(T.oX[:], T.tt[:, 48:64], ["tt3"], ["oX"])]
-        count = [lambda: ts(T.tt[:, 64:80], T.sV[:, 15:L:16], -16384.0, None, ALU.add, r=["sV"], w=["tt4"]),
-                 lambda: tt(T.tt[:, 80:96], T.tt[:, 64:80], T.DX[:], ALU.min, ["tt4", "DX"], ["tt5"]),
-                 lambda: tt(T.tt[:, 96:112], T.tt[:, 80:96], T.nT[:], ALU.max, ["tt5", "nT"], ["tt6"]),
-                 lambda: cp(T.oC[:], T.tt[:, 96:112], ["tt6"], ["oC"])]
-        if SU_FIRST:
-            weave(root[:1])
-            weave(named, root[1:])
-            weave(count, bound)
-        else:
-            weave(named, count[:2])
-            scan(T.sU, "b7", "sU")
-            weave(count[2:3])
-            weave(root, count[3:] + bound[2:])
-        add("s", lambda Xn=Xn: g.scalar.activation(T.X[:, 0:XW].indirect(T.oX[:]), T.yf[:], ACT.Silu), ["oX", "yf"], Xn)
-        add("s", lambda: g.scalar.activation(T.X[:, 16:XW].indirect(T.oR[:]), T.af[:], ACT.Silu), ["oR", "af"], ["X"] + Xn,
-            strict=True)
-        Xn = ["X"]
+            stage(t, DUE["bound"])
+            for j in range(2):
+                for h in (1, 0):
+                    mm("b6", T.b6[:, 32 + j:33 + j], T.sel14[:], T.acc[:, h:h + 1], h == 1, h == 0 and j == 0,
+                       ["sel14", "acc_%d" % h], True)
+            mm("b6", T.b6[:, 33:34], T.I32[:], c("th"), False, True, ["I32", "th"], True)
+            ts(T.ai[:, 0:1], T.b6[:, 32:33], 0.0625, -0.46875, ALU.mult, ALU.add, w=["ai"], ps=["b6"])
+            ts(c("M"), T.ai[:, 0:1], -16.0, T.b6[:, 33:34], ALU.mult, ALU.add, r=["ai"], w=["M"], ps=["b6"])
+        stage(t, DUE["write"])
+        for h in (1, 0):
+            s, s8, n = half(h)
+            scatter(T.X[:, 0:XW], T.oX[:, s8], T.yf[:, s], HL, ["oX" + n, "yf" + n], ["X"])
+        for h in (1, 0):
+            s, s8, n = half(h)
+            scatter(T.X[:, 0:CW], T.oR[:, s8], T.af[:, s], HL, ["oR", "af"], ["X"])
+        stage(t, DUE["counters"])
+        ts(T.tt[:, 0:16], T.sV[:, 15:L:16], CW - 0.5, -float(AWAY), ALU.is_gt, ALU.mult, r=both("sV"), w=["tt0"])
+        tt(T.tt[:, 16:32], T.tt[:, 0:16], T.sV[:, 15:L:16], ALU.add, both("sV") + ["tt0"], ["tt1"])
+        cp(T.oC[:], T.tt[:, 16:32], ["tt1"], ["oC"])
+        for h in (1, 0):
+            s, s8, n = half(h)
+            if last:
+                add("v", lambda s=s, s8=s8: g.vector.tensor_copy(T.C2[:, 0:CW].indirect(T.oC[:, s8]), T.tf[:, s]),
+                    ["oC", "tf" + n], ["C2"], (), 50 + HL * SCAT, strict=STRICT)
+            else:
+                scatter(T.C[:, 0:CW], T.oC[:, s8], T.tf[:, s], HL, ["oC", "tf" + n], ["C"])
+        if t == STEPS - 2:
+            dma("g", T.Cb[0:128:16, :], T.C[0:128:16, BASE:CW], ["C"], ["Cb"], "lb", 8 * W * 4)
+            dma("g", T.C2[0:128:16, BASE:CW], T.Cb[0:128:16, :], ["Cb"], ["C2"], "l2", 8 * W * 4)
+        if not last:
+            stage(t, DUE["paths1"])
+            paths(t + 1, 1)
 
-    add("v", lambda: g.vector.tensor_copy(T.C[:, 0:XW].indirect(T.oC[:]), T.tb[:]), ["oC", "tb"], ["C"])
-    add("y", lambda: g.sync.dma_start(T.r32[:], T.C[0:128:16, 16:16 + W]), ["C"], ["r32"], sem="lo")
+    stage(STEPS - 1, DUE["sums"])
+    dma("y", T.cs[:, 0:TURN], T.C2[0:128:16, CW - TURN:CW], ["C2"], (), "out", 8 * W * 4)
+    dma("y", T.cs[:, TURN:W], T.C2[0:128:16, BASE:CW - TURN], ["C2"], (), "out", 8 * W * 4)
     for j2 in range(8):
-        a, b = j2 * 512, (j2 + 1) * 512
-        if j2 % 2:
-            act(T.xb[:, a:b], T.X[:, 16 + a:16 + b], r=["X"], w=["xe%d" % j2])
-        else:
-            cp(T.xb[:, a:b], T.X[:, 16 + a:16 + b], ["X"], ["xe%d" % j2])
+        cuts = [j2 * 512] + ([TURN] if TURN // 512 == j2 else []) + [(j2 + 1) * 512]
+        names = []
+        for a, b in zip(cuts, cuts[1:]):
+            p = BASE + (a - TURN) % W
+            names.append("xe%d" % a)
+            if j2 % 2:
+                ts(T.xb[:, a:b], T.X[:, p:p + b - a], 128.0, None, ALU.add, r=["X"], w=names[-1:])
+            else:
+                act(T.xb[:, a:b], T.X[:, p:p + b - a], bias=128.0, r=["X"], w=names[-1:])
         for j in (2 * j2, 2 * j2 + 1):
-            mm("b6", T.b6[:, 0:L], T.SA[:, 15 - j:143 - j], T.xb[:, j * L:(j + 1) * L], j == 0, j == 15, ["SA", "xe%d" % j2])
-    ts(T.tf[:], T.r32[:], 0.5, None, ALU.is_gt, r=["r32"], w=["tf"])
-    add("s", lambda: g.scalar.dma_start(T.cs[:], T.tf[:]), ["tf"], (), sem="out")
-    ts(T.xo[:], T.b6[:, 0:L], 0.5, c("asum"), ALU.mult, ALU.add, r=["asum"], w=["xo"], ps=["b6"])
-    add("y", lambda: g.sync.dma_start(T.xs[:], T.xo[:]), ["xo"], (), sem="out")
+            mm("b7", T.b7[:, 0:L], T.SA[:, 15 - j:143 - j], T.xb[:, j * L:(j + 1) * L], j == 0, j == 15, ["SA"] + names)
+    ts(T.xo[:], T.b7[:, 0:L], 4.0, c("asum"), ALU.mult, ALU.add, r=["asum"], w=["xo"], ps=["b7"])
+    dma("y", T.xs[:], T.xo[:], ["xo"], (), "out")
 
+    if not ORDER:
+        ORDER.extend(put_in_order(ops))
+    order = ORDER
+    place = {i: p for p, i in enumerate(order)}
     needed = set()
     for o in ops:
         best = {}
         for j in o["deps"]:
-            if ops[j]["sem"] is None:
-                best[ops[j]["q"]] = max(best.get(ops[j]["q"], -1), j)
+            if ops[j]["sem"] is None and place[j] > place.get(best.get(ops[j]["q"]), -1):
+                best[ops[j]["q"]] = j
         needed.update(best.values())
     count, total = {}, {}
-    for i, o in enumerate(ops):
+    for i in order:
+        o = ops[i]
         s = o["sem"] if o["sem"] is not None else "q" + o["q"]
         if o["sem"] is not None or i in needed:
             total[s] = total.get(s, 0) + (o["inc"] if o["sem"] is not None else 1)
         count[i] = (s, total.get(s, 0))
     seen, most = {}, {}
-    for i, o in enumerate(ops):
+    for i in order:
+        o = ops[i]
         q = o["q"]
         if q is None:
             continue

@@ -12,15 +12,19 @@ AWAY = 41 * 107
 XW = 8768
 BIG = float(2 ** 30)
 MAGIC = 1.5 * 2 ** 23
-V_GATH = 32
-S_CHUNK = 32
+V_GATH = 64
+S_CHUNK = 64
 C_S = 2304
 STRICT = False
-CYC, PE_CYC, GATH, SCAT, WAKE, LOOK = 0.92, 0.46, 1.25, 3.0, 220.0, 150.0
-DMA_LAT, REMOTE_LAT, DMA_RATE = 2000.0, 2300.0, 250.0
-ROUNDS = 1
+Y_SCAN = True
+V_HIT = 2
+CYC, PE_CYC, GATH, SCAT, WAKE = 1.0, 0.5, 1.25, 3.2, 200.0
+LOOK = 60.0
+DMA_LAT, REMOTE_LAT, DMA_RATE = 1600.0, 2000.0, 250.0
+ROUNDS = 6
 PERIOD = 11.5
-DUE = {"paths0": -3.0, "leaves": 1.0, "gather": 0.0, "chunk": 0.7, "near": (1.0, 2.3, 3.9, 5.3), "z1": 3.0, "z0": 5.5,
+DUE = {"paths0": -3.0, "leaves": 1.0, "gather": 0.0, "chunk": 0.7, "near0": 1.0, "near1": 2.3, "near2": 3.9,
+       "near3": 5.3, "z1": 3.0, "z0": 5.5,
        "named1": 6.0, "named0": 5.6, "roots": 6.5, "means": 6.4, "write": 7.0, "paths1": 5.4, "counters": 10.0,
        "bound": 9.0, "home": 8.0, "sums": 12.0}
 
@@ -37,7 +41,7 @@ SCRATCH = {
     "pI": ("sbuf", [128, 4], "int32"), "col": ("sbuf", [128, 40], "float32"),
     "im": ("sbuf", [128, 144], "bfloat16"), "ig": ("sbuf", [128, 128], "bfloat16"),
     "ic": ("sbuf", [128, L], "bfloat16"), "ib": ("sbuf", [128, 16], "float32"),
-    "ones": ("sbuf", [128, L], "bfloat16"), "onef": ("sbuf", [128, HL], "float32"),
+    "ones": ("sbuf", [128, L], "bfloat16"), "sY": ("sbuf", [128, L], "float32"),
     "dm": ("sbuf", [128, 32], "float32"),
     "Cm0": ("sbuf", [128, L], "bfloat16"), "Cm1": ("sbuf", [128, L], "bfloat16"), "RF": ("sbuf", [128, L], "bfloat16"),
     "R2": ("sbuf", [128, L], "bfloat16"), "Y0": ("sbuf", [128, 8], "bfloat16"),
@@ -56,7 +60,7 @@ SCRATCH = {
 }
 for _n in ("S2", "Sn", "SA", "SJ", "SK"):
     SCRATCH[_n] = ("sbuf", [128, 144], "bfloat16")
-for _n in ("I", "H", "BO", "BOn", "BOm", "BOb", "Wm", "A2", "TE", "TE0", "dg1", "QM", "Bm", "Bin", "c128", "tiny"):
+for _n in ("I", "H", "BO", "BOn", "BOm", "BOb", "Wm", "A2", "TE", "TE0", "dg1", "Bm", "Bin", "c128", "tiny", "BOj", "Yr"):
     SCRATCH[_n] = ("sbuf", [128, 128], "bfloat16")
 for _n in ("N64", "BOh", "R15", "c809", "c1025"):
     SCRATCH[_n] = ("sbuf", [128, 128], "float16")
@@ -267,9 +271,8 @@ def rank_program(g, core, T, topo):
     iota(T.im[:], [[1, 144]], 0, 0, "im")
     iota(T.ic[:], [[0, 16], [1, 16]], 0, 0, "ic")
     iota(T.ib[:], [[16, 16]], 0, 0, "ib")
-    dma("g", T.LI[0:128:16, L:L + 1], T.th[:], (), ["LIt"], "lt", allow_slow_non_contiguous=True)
+    dma("g", T.LI[0:128:16, L:L + 1], T.th[:], (), ["LIt"], "lt", 2500 * DMA_RATE, allow_slow_non_contiguous=True)
     ms(T.ones[:], 1.0, ["ones"])
-    ms(T.onef[:], 1.0, ["onef"])
     ms(T.c128[0:32, :], 128.0, ["c128"])
     ms(T.tiny[0:32, :], 2.0 ** -17, ["tiny"])
     ts(T.c809[0:32, :], T.ones[0:32, 0:128], 809.0, None, ALU.mult, r=["ones"], w=["c809"], fast=True)
@@ -297,11 +300,15 @@ def rank_program(g, core, T, topo):
     mat("dg1", "im", "p", "pw", ALU.is_equal, ALU.mult)
     mm("b7", T.b7[:, 0:128], T.BO[:], T.dg1[:], True, True, ["BO", "dg1"])
     cc("k0", "k", 0.0, 8.0, ALU.is_equal, ALU.mult)
-    ts(T.L8[:], T.b7[:, 0:128], c("k0"), None, ALU.mult, r=["k0"], w=["L8"], ps=["b7"])
+    cc("e15", "k", 15.0, None, ALU.is_equal)
+    cc("r15", "e15", -19615.5 / 2453, "k0", ALU.mult, ALU.add)
+    cc("h15", "e15", -0.5 / 2453, None, ALU.mult)
+    cc("f15", "e15", 2452.0, None, ALU.add)
+    act(T.DG[:], T.BO[:], scale=c("h15"), r=["BO", "h15"], w=["DG"])
+    ts(T.Cs1[:], T.b7[:, 0:128], c("r15"), None, ALU.mult, r=["r15"], w=["Cs1"], ps=["b7"])
+    tt(T.L8[:], T.Cs1[:], T.DG[:], ALU.add, ["Cs1", "DG"], ["L8"])
     ts(T.Bm[:], T.b7[:, 0:128], T.wf[:, 1:2], 4.0, ALU.mult, ALU.mult, r=["wf"], w=["Bm"], ps=["b7"])
-    ts(T.fin[:, 0:L], T.LI[:, 0:L], 0.125, 2452.0, ALU.mult, ALU.add, r=["LI"], w=["fin0"])
-    cc("ck", "pw", -19615.5, -0.5, ALU.mult, ALU.add)
-    mat("DG", "im", "p", "ck", ALU.is_equal, ALU.mult)
+    ts(T.fin[:, 0:L], T.LI[:, 0:L], 0.125, c("f15"), ALU.mult, ALU.add, r=["LI", "f15"], w=["fin0"])
     cc("nT", "pw", -32768.0, -4096.0, ALU.mult, ALU.max)
     cc("bq", "nT", 128.5, -0.5, ALU.mult, ALU.add)
     cc("k4", "k", 4.0, "pw", ALU.is_ge, ALU.mult)
@@ -315,11 +322,15 @@ def rank_program(g, core, T, topo):
     mat("S2", "im", "g15", 2.0, ALU.is_equal, ALU.mult)
     mat("Sn", "im", "g15", -1.0, ALU.is_equal, ALU.mult)
     cc("kp1", "k", 1.0, None, ALU.add)
-    mat("SJ", "im", "g15", "kp1", ALU.is_equal, ALU.mult)
+    if Y_SCAN:
+        mat("BOj", "BO", "kp1", None, ALU.mult)
+        mat("Yr", "im", 16.0, None, ALU.mult)
+    else:
+        mat("SJ", "im", "g15", "kp1", ALU.is_equal, ALU.mult)
+        ts(T.Y0[:], T.ib[:, 0:8], c("k"), 16.0, ALU.add, ALU.mult, r=["ib", "k"], w=["Y0"])
     mat("SK", "im", "g15", 0.0625, ALU.is_equal, ALU.mult)
     ts(T.SA[:], T.im[:], c("g15"), T.wf[:, 0:1], ALU.is_equal, ALU.mult, r=["im", "g15", "wf"], w=["SA"], fast=True)
     mat("Cm0", "ic", "k", -BIG, ALU.not_equal, ALU.mult)
-    cc("e15", "k", 15.0, None, ALU.is_equal)
     cc("k14", "k", 14.0, None, ALU.is_equal)
     cc("hold", "k", -8192.0, 15 * 8192.0, ALU.mult, ALU.add)
     cc("big15", "e15", 4096.0, 2048.5, ALU.mult, ALU.add)
@@ -329,12 +340,10 @@ def rank_program(g, core, T, topo):
     mat("R15", "BO", "e15", None, ALU.mult)
     ms(T.RF[:], BIG, ["RF0"])
     ts(T.RF[:, 0:L:16], T.ib[:], -1.0, c("top"), ALU.mult, ALU.add, r=["ib", "top", "RF0"], w=["RF"])
-    ts(T.Y0[:], T.ib[:, 0:8], c("k"), 16.0, ALU.add, ALU.mult, r=["ib", "k"], w=["Y0"])
     act(T.BOn[:], T.BO[:], scale=-1.0, r=["BO"], w=["BOn"])
     act(T.BOm[:], T.BO[:], scale=-32768.0, r=["BO"], w=["BOm"])
     act(T.BOb[:], T.BO[:], scale=2048.0 + BASE, r=["BO"], w=["BOb"])
     act(T.BO32[:], T.BO[:], r=["BO"], w=["BO32"])
-    act(T.I32[:], T.I[:], r=["I"], w=["I32"])
     act(T.H[:], T.I[:], scale=0.5, r=["I"], w=["H"])
     act(T.sel14[:], T.ones[:, 0:128], scale=c("k14"), r=["ones", "k14"], w=["sel14"])
     cc("k0a", "k0", AWAY / ONE / 8, None, ALU.mult)
@@ -370,8 +379,7 @@ def rank_program(g, core, T, topo):
             if h == 1:
                 arrival("fin%d" % t, "farr%d" % t, n_in)
             arrival(zn, "zarr%d_%d" % (t, h), n_in)
-        mm("b5", T.b5[:, q0], T.DG[:], T.onef[:], True, False, ["DG", "onef"], True)
-        mm("b5", T.b5[:, q0], T.L8[:], T.fin[:, st], False, t == 0, ["L8", "fin%d" % t], True)
+        mm("b5", T.b5[:, q0], T.L8[:], T.fin[:, st], True, t == 0, ["L8", "fin%d" % t], True)
         mm("b4", T.b4[:, q0], T.c809[0:1, :], T.c1025[0:1, :], True, False, ["c809", "c1025"])
         if t > 0:
             mm("b5", T.b5[:, q0], T.Bin[:], z, False, True, ["Bin", zn])
@@ -411,7 +419,7 @@ def rank_program(g, core, T, topo):
         if h and V_GATH:
             parts.append((HL, HL + V_GATH))
         for a in (h * HL, h * HL + 64):
-            stage(t, DUE["near"][(a - HL) % L // 64])
+            stage(t, DUE["near%d" % ((a - HL) % L // 64)])
             if a == h * HL:
                 mm(db, T[db][:, q0], T.BOn[:], T.zin[:, t * L + h * HL:t * L + (h + 1) * HL], True, False,
                    ["BOn", "zin%d_%d" % (t, h)])
@@ -446,22 +454,36 @@ def rank_program(g, core, T, topo):
         zb, db = ZB[h], DB[h]
         M = "th" if t == 0 else "M"
         stage(t, DUE["z%d" % h])
-        act(T.hit[:, s], T[db][:, q0], ACT.Sign, bias=c(M), scale=-1.0, r=[M], w=["hit" + n], ps=[db])
+        on_v = h and V_HIT
+        bias, scale = (0.0, 1.0) if on_v else (c("kh"), 0.5)
+        if on_v:
+            ts(T.hit[:, s], T[db][:, q0], c(M), None, ALU.is_le, r=[M], w=["hit" + n], ps=[db])
+        else:
+            act(T.hit[:, s], T[db][:, q0], ACT.Sign, bias=c(M), scale=-1.0, r=[M], w=["hit" + n], ps=[db])
         mm(db, T[db][:, q1], T.TE[:], T.hit[:, s], True, True, ["TE", "hit" + n])
-
-        def under(where):
-            if where == "psum":
-                act(T[zb][:, q1], T[db][:, q1], ACT.Relu, bias=c("kh"), scale=0.5, r=["kh"], ps=[db, zb])
-            else:
-                act(T.oh[:, s], T[db][:, q1], ACT.Relu, bias=c("kh"), scale=0.5, r=["kh"], w=["oh" + n, "acc" + n],
-                    ps=[db], acc=None if last else T.acc[:, h:h + 1])
-        for where in (("sbuf", "psum") if h else ("psum", "sbuf")):
-            under(where)
-        mm("b6", T.b6[:, s8], T.I[:], T.Y0[:], True, False, ["I", "Y0"])
-        for j in range(16):
-            mm("b6", T.b6[:, s8], T.SJ[:, 15 - j:143 - j], T.oh[:, h * HL + j:(h + 1) * HL:16], False, j == 15,
-               ["SJ", "oh" + n])
-        cp(T.oY[:, s8], T.b6[:, s8], (), ["oY" + n], ["b6"])
+        acc = None if last else T.acc[:, h:h + 1]
+        if on_v and V_HIT > 1:
+            ts(T.oh[:, s], T[db][:, q1], 0.0, None, ALU.max, w=["oh" + n], ps=[db])
+            act(T[zb][:, q1], T[db][:, q1], ACT.Relu, w=["acc" + n], ps=[db, zb], acc=acc)
+        else:
+            for where in (("sbuf", "psum") if h else ("psum", "sbuf")):
+                if where == "psum":
+                    act(T[zb][:, q1], T[db][:, q1], ACT.Relu, bias=bias, scale=scale, r=["kh"], ps=[db, zb])
+                else:
+                    act(T.oh[:, s], T[db][:, q1], ACT.Relu, bias=bias, scale=scale, r=["kh"], w=["oh" + n, "acc" + n],
+                        ps=[db], acc=acc)
+        if Y_SCAN:
+            mm("b6", T.b6[:, q0], T.I[:], T.Yr[:], True, False, ["I", "Yr"])
+            mm("b6", T.b6[:, q0], T.BOj[:], T.oh[:, s], False, True, ["BOj", "oh" + n])
+            scan(T.sY[:, s], T.R2[:, s], T.b6[:, q0], 0.0, ALU.add, ["R2"], ["sY" + n], ["b6"])
+            ts(T.oY[:, s8], T.sY[:, h * HL + 15:(h + 1) * HL:16], c("hold"), None, ALU.subtract, r=["sY" + n, "hold"],
+               w=["oY" + n])
+        else:
+            mm("b6", T.b6[:, s8], T.I[:], T.Y0[:], True, False, ["I", "Y0"])
+            for j in range(16):
+                mm("b6", T.b6[:, s8], T.SJ[:, 15 - j:143 - j], T.oh[:, h * HL + j:(h + 1) * HL:16], False, j == 15,
+                   ["SJ", "oh" + n])
+            cp(T.oY[:, s8], T.b6[:, s8], (), ["oY" + n], ["b6"])
         win = T.xk[:, 16 * HL * h:16 * HL * (h + 1)]
         add("v", lambda: g.vector.tensor_tensor(T.dz[:, s], win.indirect(T.oY[:, s8]), T.zin[:, st], ALU.subtract),
             xk + ["oY" + n, "zin%d_%d" % (t, h)], ["dz" + n], (), 50 + HL * GATH)
@@ -535,13 +557,12 @@ def rank_program(g, core, T, topo):
             dma("y", T.zs[:, 3 * L:4 * L], T.zin[:, zt], both("zin%d" % t), (), "out")
         else:
             stage(t, DUE["bound"])
-            for j in range(2):
-                for h in (1, 0):
-                    mm("b6", T.b6[:, 32 + j:33 + j], T.sel14[:], T.acc[:, h:h + 1], h == 1, h == 0 and j == 0,
-                       ["sel14", "acc_%d" % h], True)
-            mm("b6", T.b6[:, 33:34], T.I32[:], c("th"), False, True, ["I32", "th"], True)
-            ts(T.ai[:, 0:1], T.b6[:, 32:33], 0.0625, -0.46875, ALU.mult, ALU.add, w=["ai"], ps=["b6"])
-            ts(c("M"), T.ai[:, 0:1], -16.0, T.b6[:, 33:34], ALU.mult, ALU.add, r=["ai"], w=["M"], ps=["b6"])
+            for h in (1, 0):
+                mm("b6", T.b6[:, q1.start:q1.start + 1], T.sel14[:], T.acc[:, h:h + 1], h == 1, h == 0,
+                   ["sel14", "acc_%d" % h], True)
+            cp(T.ai[:, 0:1], T.b6[:, q1.start:q1.start + 1], (), ["ai0"], ["b6"])
+            ts(T.ai[:, 1:2], T.ai[:, 0:1], 15, None, ALU.bitwise_and, r=["ai0"], w=["ai1"])
+            ts(c("M"), T.ai[:, 1:2], c("th"), None, ALU.add, r=["ai1", "th"], w=["M"])
         stage(t, DUE["write"])
         for h in (1, 0):
             s, s8, n = half(h)

@@ -4,29 +4,40 @@ ALU = AluOpType
 ACT = ActivationFunctionType
 W, L, STEPS, D = 4096, 256, 5, 3
 HL = L // 2
-BASE = 272
+BASE = 512
 CW = BASE + W
 TURN = 3177
 ONE = 41 / 32
-AWAY = 41 * 107
-XW = 8768
+AWAY = 41 * 113
+XW = 9248
 BIG = float(2 ** 30)
 MAGIC = 1.5 * 2 ** 23
-V_GATH = 64
-S_CHUNK = 64
-C_S = 2304
+GATHERS = [[("s", 64), ("s", 32), ("v", 32)], [("v", 32), ("s", 32), ("s", 64)]]
+C_S = 3072
 STRICT = False
-Y_SCAN = True
-V_HIT = 2
-CYC, PE_CYC, GATH, SCAT, WAKE = 1.0, 0.5, 1.25, 3.2, 200.0
-LOOK = 60.0
-DMA_LAT, REMOTE_LAT, DMA_RATE = 1600.0, 2000.0, 250.0
-ROUNDS = 6
+CS_AT = 4
+V_OH = 0
+V_HIT = ()
+S_DZ = ()
+S_PT = 0
+P_Y = ()
+P_MOD = (1,)
+TURN_X = ()
+SX_AT = 13
+V_SX = ()
+P_YF = ()
+R_HALF = 0
+CYC, PE_CYC, GATH, SCAT, WAKE = 1.1, 0.66, 1.8, 4.5, 260.0
+LOOK = 0.45
+DMA_LAT, DMA_RATE = 1600.0, 250.0
+REMOTE_LAT = 2600.0
+ISSUE = 900.0
+ROUNDS = 5
 PERIOD = 11.5
-DUE = {"paths0": -3.0, "leaves": 1.0, "gather": 0.0, "chunk": 0.7, "near0": 1.0, "near1": 2.3, "near2": 3.9,
-       "near3": 5.3, "z1": 3.0, "z0": 5.5,
-       "named1": 6.0, "named0": 5.6, "roots": 6.5, "means": 6.4, "write": 7.0, "paths1": 5.4, "counters": 10.0,
-       "bound": 9.0, "home": 8.0, "sums": 12.0}
+DUE = {"paths0": 0.0, "leaves": 3.0, "gatherv1": -3.0, "gathers1": 0.0, "gatherv0": 3.0, "gathers0": 4.5, "near0": 1.0,
+       "near1": 1.8, "near2": 3.9, "near3": 9.3, "z1": 3.0, "z0": 4.5, "named1": 7.0, "named0": 6.1, "roots": 4.5,
+       "twins": 7.0, "means": 5.4, "write": 8.5, "paths1": 5.4, "counters": 10.0, "count": 13.5, "roots1": -1.5,
+       "twins1": -1.0, "roots0": 3.0, "twins0": 6.0, "bound": 13.0, "home": 9.0, "sums": 19.5}
 
 SCRATCH = {
     "X": ("sbuf", [128, XW], "float32"), "C": ("sbuf", [128, CW], "float32"), "C2": ("sbuf", [128, CW], "float32"),
@@ -44,12 +55,12 @@ SCRATCH = {
     "ones": ("sbuf", [128, L], "bfloat16"), "sY": ("sbuf", [128, L], "float32"),
     "dm": ("sbuf", [128, 32], "float32"),
     "Cm0": ("sbuf", [128, L], "bfloat16"), "Cm1": ("sbuf", [128, L], "bfloat16"), "RF": ("sbuf", [128, L], "bfloat16"),
-    "R2": ("sbuf", [128, L], "bfloat16"), "Y0": ("sbuf", [128, 8], "bfloat16"),
+    "R2": ("sbuf", [128, L], "bfloat16"), "Cm": ("sbuf", [128, L], "bfloat16"),
     "qq": ("sbuf", [128, L], "bfloat16"), "rb": ("sbuf", [128, L], "float16"), "pb": ("sbuf", [128, L], "bfloat16"),
     "vf": ("sbuf", [128, L], "float32"), "uI": ("sbuf", [128, L], "int32"), "h32": ("sbuf", [128, L], "int32"),
     "h16": ("sbuf", [128, L], "uint16"), "hf": ("sbuf", [128, L], "float16"), "msk": ("sbuf", [128, L], "float16"),
     "hit": ("sbuf", [128, L], "bfloat16"), "oh": ("sbuf", [128, L], "bfloat16"),
-    "dz": ("sbuf", [128, L], "bfloat16"), "nrep": ("sbuf", [128, L], "uint16"),
+    "dz": ("sbuf", [128, L], "bfloat16"), "sx": ("sbuf", [128, L], "bfloat16"), "nrep": ("sbuf", [128, L], "uint16"),
     "sN": ("sbuf", [128, L], "float32"), "sV": ("sbuf", [128, L], "float32"), "sU": ("sbuf", [128, L], "float32"),
     "tf": ("sbuf", [128, L], "float32"), "yf": ("sbuf", [128, L], "float32"), "af": ("sbuf", [128, L], "float32"),
     "pT": ("sbuf", [128, 16], "float32"), "tt": ("sbuf", [128, 32], "float32"),
@@ -60,7 +71,8 @@ SCRATCH = {
 }
 for _n in ("S2", "Sn", "SA", "SJ", "SK"):
     SCRATCH[_n] = ("sbuf", [128, 144], "bfloat16")
-for _n in ("I", "H", "BO", "BOn", "BOm", "BOb", "Wm", "A2", "TE", "TE0", "dg1", "Bm", "Bin", "c128", "tiny", "BOj", "Yr"):
+for _n in ("I", "H", "BO", "BOn", "BOm", "Back", "Wm", "A2", "TE", "TE0", "TE1", "TE2", "TE3", "Kc", "dg1", "Bm", "Bin",
+           "c128", "tiny", "BOj", "Yr", "dump", "In", "TEv", "Backv", "Y0", "c16"):
     SCRATCH[_n] = ("sbuf", [128, 128], "bfloat16")
 for _n in ("N64", "BOh", "R15", "c809", "c1025"):
     SCRATCH[_n] = ("sbuf", [128, 128], "float16")
@@ -70,7 +82,7 @@ for _b in range(8):
     SCRATCH["b%d" % _b] = ("psum", [128, 512], "float32")
 
 SEMAPHORES = (["qv", "qs", "qp", "qg", "sent", "out", "barr", "lz", "lw", "ll", "lt", "lc", "lx", "lX", "lb", "l2"]
-              + ["zarr%d_%d" % (t, h) for t in range(1, 5) for h in range(2)] + ["farr%d" % t for t in range(1, 5)]
+              + ["zarr%d_%d" % (t, h) for t in range(1, 5) for h in range(2)] + ["farr%d" % i for i in range(4)]
               + ["harr1", "harr2"])
 
 ORDER = []
@@ -99,7 +111,9 @@ def list_schedule(ops, edges, release, rank):
         for q, r in ready.items():
             if r:
                 t = max(free.get(q, 0.0), min(ready_at[i] for i in r))
-                i = max((i for i in r if ready_at[i] <= t + LOOK), key=lambda i: rank[i])
+                i = max((i for i in r if ready_at[i] <= t), key=lambda i: rank[i])
+                t2 = t + LOOK * ops[i]["cost"]
+                i = max((i for i in r if ready_at[i] <= t2), key=lambda i: rank[i])
                 t = max(t, ready_at[i])
                 if best is None or t < best[0]:
                     best = (t, i)
@@ -239,9 +253,10 @@ def rank_program(g, core, T, topo):
         rid, pid = topo.addr(dst, core)
         m = topo.mask(core, dst)
         nsent[0] += len(topo.engines(core, dst))
-        sends[sem] = add("g", lambda: g.remote_dma(out, in_, T.sem[sem], T.sem.sent, pid, rid, m), r, (), (), 600.0,
+        sends[sem] = add("g", lambda: g.remote_dma(out, in_, T.sem[sem], T.sem.sent, pid, rid, m), r, (), (), ISSUE,
                          REMOTE_LAT + size / 60, "-")
 
+    q0, q1, q2, q3 = [slice(i * HL, (i + 1) * HL) for i in range(4)]
     nxt, prv = (rank + D) % N, (rank - D) % N
     n_in = len(topo.engines(T.cores[prv], core))
     cols = {}
@@ -280,11 +295,11 @@ def rank_program(g, core, T, topo):
     act(T.C[:, 0:L], T.ones[:], ACT.Silu, scale=0.0, r=["ones"], w=["C0"], cost=1500.0)
     for a in range(L, C_S, L):
         act(T.C[:, a:a + L], T.ones[:], scale=0.0, r=["ones"], w=["C%d" % a])
-    for a in range(C_S, CW, 516):
-        iota(T.C[:, a:a + 516], [[0, 516]], 0, 0, "C%d" % a)
+    for a in range(C_S, CW, 512):
+        iota(T.C[:, a:a + 512], [[0, 512]], 0, 0, "C%d" % a)
     turned("g", T.C, BASE, T.c0, (), "C", "lc", 8 * W * 4,
-           ["C%d" % a for a in list(range(0, C_S, L)) + list(range(C_S, CW, 516))])
-    turned("g", T.X, BASE, T.x0, ["xb"], "X", "lX", 128 * W * 4)
+           ["C%d" % a for a in list(range(0, C_S, L)) + list(range(C_S, CW, 512))])
+    turned("g", T.X, BASE, T.x0, ["wi"], "X", "lX", 128 * W * 6)
 
     ts(T.pI[:, 1:2], T.pI[:, 0:1], 15, None, ALU.bitwise_and, r=["pI"], w=["kI"])
     ts(T.pI[:, 2:3], T.pI[:, 0:1], 4, None, ALU.arith_shift_right, r=["pI"], w=["gI"])
@@ -302,18 +317,15 @@ def rank_program(g, core, T, topo):
     cc("k0", "k", 0.0, 8.0, ALU.is_equal, ALU.mult)
     cc("e15", "k", 15.0, None, ALU.is_equal)
     cc("r15", "e15", -19615.5 / 2453, "k0", ALU.mult, ALU.add)
-    cc("h15", "e15", -0.5 / 2453, None, ALU.mult)
+    cc("h15", "e15", -0.5 / 2453 / 8, None, ALU.mult)
     cc("f15", "e15", 2452.0, None, ALU.add)
-    act(T.DG[:], T.BO[:], scale=c("h15"), r=["BO", "h15"], w=["DG"])
-    ts(T.Cs1[:], T.b7[:, 0:128], c("r15"), None, ALU.mult, r=["r15"], w=["Cs1"], ps=["b7"])
-    tt(T.L8[:], T.Cs1[:], T.DG[:], ALU.add, ["Cs1", "DG"], ["L8"])
+    ts(T.L8[:], T.b7[:, 0:128], c("r15"), c("h15"), ALU.mult, ALU.add, r=["r15", "h15"], w=["L8"], ps=["b7"])
     ts(T.Bm[:], T.b7[:, 0:128], T.wf[:, 1:2], 4.0, ALU.mult, ALU.mult, r=["wf"], w=["Bm"], ps=["b7"])
     ts(T.fin[:, 0:L], T.LI[:, 0:L], 0.125, c("f15"), ALU.mult, ALU.add, r=["LI", "f15"], w=["fin0"])
     cc("nT", "pw", -32768.0, -4096.0, ALU.mult, ALU.max)
     cc("bq", "nT", 128.5, -0.5, ALU.mult, ALU.add)
-    cc("k4", "k", 4.0, "pw", ALU.is_ge, ALU.mult)
-    cc("mg0", "nT", -129.0, MAGIC, ALU.mult, ALU.add)
-    cc("mg", "k4", 32768.0, "mg0", ALU.mult, ALU.add)
+    cc("mg0", "pw", 130 * 32768.0, 129 * 4096.0, ALU.mult, ALU.min)
+    cc("mg", "mg0", MAGIC, None, ALU.add)
     mat("N64", "I", -64.0, None, ALU.mult)
     send(nxt, T.Bin[:], T.Bm[:], "barr", ["Bm"], 128 * 256)
     arrival("Bin", "barr", n_in)
@@ -321,20 +333,26 @@ def rank_program(g, core, T, topo):
     cc("g15", "g", 16.0, 15.0, ALU.mult, ALU.add)
     mat("S2", "im", "g15", 2.0, ALU.is_equal, ALU.mult)
     mat("Sn", "im", "g15", -1.0, ALU.is_equal, ALU.mult)
-    cc("kp1", "k", 1.0, None, ALU.add)
-    if Y_SCAN:
+    cc("kp1", "k", 1.0, 2.0 ** -12, ALU.add, ALU.mult)
+    if len(P_Y) < 2:
         mat("BOj", "BO", "kp1", None, ALU.mult)
-        mat("Yr", "im", 16.0, None, ALU.mult)
-    else:
+        mat("Yr", "im", 16.0, -256.0, ALU.mult, ALU.add)
+    if P_Y:
         mat("SJ", "im", "g15", "kp1", ALU.is_equal, ALU.mult)
-        ts(T.Y0[:], T.ib[:, 0:8], c("k"), 16.0, ALU.add, ALU.mult, r=["ib", "k"], w=["Y0"])
+        ts(T.Y0[:, 0:8], T.ib[:, 0:8], c("k"), 16.0, ALU.add, ALU.mult, r=["ib", "k"], w=["Y0"])
     mat("SK", "im", "g15", 0.0625, ALU.is_equal, ALU.mult)
     ts(T.SA[:], T.im[:], c("g15"), T.wf[:, 0:1], ALU.is_equal, ALU.mult, r=["im", "g15", "wf"], w=["SA"], fast=True)
-    mat("Cm0", "ic", "k", -BIG, ALU.not_equal, ALU.mult)
-    cc("k14", "k", 14.0, None, ALU.is_equal)
-    cc("hold", "k", -8192.0, 15 * 8192.0, ALU.mult, ALU.add)
-    cc("big15", "e15", 4096.0, 2048.5, ALU.mult, ALU.add)
-    cc("kh", "k", -0.5, None, ALU.mult)
+    mat("Cm", "ic", "k", -BIG, ALU.not_equal, ALU.mult)
+    cc("k14", "k", 14.0, 2.0 ** -12, ALU.is_equal, ALU.mult)
+    cc("holdn", "k", -8192.0, 15 * 8192.0 - 256, ALU.mult, ALU.add)
+    cc("bk0", "k", -2048.0, 14 * 2048.0, ALU.mult, ALU.add)
+    cc("bk1", "k0", -32.0, "bk0", ALU.mult, ALU.add)
+    cc("bk", "e15", 137 * 2048.0, "bk1", ALU.mult, ALU.add)
+    act(T.Back[:], T.BO[:], scale=c("bk"), r=["BO", "bk"], w=["Back"])
+    ts(T.Kc[:], T.ic[:, 0:128], 1.0, -2048.0, ALU.add, ALU.mult, r=["ic"], w=["Kc"], fast=True)
+    mat("TE1", "BO", "e15", None, ALU.mult)
+    tt(T.TE3[:], T.TE1[:], T.Kc[:], ALU.mult, ["TE1", "Kc"], ["TE3"])
+    act(T.TE2[:], T.BO[:], scale=-2048.0, r=["BO"], w=["TE2"])
     cc("top", "k", -1.0, 256.0, ALU.mult, ALU.add)
     mat("BOh", "BO", 1.0, None, ALU.mult)
     mat("R15", "BO", "e15", None, ALU.mult)
@@ -342,28 +360,35 @@ def rank_program(g, core, T, topo):
     ts(T.RF[:, 0:L:16], T.ib[:], -1.0, c("top"), ALU.mult, ALU.add, r=["ib", "top", "RF0"], w=["RF"])
     act(T.BOn[:], T.BO[:], scale=-1.0, r=["BO"], w=["BOn"])
     act(T.BOm[:], T.BO[:], scale=-32768.0, r=["BO"], w=["BOm"])
-    act(T.BOb[:], T.BO[:], scale=2048.0 + BASE, r=["BO"], w=["BOb"])
     act(T.BO32[:], T.BO[:], r=["BO"], w=["BO32"])
     act(T.H[:], T.I[:], scale=0.5, r=["I"], w=["H"])
+    if len(TURN_X) == 1:
+        ms(T.c16[0:32, :], -16.0, ["c16"])
+    if S_DZ or TURN_X:
+        act(T.In[:], T.I[:], scale=-1.0, r=["I"], w=["In"])
     act(T.sel14[:], T.ones[:, 0:128], scale=c("k14"), r=["ones", "k14"], w=["sel14"])
     cc("k0a", "k0", AWAY / ONE / 8, None, ALU.mult)
-    cc("k0b", "k0", AWAY / 8, None, ALU.mult)
     act(T.Cs[:], T.BO[:], scale=c("k0a"), r=["BO", "k0a"], w=["Cs"])
-    act(T.Cs1[:], T.BO[:], scale=c("k0b"), r=["BO", "k0b"], w=["Cs1"])
-    act(T.R2[:], T.Cm0[:], bias=8192.0 - 2.0 ** 20, scale=-2.0 ** 20 / BIG, r=["Cm0"], w=["R2"])
-    act(T.Cm1[:], T.Cm0[:], bias=2048.0 + BASE, r=["Cm0"], w=["Cm1"])
+    act(T.Cs1[:], T.Cs[:], scale=ONE, r=["Cs"], w=["Cs1"])
+    act(T.R2[:, q0], T.Cm[:, q0], bias=8192.0 - 2.0 ** 20, scale=-2.0 ** 20 / BIG, r=["Cm"], w=["R2"])
+    act(T.Cm0[:, q0], T.Cm[:, q0], bias=256.0, r=["Cm"], w=["Cm0"])
+    act(T.Cm1[:], T.Cm[:], bias=2048.0 + BASE, r=["Cm"], w=["Cm1"])
     asel = 170 + 256 * CYC
-    add("g", lambda: g.affine_select(T.TE0[:], T.BOn[:], [[1, 128]], ALU.is_ge, 0.0, 1, -1), ["BOn"], ["TE0"], (), asel)
-    add("g", lambda: g.affine_select(T.TE[:], T.TE0[:], [[1, 128]], ALU.not_equal, 1.0, 1, -1), ["TE0"], ["TE"], (), asel)
+    add("g", lambda: g.affine_select(T.TE0[:], T.TE2[:], [[1, 128]], ALU.is_ge, 0.0, 0, -1), ["TE2"], ["TE0"], (), asel)
+    add("g", lambda: g.affine_select(T.TE2[:], T.TE0[:], [[1, 128]], ALU.not_equal, 2048.0, 1, -1), ["TE0"], ["TE2"], (), asel)
+    ms(T.TE2[:, 15:128:16], 0.0, ["TE2"])
+    tt(T.TE[:], T.TE2[:], T.TE3[:], ALU.add, ["TE2", "TE3"], ["TE"])
     add("g", lambda: g.affine_select(T.Wm[:], T.BOm[:], [[1, 128]], ALU.is_gt, 0.0, 0, -1), ["BOm"], ["Wm"], (), asel)
+    if V_HIT:
+        act(T.TEv[:], T.TE[:], scale=2.0, r=["TE"], w=["TEv"])
+        act(T.Backv[:], T.Back[:], scale=2.0, r=["Back"], w=["Backv"])
     cp(T.thf[:], T.LI[:, L:L + 2], ["LIt"], ["thf"])
     mm("b7", T.b7[:, 2:4], T.A2[:], T.ones[:, 0:2], True, True, ["A2", "ones"])
     mm("b7", T.b7[:, 0:2], T.BO32[:], T.thf[:], True, True, ["BO32", "thf"], True)
-    ts(c("th"), T.b7[:, 0:1], c("big15"), None, ALU.add, r=["big15"], w=["th"], ps=["b7"])
+    ts(c("th"), T.b7[:, 0:1], 4096.5 if len(TURN_X) == 2 else 2048.5, None, ALU.add, w=["th"], ps=["b7"])
     ts(c("asum"), T.b7[:, 2:3], -512.0, None, ALU.mult, w=["asum"], ps=["b7"])
 
     ZB, DB = ["b1", "b0"], ["b3", "b2"]
-    q0, q1, q2, q3 = [slice(i * HL, (i + 1) * HL) for i in range(4)]
 
     def half(h):
         return slice(h * HL, (h + 1) * HL), slice(h * 8, (h + 1) * 8), "_%d" % h
@@ -376,8 +401,6 @@ def rank_program(g, core, T, topo):
         st = slice(t * L + h * HL, t * L + (h + 1) * HL)
         z, zn, zb = T.zin[:, st], "zin%d_%d" % (t, h), ZB[h]
         if t > 0:
-            if h == 1:
-                arrival("fin%d" % t, "farr%d" % t, n_in)
             arrival(zn, "zarr%d_%d" % (t, h), n_in)
         mm("b5", T.b5[:, q0], T.L8[:], T.fin[:, st], True, t == 0, ["L8", "fin%d" % t], True)
         mm("b4", T.b4[:, q0], T.c809[0:1, :], T.c1025[0:1, :], True, False, ["c809", "c1025"])
@@ -387,11 +410,21 @@ def rank_program(g, core, T, topo):
         mm("b4", T.b4[:, q0], T.A2[:], z, False, False, ["A2", zn])
         act(T.qq[:, s], T.b5[:, q0], bias=c("bq"), scale=-1.0, r=["bq"], w=["qq" + n], ps=["b5"])
         ts(T.rb[:, s], T[zb][:, q2], 2.0 ** -6, 1619.0 - 255.0 / 512, ALU.mult, ALU.add, w=["rb" + n], ps=[zb])
-        tt(T.vf[:, s], T.qq[:, s], T.b5[:, q0], ALU.add, ["qq" + n], ["vf" + n], ["b5"])
+        db = DB[h]
+        if h in P_MOD:
+            mm(db, T[db][:, q0], T.L8[:], T.fin[:, st], True, False, ["L8", "fin%d" % t], True)
+            if t > 0:
+                mm(db, T[db][:, q0], T.Bin[:], z, False, False, ["Bin", zn])
+            mm(db, T[db][:, q0], T.I[:], T.qq[:, s], False, True, ["I", "qq" + n])
+        else:
+            tt(T.vf[:, s], T.qq[:, s], T.b5[:, q0], ALU.add, ["qq" + n], ["vf" + n], ["b5"])
         mm("b4", T.b4[:, q0], T.N64[:], T.rb[:, s], False, False, ["N64", "rb" + n])
         mm("b4", T.b4[:, q0], T.tiny[0:1, :], T.ones[0:1, 0:HL], False, True, ["tiny", "ones"])
         mn = "mI%d_%d" % (t, h)
-        ts(T.mI[:, st], T.vf[:, s], c("mg"), MAGIC - 2452.0, ALU.add, ALU.subtract, r=["mg", "vf" + n], w=[mn])
+        if h in P_MOD:
+            ts(T.mI[:, st], T[db][:, q0], c("mg"), MAGIC - 2452.0, ALU.add, ALU.subtract, r=["mg"], w=[mn], ps=[db])
+        else:
+            ts(T.mI[:, st], T.vf[:, s], c("mg"), MAGIC - 2452.0, ALU.add, ALU.subtract, r=["mg", "vf" + n], w=[mn])
         tt(T.uI[:, s], T.mI[:, st], T.b4[:, q0], ALU.mult, [mn], ["uI" + n], ["b4"])
         ts(T.h32[:, s], T.uI[:, s], 4095, None, ALU.bitwise_and, r=["uI" + n], w=["h32" + n])
         cp(T.h16[:, s], T.h32[:, s], ["h32" + n], ["h16" + n])
@@ -399,25 +432,28 @@ def rank_program(g, core, T, topo):
         mm(zb, T[zb][:, q0], T.I[:], z, False, True, ["I", zn])
         act(T.pb[:, s], T.b4[:, q0], bias=-148.5, scale=4.0, w=["pb" + n], ps=["b4"])
         ts(T.hf[:, s], T.h16[:, s], -2048.0, None, ALU.add, r=["h16" + n], w=["hf" + n], fast=True)
+        if t < STEPS - 1 and h == 0:
+            stage(t, DUE["leaves"])
+            send(nxt, T.fin[:, (t + 1) * L:(t + 2) * L], T.mI[:, t * L:(t + 1) * L], "farr%d" % t, both("mI%d" % t), 128 * 1024)
+            arrival("fin%d" % (t + 1), "farr%d" % t, n_in)
 
     def records(t, h):
         _, _, n = half(h)
         win, wn = (T.xb[:, 0:W], ["xb"]) if t == 0 else (T.X[:, BASE:CW], ["X"])
         zb, db = ZB[h], DB[h]
-        cuts = list(range(h * HL + (V_GATH if h else 0), (h + 1) * HL, S_CHUNK)) + [(h + 1) * HL]
-        parts = [(a, b) for a, b in zip(cuts, cuts[1:])]
-        if h and V_GATH:
-            a, b = HL, HL + V_GATH
-            stage(t, DUE["gather"])
-            add("v", lambda a=a, b=b: g.vector.tensor_scalar(T.xk[:, 16 * a:16 * b], win.indirect(T.h16[:, a:b]), 128.0,
-                                                             None, ALU.add),
-                wn + ["h16" + n], ["xk%d" % a], (), 50 + 16 * (b - a) * GATH)
-        for a, b in parts:
-            stage(t, DUE["gather"] + DUE["chunk"] * ((a - HL) % L - V_GATH) / S_CHUNK)
-            act(T.xk[:, 16 * a:16 * b], win.indirect(T.h16[:, a:b]), bias=128.0, r=wn + ["h16" + n],
-                w=["xk%d" % a, "in turn"], cost=65 + 16 * (b - a) * GATH)
-        if h and V_GATH:
-            parts.append((HL, HL + V_GATH))
+        parts, a = [], h * HL
+        for q, m in GATHERS[h]:
+            b = a + m
+            parts.append((a, b))
+            stage(t, DUE["gather%s%d" % (q, h)])
+            if q == "v":
+                add("v", lambda a=a, b=b: g.vector.tensor_scalar(T.xk[:, 16 * a:16 * b], win.indirect(T.h16[:, a:b]),
+                                                                 128.0, None, ALU.add),
+                    wn + ["h16" + n], ["xk%d" % a], (), 50 + 16 * m * GATH)
+            else:
+                act(T.xk[:, 16 * a:16 * b], win.indirect(T.h16[:, a:b]), bias=128.0, r=wn + ["h16" + n],
+                    w=["xk%d" % a, "in turn"], cost=65 + 16 * m * GATH)
+            a = b
         for a in (h * HL, h * HL + 64):
             stage(t, DUE["near%d" % ((a - HL) % L // 64)])
             if a == h * HL:
@@ -425,15 +461,27 @@ def rank_program(g, core, T, topo):
                    ["BOn", "zin%d_%d" % (t, h)])
             b, o = a + 64, slice(a - h * HL, a - h * HL + 64)
             need = ["xk%d" % aa for aa, bb in parts if aa < b and bb > a]
-            for k in range(15):
-                mm(db, T[db][:, o], T.Sn[:, 15 - k:143 - k], T.xk[:, 16 * a + k:16 * b:16], False, False, ["Sn"] + need)
+            if h not in TURN_X:
+                for k in range(15):
+                    mm(db, T[db][:, o], T.Sn[:, 15 - k:143 - k], T.xk[:, 16 * a + k:16 * b:16], False, False, ["Sn"] + need)
+            elif a > h * HL:
+                for k in range(16):
+                    mm("b5", T.b5[:, HL + k:L:16], T.xk[:, 16 * h * HL + k:16 * b:16], T.BO[:, 0:128:16], True, True,
+                       ["BO"] + ["xk%d" % aa for aa, bb in parts])
+                if h in V_SX:
+                    ts(T.sx[:, h * HL:(h + 1) * HL], T.b5[:, q1], -2048.0, None, ALU.add, w=["sx" + n], ps=["b5"])
+                else:
+                    act(T.sx[:, h * HL:(h + 1) * HL], T.b5[:, q1], bias=-2048.0, w=["sx" + n], ps=["b5"])
             for k in range(15):
                 x, m = T.xk[:, 16 * a + k:16 * b:16], T.mx[:, k * L + a:k * L + b]
                 tt(m, x, T[zb][:, o], ALU.max, need, ["mx%d_%d" % (a, k)], [zb])
+                if h in TURN_X and a > h * HL and k == SX_AT:
+                    mm(db, T[db][:, q0], T.sx[:, h * HL:(h + 1) * HL], T.In[:], False, False, ["sx" + n, "In"])
+                    mm(db, T[db][:, q0], T.c128[0:1, :], T.c16[0:1, :], False, False, ["c128", "c16"]) if len(TURN_X) < 2 else None
                 mm(db, T[db][:, o], T.S2[:, 15 - k:143 - k], m, False, a > h * HL and k == 14, ["S2", "mx%d_%d" % (a, k)])
         return ["xk%d" % a for a, b in parts]
 
-    def matches(h, keys, kn, shift, scal, sn, en, b, out, stop):
+    def matches(h, keys, kn, shift, scal, sn, en, b, out, stop, extra=None):
         E = T[en]
         for j in range(8):
             e, src, n = E[:, 8 * h + j, 0:HL - 16 * j], keys[:, h * HL + 16 * j:(h + 1) * HL], en + "%d" % (8 * h + j)
@@ -444,6 +492,8 @@ def rank_program(g, core, T, topo):
             if j < 7:
                 mm(b, T[b][:, out + 16 * j + 16:out + HL], T.BOm[:], E[:, 8 * h + j, 16:HL - 16 * j], False, False,
                    ["BOm", n])
+            if j == CS_AT and extra:
+                extra()
         mm(b, T[b][:, out:out + HL], T.Wm[:], E[:, 8 * h:8 * h + 8, 0:16], False, stop,
            ["Wm"] + [en + "%d" % (8 * h + j) for j in range(8)])
 
@@ -454,69 +504,105 @@ def rank_program(g, core, T, topo):
         zb, db = ZB[h], DB[h]
         M = "th" if t == 0 else "M"
         stage(t, DUE["z%d" % h])
-        on_v = h and V_HIT
-        bias, scale = (0.0, 1.0) if on_v else (c("kh"), 0.5)
-        if on_v:
-            ts(T.hit[:, s], T[db][:, q0], c(M), None, ALU.is_le, r=[M], w=["hit" + n], ps=[db])
+        TE, Back = ("TEv", "Backv") if h in V_HIT else ("TE", "Back")
+        if h in V_HIT:
+            ts(T.hit[:, s], T[db][:, q0], c(M), 0.5, ALU.is_le, ALU.subtract, r=[M], w=["hit" + n], ps=[db])
         else:
             act(T.hit[:, s], T[db][:, q0], ACT.Sign, bias=c(M), scale=-1.0, r=[M], w=["hit" + n], ps=[db])
-        mm(db, T[db][:, q1], T.TE[:], T.hit[:, s], True, True, ["TE", "hit" + n])
-        acc = None if last else T.acc[:, h:h + 1]
-        if on_v and V_HIT > 1:
-            ts(T.oh[:, s], T[db][:, q1], 0.0, None, ALU.max, w=["oh" + n], ps=[db])
-            act(T[zb][:, q1], T[db][:, q1], ACT.Relu, w=["acc" + n], ps=[db, zb], acc=acc)
+        for b in (db, zb):
+            mm(b, T[b][:, q1], T[TE][:], T.hit[:, s], True, True, [TE, "hit" + n])
+        if h and V_OH:
+            ts(T.oh[:, s], T[db][:, q1], 2048.0, 0.0, ALU.add, ALU.max, w=["oh" + n], ps=[db])
+            if not last:
+                keep = due[0]
+                stage(t, DUE["bound"] - 1)
+                act(T.dump[:], T.oh[:, s], r=["oh" + n], w=["dump", "acc" + n], acc=T.acc[:, h:h + 1])
+                due[0] = keep
         else:
-            for where in (("sbuf", "psum") if h else ("psum", "sbuf")):
-                if where == "psum":
-                    act(T[zb][:, q1], T[db][:, q1], ACT.Relu, bias=bias, scale=scale, r=["kh"], ps=[db, zb])
-                else:
-                    act(T.oh[:, s], T[db][:, q1], ACT.Relu, bias=bias, scale=scale, r=["kh"], w=["oh" + n, "acc" + n],
-                        ps=[db], acc=acc)
-        if Y_SCAN:
+            act(T.oh[:, s], T[db][:, q1], ACT.Relu, bias=2048.0, w=["oh" + n, "acc" + n], ps=[db],
+                acc=None if last else T.acc[:, h:h + 1])
+        if h in P_Y:
+            mm("b6", T.b6[:, 0:8], T.I[:], T.Y0[:, 0:8], True, False, ["I", "Y0"])
+            for j in range(16):
+                mm("b6", T.b6[:, 0:8], T.SJ[:, 15 - j:143 - j], T.oh[:, h * HL + j:(h + 1) * HL:16], False, j == 15,
+                   ["SJ", "oh" + n])
+            cp(T.oY[:, s8], T.b6[:, 0:8], (), ["oY" + n], ["b6"])
+        else:
             mm("b6", T.b6[:, q0], T.I[:], T.Yr[:], True, False, ["I", "Yr"])
             mm("b6", T.b6[:, q0], T.BOj[:], T.oh[:, s], False, True, ["BOj", "oh" + n])
-            scan(T.sY[:, s], T.R2[:, s], T.b6[:, q0], 0.0, ALU.add, ["R2"], ["sY" + n], ["b6"])
-            ts(T.oY[:, s8], T.sY[:, h * HL + 15:(h + 1) * HL:16], c("hold"), None, ALU.subtract, r=["sY" + n, "hold"],
+            scan(T.sY[:, s], T.R2[:, q0], T.b6[:, q0], 0.0, ALU.add, ["R2"], ["sY" + n], ["b6"])
+            ts(T.oY[:, s8], T.sY[:, h * HL + 15:(h + 1) * HL:16], c("holdn"), None, ALU.subtract, r=["sY" + n, "holdn"],
                w=["oY" + n])
-        else:
-            mm("b6", T.b6[:, s8], T.I[:], T.Y0[:], True, False, ["I", "Y0"])
-            for j in range(16):
-                mm("b6", T.b6[:, s8], T.SJ[:, 15 - j:143 - j], T.oh[:, h * HL + j:(h + 1) * HL:16], False, j == 15,
-                   ["SJ", "oh" + n])
-            cp(T.oY[:, s8], T.b6[:, s8], (), ["oY" + n], ["b6"])
         win = T.xk[:, 16 * HL * h:16 * HL * (h + 1)]
-        add("v", lambda: g.vector.tensor_tensor(T.dz[:, s], win.indirect(T.oY[:, s8]), T.zin[:, st], ALU.subtract),
-            xk + ["oY" + n, "zin%d_%d" % (t, h)], ["dz" + n], (), 50 + HL * GATH)
         zon = "zout%d_%d" % (t, h)
-        act(T.zout[:, st], T.dz[:, s], ACT.Abs, bias=-128.0, r=["dz" + n], w=[zon])
+        if h in S_DZ:
+            act(T.dz[:, s], win.indirect(T.oY[:, s8]), r=xk + ["oY" + n], w=["dz" + n], cost=65 + HL * GATH)
+            mm("b6", T.b6[:, q1], T.In[:], T.zin[:, st], True, False, ["In", "zin%d_%d" % (t, h)])
+            mm("b6", T.b6[:, q1], T.I[:], T.dz[:, s], False, True, ["I", "dz" + n])
+            act(T.zout[:, st], T.b6[:, q1], ACT.Abs, bias=-128.0, w=[zon], ps=["b6"])
+        else:
+            add("v", lambda: g.vector.tensor_tensor(T.dz[:, s], win.indirect(T.oY[:, s8]), T.zin[:, st], ALU.subtract),
+                xk + ["oY" + n, "zin%d_%d" % (t, h)], ["dz" + n], (), 50 + HL * GATH)
+            act(T.zout[:, st], T.dz[:, s], ACT.Abs, bias=-128.0, r=["dz" + n], w=[zon])
         if not last:
             send(nxt, T.zin[:, st.start + L:st.stop + L], T.zout[:, st], "zarr%d_%d" % (t + 1, h), [zon], 128 * 256)
         stage(t, DUE["named%d" % h] - (0.2 if h == 0 else 0))
-        tt(T.msk[:, s], T.hf[:, s], T[zb][:, q1], ALU.mult, ["hf" + n], ["msk" + n], [zb])
-        mm(db, T[db][:, q2], T.BOb[:], T.oh[:, s], True, False, ["BOb", "oh" + n])
-        mm(db, T[db][:, q2], T.BOh[:], T.msk[:, s], False, True, ["BOh", "msk" + n])
+        tt(T.msk[:, s], T.hf[:, s], T[zb][:, q1], ALU.min, ["hf" + n], ["msk" + n], [zb])
+        mm(zb, T[zb][:, q3], T[Back][:], T.hit[:, s], True, False, [Back, "hit" + n])
+        mm(zb, T[zb][:, q3], T.BOh[:], T.msk[:, s], False, True, ["BOh", "msk" + n])
         stage(t, DUE["named%d" % h])
-        scan(T.sN[:, s], T.R2[:, s], T[db][:, q2], 0.0, ALU.add, ["R2"], ["sN" + n], [db])
-        cp(T.nrep[:, s], T[db][:, q2], (), ["nrep" + n], [db])
-        ts(T.oN[:, s8], T.sN[:, h * HL + 15:(h + 1) * HL:16], c("hold"), None, ALU.subtract, r=["sN" + n, "hold"],
+        scan(T.sN[:, s], T.R2[:, q0], T[zb][:, q3], 0.0, ALU.add, ["R2"], ["sN" + n], [zb])
+        ts(T.nrep[:, s], T[zb][:, q3], 256.0, None, ALU.add, w=["nrep" + n], ps=[zb])
+        ts(T.oN[:, s8], T.sN[:, h * HL + 15:(h + 1) * HL:16], c("holdn"), None, ALU.subtract, r=["sN" + n, "holdn"],
            w=["oN" + n])
         act(T.tf[:, s], T.C[:, 0:CW].indirect(T.oN[:, s8]), ACT.Relu, bias=1.0 if last else ONE, scale=-2.0,
             r=["C", "oN" + n], w=["tf" + n], cost=65 + HL * GATH)
-        act(T.yf[:, s], win.indirect(T.oY[:, s8]), bias=-127.75, r=xk + ["oY" + n], w=["yf" + n], cost=65 + HL * GATH)
-        mm(db, T[db][:, q3], T.I[:], T.Cm0[:, s], True, False, ["I", "Cm0"])
-        mm(db, T[db][:, q3], T.BOb[:], T.oh[:, s], False, False, ["BOb", "oh" + n])
+        if h in S_DZ:
+            act(T.yf[:, s], T.dz[:, s], bias=-127.75, r=["dz" + n], w=["yf" + n])
+        elif h in P_YF:
+            mm("b6", T.b6[:, q1], T.I[:], T.zin[:, st], True, False, ["I", "zin%d_%d" % (t, h)])
+            mm("b6", T.b6[:, q1], T.I[:], T.dz[:, s], False, True, ["I", "dz" + n])
+            act(T.yf[:, s], T.b6[:, q1], bias=-127.75, w=["yf" + n], ps=["b6"])
+        else:
+            act(T.yf[:, s], win.indirect(T.oY[:, s8]), bias=-127.75, r=xk + ["oY" + n], w=["yf" + n], cost=65 + HL * GATH)
+        mm(db, T[db][:, q3], T.I[:], T.Cm0[:, q0], True, False, ["I", "Cm0"])
+        mm(db, T[db][:, q3], T[Back][:], T.hit[:, s], False, False, [Back, "hit" + n])
         mm(db, T[db][:, q3], T.BOh[:], T.msk[:, s], False, False, ["BOh", "msk" + n])
-        matches(h, T.nrep, "nrep" + n, "hold", lambda j: T.sN[:, 16 * j + 15:16 * j + 16], "sN" + n, "E", db, 3 * HL, False)
         cs = "Cs1" if last else "Cs"
-        mm(db, T[db][:, q3], T[cs][:], T.tf[:, s], False, True, [cs, "tf" + n], True)
+        matches(h, T.nrep, "nrep" + n, "holdn", lambda j: T.sN[:, 16 * j + 15:16 * j + 16], "sN" + n, "E", db, 3 * HL, True,
+                lambda: mm(db, T[db][:, q3], T[cs][:], T.tf[:, s], False, False, [cs, "tf" + n], True))
         scan(T.sV[:, s], T.RF[:, s], T[db][:, q3], BIG, ALU.min, ["RF"], ["sV" + n], [db])
         cp(T.oX[:, s8], T.sV[:, h * HL + 15:(h + 1) * HL:16], ["sV" + n], ["oX" + n])
 
     def roots(t):
+        for h in (1, 0) if R_HALF else ():
+            s, s8, n = half(h)
+            stage(t, DUE["roots%d" % h])
+            for j in range(16):
+                mm("b7", T.b7[:, L:L + 8], T.SK[:, 15 - j:143 - j], T.pb[:, h * HL + j:(h + 1) * HL:16], j == 0, j == 15,
+                   ["SK", "pb" + n])
+            if S_PT:
+                act(T.pT[:, s8], T.b7[:, L:L + 8], w=["pT" + n], ps=["b7"])
+            else:
+                cp(T.pT[:, s8], T.b7[:, L:L + 8], (), ["pT" + n], ["b7"])
+            stage(t, DUE["twins%d" % h])
+            o = slice(h * HL, (h + 1) * HL)
+            mm("b7", T.b7[:, o], T.I[:], T.Cm1[:, s], True, False, ["I", "Cm1"])
+            mm("b7", T.b7[:, o], T.R15[:], T.hf[:, s], False, False, ["R15", "hf" + n])
+            matches(h, T.pb, "pb" + n, None, lambda j: T.pT[:, j:j + 1], "pT" + n, "E2", "b7", h * HL, True)
+            if h == 0:
+                scan(T.sU[:], T.RF[:], T.b7[:, 0:L], BIG, ALU.min, ["RF"], ["sU"], ["b7"])
+                cp(T.oR[:], T.sU[:, 15:L:16], ["sU"], ["oR"])
+        if R_HALF:
+            return
         stage(t, DUE["roots"])
         for j in range(16):
             mm("b7", T.b7[:, L:L + 16], T.SK[:, 15 - j:143 - j], T.pb[:, j:L:16], j == 0, j == 15, ["SK"] + both("pb"))
-        cp(T.pT[:], T.b7[:, L:L + 16], (), ["pT"], ["b7"])
+        if S_PT:
+            act(T.pT[:], T.b7[:, L:L + 16], w=["pT"], ps=["b7"])
+        else:
+            cp(T.pT[:], T.b7[:, L:L + 16], (), ["pT"], ["b7"])
+        stage(t, DUE["twins"])
         mm("b7", T.b7[:, 0:L], T.I[:], T.Cm1[:], True, False, ["I", "Cm1"])
         mm("b7", T.b7[:, 0:L], T.R15[:], T.hf[:], False, False, ["R15"] + both("hf"))
         for h in (1, 0):
@@ -537,9 +623,6 @@ def rank_program(g, core, T, topo):
         zt = slice(t * L, (t + 1) * L)
         stage(t, DUE["paths0"])
         paths(t, 0)
-        if not last:
-            stage(t, DUE["leaves"])
-            send(nxt, T.fin[:, (t + 1) * L:(t + 2) * L], T.mI[:, zt], "farr%d" % (t + 1), both("mI%d" % t), 128 * 1024)
         xk1 = records(t, 1)
         answers(t, 1, xk1)
         xk0 = records(t, 0)
@@ -557,10 +640,8 @@ def rank_program(g, core, T, topo):
             dma("y", T.zs[:, 3 * L:4 * L], T.zin[:, zt], both("zin%d" % t), (), "out")
         else:
             stage(t, DUE["bound"])
-            for h in (1, 0):
-                mm("b6", T.b6[:, q1.start:q1.start + 1], T.sel14[:], T.acc[:, h:h + 1], h == 1, h == 0,
-                   ["sel14", "acc_%d" % h], True)
-            cp(T.ai[:, 0:1], T.b6[:, q1.start:q1.start + 1], (), ["ai0"], ["b6"])
+            mm("b4", T.b4[:, HL:HL + 2], T.sel14[:], T.acc[:, 0:2], True, True, ["sel14"] + both("acc"), True)
+            ts(T.ai[:, 0:1], T.b4[:, HL:HL + 1], T.b4[:, HL + 1:HL + 2], None, ALU.add, w=["ai0"], ps=["b4"])
             ts(T.ai[:, 1:2], T.ai[:, 0:1], 15, None, ALU.bitwise_and, r=["ai0"], w=["ai1"])
             ts(c("M"), T.ai[:, 1:2], c("th"), None, ALU.add, r=["ai1", "th"], w=["M"])
         stage(t, DUE["write"])
@@ -574,11 +655,12 @@ def rank_program(g, core, T, topo):
         ts(T.tt[:, 0:16], T.sV[:, 15:L:16], CW - 0.5, -float(AWAY), ALU.is_gt, ALU.mult, r=both("sV"), w=["tt0"])
         tt(T.tt[:, 16:32], T.tt[:, 0:16], T.sV[:, 15:L:16], ALU.add, both("sV") + ["tt0"], ["tt1"])
         cp(T.oC[:], T.tt[:, 16:32], ["tt1"], ["oC"])
+        stage(t, DUE["count"])
         for h in (1, 0):
             s, s8, n = half(h)
             if last:
                 add("v", lambda s=s, s8=s8: g.vector.tensor_copy(T.C2[:, 0:CW].indirect(T.oC[:, s8]), T.tf[:, s]),
-                    ["oC", "tf" + n], ["C2"], (), 50 + HL * SCAT, strict=STRICT)
+                    ["oC", "tf" + n], ["C2"], (), 50 + HL * SCAT)
             else:
                 scatter(T.C[:, 0:CW], T.oC[:, s8], T.tf[:, s], HL, ["oC", "tf" + n], ["C"])
         if t == STEPS - 2:
@@ -591,20 +673,27 @@ def rank_program(g, core, T, topo):
     stage(STEPS - 1, DUE["sums"])
     dma("y", T.cs[:, 0:TURN], T.C2[0:128:16, CW - TURN:CW], ["C2"], (), "out", 8 * W * 4)
     dma("y", T.cs[:, TURN:W], T.C2[0:128:16, BASE:CW - TURN], ["C2"], (), "out", 8 * W * 4)
-    for j2 in range(8):
-        cuts = [j2 * 512] + ([TURN] if TURN // 512 == j2 else []) + [(j2 + 1) * 512]
+    for i in range(W // L):
+        cuts = [i * L] + ([TURN] if TURN // L == i else []) + [(i + 1) * L]
         names = []
         for a, b in zip(cuts, cuts[1:]):
             p = BASE + (a - TURN) % W
             names.append("xe%d" % a)
-            if j2 % 2:
+            if i % 2:
                 ts(T.xb[:, a:b], T.X[:, p:p + b - a], 128.0, None, ALU.add, r=["X"], w=names[-1:])
             else:
                 act(T.xb[:, a:b], T.X[:, p:p + b - a], bias=128.0, r=["X"], w=names[-1:])
-        for j in (2 * j2, 2 * j2 + 1):
-            mm("b7", T.b7[:, 0:L], T.SA[:, 15 - j:143 - j], T.xb[:, j * L:(j + 1) * L], j == 0, j == 15, ["SA"] + names)
-    ts(T.xo[:], T.b7[:, 0:L], 4.0, c("asum"), ALU.mult, ALU.add, r=["asum"], w=["xo"], ps=["b7"])
-    dma("y", T.xs[:], T.xo[:], ["xo"], (), "out")
+        h, b = i // 8, ("b7", "b5")[i // 8]
+        for j in (2 * i % 16, 2 * i % 16 + 1):
+            a = h * W // 2 + j * HL
+            mm(b, T[b][:, q0], T.SA[:, 15 - j:143 - j], T.xb[:, a:a + HL], j == 0, j == 15, ["SA"] + names)
+        if i % 8 == 7:
+            s, _, n = half(h)
+            if h:
+                ts(T.xo[:, s], T[b][:, q0], 4.0, c("asum"), ALU.mult, ALU.add, r=["asum"], w=["xo" + n], ps=[b])
+            else:
+                act(T.xo[:, s], T[b][:, q0], bias=c("asum"), scale=4.0, r=["asum"], w=["xo" + n], ps=[b])
+            dma("y", T.xs[:, h * W // 2:(h + 1) * W // 2], T.xo[:, s], ["xo" + n], (), "out")
 
     if not ORDER:
         ORDER.extend(put_in_order(ops))

from concourse.mybir import AluOpType, AxisListType, ActivationFunctionType

ALU = AluOpType
ACT = ActivationFunctionType
W, L, STEPS, D = 4096, 256, 5, 3
HL = L // 2
BASE = 512
CW = BASE + W
TURN = 3177
ONE = 41 / 32
AWAY = 41 * 113
XW = 9248
BIG = float(2 ** 30)
MAGIC = 1.5 * 2 ** 23
GATHERS = [[("s", 64), ("s", 32), ("v", 32)], [("v", 32), ("s", 32), ("s", 64)]]
C_S = 3072
STRICT = False
CS_AT = 4
V_OH = 0
V_HIT = ()
S_DZ = ()
S_PT = 0
P_Y = ()
P_MOD = (1,)
TURN_X = ()
SX_AT = 13
V_SX = ()
P_YF = ()
R_HALF = 0
CYC, PE_CYC, GATH, SCAT, WAKE = 1.1, 0.66, 1.8, 4.5, 260.0
LOOK = 0.45
DMA_LAT, DMA_RATE = 1600.0, 250.0
REMOTE_LAT = 2600.0
ISSUE = 900.0
ROUNDS = 5
PERIOD = 11.5
DUE = {"paths0": 0.0, "leaves": 3.0, "gatherv1": -3.0, "gathers1": 0.0, "gatherv0": 3.0, "gathers0": 4.5, "near0": 1.0,
       "near1": 1.8, "near2": 3.9, "near3": 9.3, "z1": 3.0, "z0": 4.5, "named1": 7.0, "named0": 6.1, "roots": 4.5,
       "twins": 7.0, "means": 5.4, "write": 8.5, "paths1": 5.4, "counters": 10.0, "count": 13.5, "roots1": -1.5,
       "twins1": -1.0, "roots0": 3.0, "twins0": 6.0, "bound": 13.0, "home": 9.0, "sums": 19.5}

SCRATCH = {
    "X": ("sbuf", [128, XW], "float32"), "C": ("sbuf", [128, CW], "float32"), "C2": ("sbuf", [128, CW], "float32"),
    "Cb": ("sbuf", [128, W], "bfloat16"),
    "xk": ("sbuf", [128, W], "bfloat16"), "mx": ("sbuf", [128, W], "bfloat16"), "xb": ("sbuf", [128, W], "bfloat16"),
    "E": ("sbuf", [128, 16, HL], "bfloat16"), "E2": ("sbuf", [128, 16, HL], "bfloat16"),
    "zin": ("sbuf", [128, 5 * L], "bfloat16"), "zout": ("sbuf", [128, 5 * L], "bfloat16"),
    "zhome": ("sbuf", [128, 2 * L], "bfloat16"),
    "fin": ("sbuf", [128, 5 * L], "float32"), "mI": ("sbuf", [128, 5 * L], "float32"),
    "LI": ("sbuf", [128, 264], "int32"), "thf": ("sbuf", [128, 2], "float32"),
    "wi": ("sbuf", [128, 2], "int32"), "wf": ("sbuf", [128, 2], "float32"),
    "pI": ("sbuf", [128, 4], "int32"), "col": ("sbuf", [128, 40], "float32"),
    "im": ("sbuf", [128, 144], "bfloat16"), "ig": ("sbuf", [128, 128], "bfloat16"),
    "ic": ("sbuf", [128, L], "bfloat16"), "ib": ("sbuf", [128, 16], "float32"),
    "ones": ("sbuf", [128, L], "bfloat16"), "sY": ("sbuf", [128, L], "float32"),
    "dm": ("sbuf", [128, 32], "float32"),
    "Cm0": ("sbuf", [128, L], "bfloat16"), "Cm1": ("sbuf", [128, L], "bfloat16"), "RF": ("sbuf", [128, L], "bfloat16"),
    "R2": ("sbuf", [128, L], "bfloat16"), "Cm": ("sbuf", [128, L], "bfloat16"),
    "qq": ("sbuf", [128, L], "bfloat16"), "rb": ("sbuf", [128, L], "float16"), "pb": ("sbuf", [128, L], "bfloat16"),
    "vf": ("sbuf", [128, L], "float32"), "uI": ("sbuf", [128, L], "int32"), "h32": ("sbuf", [128, L], "int32"),
    "h16": ("sbuf", [128, L], "uint16"), "hf": ("sbuf", [128, L], "float16"), "msk": ("sbuf", [128, L], "float16"),
    "hit": ("sbuf", [128, L], "bfloat16"), "oh": ("sbuf", [128, L], "bfloat16"),
    "dz": ("sbuf", [128, L], "bfloat16"), "sx": ("sbuf", [128, L], "bfloat16"), "nrep": ("sbuf", [128, L], "uint16"),
    "sN": ("sbuf", [128, L], "float32"), "sV": ("sbuf", [128, L], "float32"), "sU": ("sbuf", [128, L], "float32"),
    "tf": ("sbuf", [128, L], "float32"), "yf": ("sbuf", [128, L], "float32"), "af": ("sbuf", [128, L], "float32"),
    "pT": ("sbuf", [128, 16], "float32"), "tt": ("sbuf", [128, 32], "float32"),
    "oY": ("sbuf", [128, 16], "uint16"), "oN": ("sbuf", [128, 16], "uint16"), "oX": ("sbuf", [128, 16], "uint16"),
    "oC": ("sbuf", [128, 16], "uint16"), "oR": ("sbuf", [128, 16], "uint16"),
    "acc": ("sbuf", [128, 4], "float32"), "ai": ("sbuf", [128, 4], "int32"),
    "xo": ("sbuf", [128, L], "float32"),
}
for _n in ("S2", "Sn", "SA", "SJ", "SK"):
    SCRATCH[_n] = ("sbuf", [128, 144], "bfloat16")
for _n in ("I", "H", "BO", "BOn", "BOm", "Back", "Wm", "A2", "TE", "TE0", "TE1", "TE2", "TE3", "Kc", "dg1", "Bm", "Bin",
           "c128", "tiny", "BOj", "Yr", "dump", "In", "TEv", "Backv", "Y0", "c16"):
    SCRATCH[_n] = ("sbuf", [128, 128], "bfloat16")
for _n in ("N64", "BOh", "R15", "c809", "c1025"):
    SCRATCH[_n] = ("sbuf", [128, 128], "float16")
for _n in ("L8", "DG", "Cs", "Cs1", "sel14", "BO32", "I32"):
    SCRATCH[_n] = ("sbuf", [128, 128], "float32")
for _b in range(8):
    SCRATCH["b%d" % _b] = ("psum", [128, 512], "float32")

SEMAPHORES = (["qv", "qs", "qp", "qg", "sent", "out", "barr", "lz", "lw", "ll", "lt", "lc", "lx", "lX", "lb", "l2"]
              + ["zarr%d_%d" % (t, h) for t in range(1, 5) for h in range(2)] + ["farr%d" % i for i in range(4)]
              + ["harr1", "harr2"])

ORDER = []


def elems(ap):
    n = 1
    for s in ap.shape[1:]:
        n *= s
    return n


def list_schedule(ops, edges, release, rank):
    n = len(ops)
    left = [0] * n
    for e in edges:
        for u, _ in e:
            left[u] += 1
    ready_at, start = list(release), [0.0] * n
    ready, free, order = {}, {}, []
    for i in range(n):
        if left[i] == 0:
            ready.setdefault(ops[i]["q"], []).append(i)
    while len(order) < n:
        best = None
        for q, r in ready.items():
            if r:
                t = max(free.get(q, 0.0), min(ready_at[i] for i in r))
                i = max((i for i in r if ready_at[i] <= t), key=lambda i: rank[i])
                t2 = t + LOOK * ops[i]["cost"]
                i = max((i for i in r if ready_at[i] <= t2), key=lambda i: rank[i])
                t = max(t, ready_at[i])
                if best is None or t < best[0]:
                    best = (t, i)
        t, i = best
        ready[ops[i]["q"]].remove(i)
        free[ops[i]["q"]] = t + ops[i]["cost"]
        start[i] = t
        order.append(i)
        for u, gap in edges[i]:
            ready_at[u] = max(ready_at[u], t + gap)
            left[u] -= 1
            if left[u] == 0:
                ready.setdefault(ops[u]["q"], []).append(u)
    return order, start


def put_in_order(ops):
    n = len(ops)
    ahead, back = [[] for _ in ops], [[] for _ in ops]
    for u, o in enumerate(ops):
        for i in o["deps"] | o["after"]:
            gap = ops[i]["lat"] + (WAKE if o["q"] else 0.0) if i in o["deps"] else ops[i]["cost"]
            ahead[i].append((u, gap))
            back[u].append((i, gap + o["cost"] - ops[i]["cost"]))
    due = [o["due"] for o in ops]
    for i in range(n - 1, -1, -1):
        if due[i] is None:
            due[i] = min([1e9] + [due[u] - gap for u, gap in ahead[i]])
    rank, best = [(-due[i], -i) for i in range(n)], None
    for _ in range(ROUNDS):
        order, start = list_schedule(ops, ahead, [0.0] * n, rank)
        end = max(start[i] + ops[i]["lat"] for i in range(n))
        if best is None or end < best[0]:
            best = (end, order)
        rank = [(start[i] + ops[i]["cost"], i) for i in range(n)]
        _, late = list_schedule(ops, back, [o["lat"] - o["cost"] for o in ops], rank)
        rank = [(late[i] + ops[i]["cost"], -i) for i in range(n)]
    return best[1]


def rank_program(g, core, T, topo):
    rank = T.rank_of(core)
    if rank is None:
        return
    N = len(T.cores)
    Q = {"v": g.vector, "s": g.scalar, "p": g.tensor, "g": g, "y": g.sync}
    ops = []
    last_w, readers, bank, sends = {}, {}, {}, {}
    due = [None]

    def stage(t, at):
        due[0] = 1000.0 * (t * PERIOD + at)

    def add(q, fn, r=(), w=(), ps=(), cost=60.0, lat=None, sem=None, inc=16, strict=False):
        i = len(ops)
        deps, after = set(), set()
        for x in r:
            deps.update(last_w.get(x, []))
        for x in w:
            for j in readers.get(x, []) + last_w.get(x, []):
                (after if x == "in turn" else deps).add(j)
        for b in ps:
            for qq, j in bank.get(b, {}).items():
                (after if qq == q else deps).add(j)
            bank.setdefault(b, {})[q] = i
        for x in r:
            readers.setdefault(x, []).append(i)
        for x in w:
            last_w[x] = [i]
            readers[x] = []
        ops.append({"q": q, "fn": fn, "deps": deps, "after": after - deps, "sem": sem, "inc": inc, "cost": cost,
                    "lat": cost if lat is None else lat, "due": due[0]})
        return i

    def arrival(name, sem, n):
        i = add(None, None, w=[name], sem=sem, inc=n, cost=0.0)
        ops[i]["deps"].add(sends[sem])

    def vcost(n, fast=False):
        return max(64, n / 2 if fast else n) * CYC

    def ts(out, in0, s1, s2, o0, o1=None, r=(), w=(), ps=(), fast=False):
        if o1 is None:
            add("v", lambda: g.vector.tensor_scalar(out, in0, s1, None, o0), r, w, ps, vcost(elems(out), fast))
        else:
            add("v", lambda: g.vector.tensor_scalar(out, in0, s1, s2, o0, o1), r, w, ps, vcost(elems(out), fast))

    def tt(out, a, b, op, r=(), w=(), ps=()):
        add("v", lambda: g.vector.tensor_tensor(out, a, b, op), r, w, ps, vcost(elems(out)))

    def cp(out, a, r=(), w=(), ps=()):
        add("v", lambda: g.vector.tensor_copy(out, a), r, w, ps, vcost(elems(out)))

    def ms(out, c, w):
        add("v", lambda: g.vector.memset(out, c), (), w, (), vcost(elems(out), True))

    def scan(out, d0, d1, init, o0, r, w, ps):
        add("v", lambda: g.vector.tensor_tensor_scan(out, d0, d1, init, o0, ALU.max), r, w, ps, vcost(elems(out)))

    def act(out, a, f=ACT.Identity, bias=0.0, scale=1.0, r=(), w=(), ps=(), acc=None, cost=None):
        cost = vcost(elems(out)) if cost is None else cost
        if acc is None:
            add("s", lambda: g.scalar.activation(out, a, f, bias=bias, scale=scale), r, w, ps, cost)
        else:
            add("s", lambda: g.scalar.activation(out, a, f, bias=bias, scale=scale, accum_out=acc), r, w, ps, cost + 20)

    def scatter(win, off, src, n, r, w):
        add("s", lambda: g.scalar.activation(win.indirect(off), src, ACT.Silu), r, w, (), 65 + n * SCAT, strict=STRICT)

    def mm(b, out, lhsT, rhs, start, stop, r=(), f32=False):
        add("p", lambda: g.tensor.matmul(out, lhsT, rhs, start, stop), r, (), [b],
            max(64, elems(out)) * PE_CYC * (4 if f32 else 1))

    def dma(q, out, in_, r, w, sem, size=0, **k):
        return add(q, lambda: Q[q].dma_start(out, in_, **k), r, w, (), 600.0 if q == "g" else 60.0,
                   DMA_LAT + size / DMA_RATE, sem)

    def turned(q, win, base, src, r, name, sem, size, before=()):
        rows = slice(0, 128, 128 // src.shape[0])
        i = dma(q, win[rows, base + W - TURN:base + W], src[:, 0:TURN], r, list(before) + [name + "a"], sem, size)
        j = dma(q, win[rows, base:base + W - TURN], src[:, TURN:W], r, [name], sem, size)
        ops[j]["deps"] |= ops[i]["deps"]
        ops[j]["after"].add(i)
        last_w[name] = [i, j]

    def iota(out, pat, base, cm, w, small=True):
        if small:
            add("g", lambda: g.iota(out, pat, base, cm, allow_small_or_imprecise_dtypes=True), (), [w], (),
                130 + 2 * elems(out) * CYC)
        else:
            add("g", lambda: g.iota(out, pat, base, cm), (), [w], (), 130.0)

    nsent = [0]

    def send(dst_rank, out, in_, sem, r, size):
        dst = T.cores[dst_rank]
        rid, pid = topo.addr(dst, core)
        m = topo.mask(core, dst)
        nsent[0] += len(topo.engines(core, dst))
        sends[sem] = add("g", lambda: g.remote_dma(out, in_, T.sem[sem], T.sem.sent, pid, rid, m), r, (), (), ISSUE,
                         REMOTE_LAT + size / 60, "-")

    q0, q1, q2, q3 = [slice(i * HL, (i + 1) * HL) for i in range(4)]
    nxt, prv = (rank + D) % N, (rank - D) % N
    n_in = len(topo.engines(T.cores[prv], core))
    cols = {}

    def c(name):
        if name not in cols:
            cols[name] = len(cols)
        return T.col[:, cols[name]:cols[name] + 1]

    def cc(name, src, s1, s2, o0, o1=None):
        r = [src] + [x for x in (s1, s2) if isinstance(x, str)]
        s1, s2 = [c(x) if isinstance(x, str) else x for x in (s1, s2)]
        ts(c(name), c(src), s1, s2, o0, o1, r=r, w=[name])

    def mat(name, src, s1, s2, o0, o1=None):
        r = [src] + [x for x in (s1, s2) if isinstance(x, str)]
        s1, s2 = [c(x) if isinstance(x, str) else x for x in (s1, s2)]
        ts(T[name][:], T[src][:, 0:T[name].shape[1]], s1, s2, o0, o1, r=r, w=[name], fast=True)

    dma("y", T.wi[:], T.wt[:], (), ["wi"], "lw")
    dma("y", T.zin[:, 0:L], T.z0[:], (), ["zin0_0", "zin0_1"], "lz")
    ms(T.LI[:], 0, ["LI", "LIt"])
    dma("s", T.LI[0:128:16, 0:L], T.leaf[:], (), ["LI"], "ll")
    turned("y", T.xb, 0, T.x0, (), "xb", "lx", 128 * W * 2)
    iota(T.pI[:, 0:1], [[0, 1]], 0, 1, "pI", small=False)
    iota(T.ig[:], [[1, 8], [0, 16]], 0, 0, "ig")
    iota(T.im[:], [[1, 144]], 0, 0, "im")
    iota(T.ic[:], [[0, 16], [1, 16]], 0, 0, "ic")
    iota(T.ib[:], [[16, 16]], 0, 0, "ib")
    dma("g", T.LI[0:128:16, L:L + 1], T.th[:], (), ["LIt"], "lt", 2500 * DMA_RATE, allow_slow_non_contiguous=True)
    ms(T.ones[:], 1.0, ["ones"])
    ms(T.c128[0:32, :], 128.0, ["c128"])
    ms(T.tiny[0:32, :], 2.0 ** -17, ["tiny"])
    ts(T.c809[0:32, :], T.ones[0:32, 0:128], 809.0, None, ALU.mult, r=["ones"], w=["c809"], fast=True)
    ts(T.c1025[0:32, :], T.ones[0:32, 0:128], 1025.0 / 8, None, ALU.mult, r=["ones"], w=["c1025"], fast=True)
    act(T.C[:, 0:L], T.ones[:], ACT.Silu, scale=0.0, r=["ones"], w=["C0"], cost=1500.0)
    for a in range(L, C_S, L):
        act(T.C[:, a:a + L], T.ones[:], scale=0.0, r=["ones"], w=["C%d" % a])
    for a in range(C_S, CW, 512):
        iota(T.C[:, a:a + 512], [[0, 512]], 0, 0, "C%d" % a)
    turned("g", T.C, BASE, T.c0, (), "C", "lc", 8 * W * 4,
           ["C%d" % a for a in list(range(0, C_S, L)) + list(range(C_S, CW, 512))])
    turned("g", T.X, BASE, T.x0, ["wi"], "X", "lX", 128 * W * 6)

    ts(T.pI[:, 1:2], T.pI[:, 0:1], 15, None, ALU.bitwise_and, r=["pI"], w=["kI"])
    ts(T.pI[:, 2:3], T.pI[:, 0:1], 4, None, ALU.arith_shift_right, r=["pI"], w=["gI"])
    cp(c("p"), T.pI[:, 0:1], ["pI"], ["p"])
    cp(c("k"), T.pI[:, 1:2], ["kI"], ["k"])
    cp(c("g"), T.pI[:, 2:3], ["gI"], ["g"])
    ts(T.dm[:, 0:16], T.im[:, 0:16], c("k"), 0.5, ALU.is_ge, ALU.max, r=["im", "k"], w=["dm0"])
    add("v", lambda: g.vector.tensor_reduce(c("pw"), T.dm[:, 0:16], AxisListType.X, ALU.mult), ["dm0"], ["pw"])
    mat("BO", "ig", "g", None, ALU.is_equal)
    mat("I", "im", "p", None, ALU.is_equal)
    ts(T.wf[:], T.wi[:], 0.25, None, ALU.mult, r=["wi"], w=["wf"])
    ts(T.A2[:], T.ig[:], c("g"), T.wf[:, 0:1], ALU.is_equal, ALU.mult, r=["ig", "g", "wf"], w=["A2"], fast=True)
    mat("dg1", "im", "p", "pw", ALU.is_equal, ALU.mult)
    mm("b7", T.b7[:, 0:128], T.BO[:], T.dg1[:], True, True, ["BO", "dg1"])
    cc("k0", "k", 0.0, 8.0, ALU.is_equal, ALU.mult)
    cc("e15", "k", 15.0, None, ALU.is_equal)
    cc("r15", "e15", -19615.5 / 2453, "k0", ALU.mult, ALU.add)
    cc("h15", "e15", -0.5 / 2453 / 8, None, ALU.mult)
    cc("f15", "e15", 2452.0, None, ALU.add)
    ts(T.L8[:], T.b7[:, 0:128], c("r15"), c("h15"), ALU.mult, ALU.add, r=["r15", "h15"], w=["L8"], ps=["b7"])
    ts(T.Bm[:], T.b7[:, 0:128], T.wf[:, 1:2], 4.0, ALU.mult, ALU.mult, r=["wf"], w=["Bm"], ps=["b7"])
    ts(T.fin[:, 0:L], T.LI[:, 0:L], 0.125, c("f15"), ALU.mult, ALU.add, r=["LI", "f15"], w=["fin0"])
    cc("nT", "pw", -32768.0, -4096.0, ALU.mult, ALU.max)
    cc("bq", "nT", 128.5, -0.5, ALU.mult, ALU.add)
    cc("mg0", "pw", 130 * 32768.0, 129 * 4096.0, ALU.mult, ALU.min)
    cc("mg", "mg0", MAGIC, None, ALU.add)
    mat("N64", "I", -64.0, None, ALU.mult)
    send(nxt, T.Bin[:], T.Bm[:], "barr", ["Bm"], 128 * 256)
    arrival("Bin", "barr", n_in)

    cc("g15", "g", 16.0, 15.0, ALU.mult, ALU.add)
    mat("S2", "im", "g15", 2.0, ALU.is_equal, ALU.mult)
    mat("Sn", "im", "g15", -1.0, ALU.is_equal, ALU.mult)
    cc("kp1", "k", 1.0, 2.0 ** -12, ALU.add, ALU.mult)
    if len(P_Y) < 2:
        mat("BOj", "BO", "kp1", None, ALU.mult)
        mat("Yr", "im", 16.0, -256.0, ALU.mult, ALU.add)
    if P_Y:
        mat("SJ", "im", "g15", "kp1", ALU.is_equal, ALU.mult)
        ts(T.Y0[:, 0:8], T.ib[:, 0:8], c("k"), 16.0, ALU.add, ALU.mult, r=["ib", "k"], w=["Y0"])
    mat("SK", "im", "g15", 0.0625, ALU.is_equal, ALU.mult)
    ts(T.SA[:], T.im[:], c("g15"), T.wf[:, 0:1], ALU.is_equal, ALU.mult, r=["im", "g15", "wf"], w=["SA"], fast=True)
    mat("Cm", "ic", "k", -BIG, ALU.not_equal, ALU.mult)
    cc("k14", "k", 14.0, 2.0 ** -12, ALU.is_equal, ALU.mult)
    cc("holdn", "k", -8192.0, 15 * 8192.0 - 256, ALU.mult, ALU.add)
    cc("bk0", "k", -2048.0, 14 * 2048.0, ALU.mult, ALU.add)
    cc("bk1", "k0", -32.0, "bk0", ALU.mult, ALU.add)
    cc("bk", "e15", 137 * 2048.0, "bk1", ALU.mult, ALU.add)
    act(T.Back[:], T.BO[:], scale=c("bk"), r=["BO", "bk"], w=["Back"])
    ts(T.Kc[:], T.ic[:, 0:128], 1.0, -2048.0, ALU.add, ALU.mult, r=["ic"], w=["Kc"], fast=True)
    mat("TE1", "BO", "e15", None, ALU.mult)
    tt(T.TE3[:], T.TE1[:], T.Kc[:], ALU.mult, ["TE1", "Kc"], ["TE3"])
    act(T.TE2[:], T.BO[:], scale=-2048.0, r=["BO"], w=["TE2"])
    cc("top", "k", -1.0, 256.0, ALU.mult, ALU.add)
    mat("BOh", "BO", 1.0, None, ALU.mult)
    mat("R15", "BO", "e15", None, ALU.mult)
    ms(T.RF[:], BIG, ["RF0"])
    ts(T.RF[:, 0:L:16], T.ib[:], -1.0, c("top"), ALU.mult, ALU.add, r=["ib", "top", "RF0"], w=["RF"])
    act(T.BOn[:], T.BO[:], scale=-1.0, r=["BO"], w=["BOn"])
    act(T.BOm[:], T.BO[:], scale=-32768.0, r=["BO"], w=["BOm"])
    act(T.BO32[:], T.BO[:], r=["BO"], w=["BO32"])
    act(T.H[:], T.I[:], scale=0.5, r=["I"], w=["H"])
    if len(TURN_X) == 1:
        ms(T.c16[0:32, :], -16.0, ["c16"])
    if S_DZ or TURN_X:
        act(T.In[:], T.I[:], scale=-1.0, r=["I"], w=["In"])
    act(T.sel14[:], T.ones[:, 0:128], scale=c("k14"), r=["ones", "k14"], w=["sel14"])
    cc("k0a", "k0", AWAY / ONE / 8, None, ALU.mult)
    act(T.Cs[:], T.BO[:], scale=c("k0a"), r=["BO", "k0a"], w=["Cs"])
    act(T.Cs1[:], T.Cs[:], scale=ONE, r=["Cs"], w=["Cs1"])
    act(T.R2[:, q0], T.Cm[:, q0], bias=8192.0 - 2.0 ** 20, scale=-2.0 ** 20 / BIG, r=["Cm"], w=["R2"])
    act(T.Cm0[:, q0], T.Cm[:, q0], bias=256.0, r=["Cm"], w=["Cm0"])
    act(T.Cm1[:], T.Cm[:], bias=2048.0 + BASE, r=["Cm"], w=["Cm1"])
    asel = 170 + 256 * CYC
    add("g", lambda: g.affine_select(T.TE0[:], T.TE2[:], [[1, 128]], ALU.is_ge, 0.0, 0, -1), ["TE2"], ["TE0"], (), asel)
    add("g", lambda: g.affine_select(T.TE2[:], T.TE0[:], [[1, 128]], ALU.not_equal, 2048.0, 1, -1), ["TE0"], ["TE2"], (), asel)
    ms(T.TE2[:, 15:128:16], 0.0, ["TE2"])
    tt(T.TE[:], T.TE2[:], T.TE3[:], ALU.add, ["TE2", "TE3"], ["TE"])
    add("g", lambda: g.affine_select(T.Wm[:], T.BOm[:], [[1, 128]], ALU.is_gt, 0.0, 0, -1), ["BOm"], ["Wm"], (), asel)
    if V_HIT:
        act(T.TEv[:], T.TE[:], scale=2.0, r=["TE"], w=["TEv"])
        act(T.Backv[:], T.Back[:], scale=2.0, r=["Back"], w=["Backv"])
    cp(T.thf[:], T.LI[:, L:L + 2], ["LIt"], ["thf"])
    mm("b7", T.b7[:, 2:4], T.A2[:], T.ones[:, 0:2], True, True, ["A2", "ones"])
    mm("b7", T.b7[:, 0:2], T.BO32[:], T.thf[:], True, True, ["BO32", "thf"], True)
    ts(c("th"), T.b7[:, 0:1], 4096.5 if len(TURN_X) == 2 else 2048.5, None, ALU.add, w=["th"], ps=["b7"])
    ts(c("asum"), T.b7[:, 2:3], -512.0, None, ALU.mult, w=["asum"], ps=["b7"])

    ZB, DB = ["b1", "b0"], ["b3", "b2"]

    def half(h):
        return slice(h * HL, (h + 1) * HL), slice(h * 8, (h + 1) * 8), "_%d" % h

    def both(x):
        return [x + "_0", x + "_1"]

    def paths(t, h):
        s, _, n = half(h)
        st = slice(t * L + h * HL, t * L + (h + 1) * HL)
        z, zn, zb = T.zin[:, st], "zin%d_%d" % (t, h), ZB[h]
        if t > 0:
            arrival(zn, "zarr%d_%d" % (t, h), n_in)
        mm("b5", T.b5[:, q0], T.L8[:], T.fin[:, st], True, t == 0, ["L8", "fin%d" % t], True)
        mm("b4", T.b4[:, q0], T.c809[0:1, :], T.c1025[0:1, :], True, False, ["c809", "c1025"])
        if t > 0:
            mm("b5", T.b5[:, q0], T.Bin[:], z, False, True, ["Bin", zn])
        mm(zb, T[zb][:, q2], T.A2[:], z, True, True, ["A2", zn])
        mm("b4", T.b4[:, q0], T.A2[:], z, False, False, ["A2", zn])
        act(T.qq[:, s], T.b5[:, q0], bias=c("bq"), scale=-1.0, r=["bq"], w=["qq" + n], ps=["b5"])
        ts(T.rb[:, s], T[zb][:, q2], 2.0 ** -6, 1619.0 - 255.0 / 512, ALU.mult, ALU.add, w=["rb" + n], ps=[zb])
        db = DB[h]
        if h in P_MOD:
            mm(db, T[db][:, q0], T.L8[:], T.fin[:, st], True, False, ["L8", "fin%d" % t], True)
            if t > 0:
                mm(db, T[db][:, q0], T.Bin[:], z, False, False, ["Bin", zn])
            mm(db, T[db][:, q0], T.I[:], T.qq[:, s], False, True, ["I", "qq" + n])
        else:
            tt(T.vf[:, s], T.qq[:, s], T.b5[:, q0], ALU.add, ["qq" + n], ["vf" + n], ["b5"])
        mm("b4", T.b4[:, q0], T.N64[:], T.rb[:, s], False, False, ["N64", "rb" + n])
        mm("b4", T.b4[:, q0], T.tiny[0:1, :], T.ones[0:1, 0:HL], False, True, ["tiny", "ones"])
        mn = "mI%d_%d" % (t, h)
        if h in P_MOD:
            ts(T.mI[:, st], T[db][:, q0], c("mg"), MAGIC - 2452.0, ALU.add, ALU.subtract, r=["mg"], w=[mn], ps=[db])
        else:
            ts(T.mI[:, st], T.vf[:, s], c("mg"), MAGIC - 2452.0, ALU.add, ALU.subtract, r=["mg", "vf" + n], w=[mn])
        tt(T.uI[:, s], T.mI[:, st], T.b4[:, q0], ALU.mult, [mn], ["uI" + n], ["b4"])
        ts(T.h32[:, s], T.uI[:, s], 4095, None, ALU.bitwise_and, r=["uI" + n], w=["h32" + n])
        cp(T.h16[:, s], T.h32[:, s], ["h32" + n], ["h16" + n])
        mm(zb, T[zb][:, q0], T.c128[0:1, :], T.ones[0:1, 0:HL], True, False, ["c128", "ones"])
        mm(zb, T[zb][:, q0], T.I[:], z, False, True, ["I", zn])
        act(T.pb[:, s], T.b4[:, q0], bias=-148.5, scale=4.0, w=["pb" + n], ps=["b4"])
        ts(T.hf[:, s], T.h16[:, s], -2048.0, None, ALU.add, r=["h16" + n], w=["hf" + n], fast=True)
        if t < STEPS - 1 and h == 0:
            stage(t, DUE["leaves"])
            send(nxt, T.fin[:, (t + 1) * L:(t + 2) * L], T.mI[:, t * L:(t + 1) * L], "farr%d" % t, both("mI%d" % t), 128 * 1024)
            arrival("fin%d" % (t + 1), "farr%d" % t, n_in)

    def records(t, h):
        _, _, n = half(h)
        win, wn = (T.xb[:, 0:W], ["xb"]) if t == 0 else (T.X[:, BASE:CW], ["X"])
        zb, db = ZB[h], DB[h]
        parts, a = [], h * HL
        for q, m in GATHERS[h]:
            b = a + m
            parts.append((a, b))
            stage(t, DUE["gather%s%d" % (q, h)])
            if q == "v":
                add("v", lambda a=a, b=b: g.vector.tensor_scalar(T.xk[:, 16 * a:16 * b], win.indirect(T.h16[:, a:b]),
                                                                 128.0, None, ALU.add),
                    wn + ["h16" + n], ["xk%d" % a], (), 50 + 16 * m * GATH)
            else:
                act(T.xk[:, 16 * a:16 * b], win.indirect(T.h16[:, a:b]), bias=128.0, r=wn + ["h16" + n],
                    w=["xk%d" % a, "in turn"], cost=65 + 16 * m * GATH)
            a = b
        for a in (h * HL, h * HL + 64):
            stage(t, DUE["near%d" % ((a - HL) % L // 64)])
            if a == h * HL:
                mm(db, T[db][:, q0], T.BOn[:], T.zin[:, t * L + h * HL:t * L + (h + 1) * HL], True, False,
                   ["BOn", "zin%d_%d" % (t, h)])
            b, o = a + 64, slice(a - h * HL, a - h * HL + 64)
            need = ["xk%d" % aa for aa, bb in parts if aa < b and bb > a]
            if h not in TURN_X:
                for k in range(15):
                    mm(db, T[db][:, o], T.Sn[:, 15 - k:143 - k], T.xk[:, 16 * a + k:16 * b:16], False, False, ["Sn"] + need)
            elif a > h * HL:
                for k in range(16):
                    mm("b5", T.b5[:, HL + k:L:16], T.xk[:, 16 * h * HL + k:16 * b:16], T.BO[:, 0:128:16], True, True,
                       ["BO"] + ["xk%d" % aa for aa, bb in parts])
                if h in V_SX:
                    ts(T.sx[:, h * HL:(h + 1) * HL], T.b5[:, q1], -2048.0, None, ALU.add, w=["sx" + n], ps=["b5"])
                else:
                    act(T.sx[:, h * HL:(h + 1) * HL], T.b5[:, q1], bias=-2048.0, w=["sx" + n], ps=["b5"])
            for k in range(15):
                x, m = T.xk[:, 16 * a + k:16 * b:16], T.mx[:, k * L + a:k * L + b]
                tt(m, x, T[zb][:, o], ALU.max, need, ["mx%d_%d" % (a, k)], [zb])
                if h in TURN_X and a > h * HL and k == SX_AT:
                    mm(db, T[db][:, q0], T.sx[:, h * HL:(h + 1) * HL], T.In[:], False, False, ["sx" + n, "In"])
                    mm(db, T[db][:, q0], T.c128[0:1, :], T.c16[0:1, :], False, False, ["c128", "c16"]) if len(TURN_X) < 2 else None
                mm(db, T[db][:, o], T.S2[:, 15 - k:143 - k], m, False, a > h * HL and k == 14, ["S2", "mx%d_%d" % (a, k)])
        return ["xk%d" % a for a, b in parts]

    def matches(h, keys, kn, shift, scal, sn, en, b, out, stop, extra=None):
        E = T[en]
        for j in range(8):
            e, src, n = E[:, 8 * h + j, 0:HL - 16 * j], keys[:, h * HL + 16 * j:(h + 1) * HL], en + "%d" % (8 * h + j)
            if shift is None:
                ts(e, src, scal(8 * h + j), None, ALU.is_equal, r=[kn, sn], w=[n], fast=True)
            else:
                ts(e, src, c(shift), scal(8 * h + j), ALU.add, ALU.is_equal, r=[kn, sn, shift], w=[n], fast=True)
            if j < 7:
                mm(b, T[b][:, out + 16 * j + 16:out + HL], T.BOm[:], E[:, 8 * h + j, 16:HL - 16 * j], False, False,
                   ["BOm", n])
            if j == CS_AT and extra:
                extra()
        mm(b, T[b][:, out:out + HL], T.Wm[:], E[:, 8 * h:8 * h + 8, 0:16], False, stop,
           ["Wm"] + [en + "%d" % (8 * h + j) for j in range(8)])

    def answers(t, h, xk):
        s, s8, n = half(h)
        last = t == STEPS - 1
        st = slice(t * L + h * HL, t * L + (h + 1) * HL)
        zb, db = ZB[h], DB[h]
        M = "th" if t == 0 else "M"
        stage(t, DUE["z%d" % h])
        TE, Back = ("TEv", "Backv") if h in V_HIT else ("TE", "Back")
        if h in V_HIT:
            ts(T.hit[:, s], T[db][:, q0], c(M), 0.5, ALU.is_le, ALU.subtract, r=[M], w=["hit" + n], ps=[db])
        else:
            act(T.hit[:, s], T[db][:, q0], ACT.Sign, bias=c(M), scale=-1.0, r=[M], w=["hit" + n], ps=[db])
        for b in (db, zb):
            mm(b, T[b][:, q1], T[TE][:], T.hit[:, s], True, True, [TE, "hit" + n])
        if h and V_OH:
            ts(T.oh[:, s], T[db][:, q1], 2048.0, 0.0, ALU.add, ALU.max, w=["oh" + n], ps=[db])
            if not last:
                keep = due[0]
                stage(t, DUE["bound"] - 1)
                act(T.dump[:], T.oh[:, s], r=["oh" + n], w=["dump", "acc" + n], acc=T.acc[:, h:h + 1])
                due[0] = keep
        else:
            act(T.oh[:, s], T[db][:, q1], ACT.Relu, bias=2048.0, w=["oh" + n, "acc" + n], ps=[db],
                acc=None if last else T.acc[:, h:h + 1])
        if h in P_Y:
            mm("b6", T.b6[:, 0:8], T.I[:], T.Y0[:, 0:8], True, False, ["I", "Y0"])
            for j in range(16):
                mm("b6", T.b6[:, 0:8], T.SJ[:, 15 - j:143 - j], T.oh[:, h * HL + j:(h + 1) * HL:16], False, j == 15,
                   ["SJ", "oh" + n])
            cp(T.oY[:, s8], T.b6[:, 0:8], (), ["oY" + n], ["b6"])
        else:
            mm("b6", T.b6[:, q0], T.I[:], T.Yr[:], True, False, ["I", "Yr"])
            mm("b6", T.b6[:, q0], T.BOj[:], T.oh[:, s], False, True, ["BOj", "oh" + n])
            scan(T.sY[:, s], T.R2[:, q0], T.b6[:, q0], 0.0, ALU.add, ["R2"], ["sY" + n], ["b6"])
            ts(T.oY[:, s8], T.sY[:, h * HL + 15:(h + 1) * HL:16], c("holdn"), None, ALU.subtract, r=["sY" + n, "holdn"],
               w=["oY" + n])
        win = T.xk[:, 16 * HL * h:16 * HL * (h + 1)]
        zon = "zout%d_%d" % (t, h)
        if h in S_DZ:
            act(T.dz[:, s], win.indirect(T.oY[:, s8]), r=xk + ["oY" + n], w=["dz" + n], cost=65 + HL * GATH)
            mm("b6", T.b6[:, q1], T.In[:], T.zin[:, st], True, False, ["In", "zin%d_%d" % (t, h)])
            mm("b6", T.b6[:, q1], T.I[:], T.dz[:, s], False, True, ["I", "dz" + n])
            act(T.zout[:, st], T.b6[:, q1], ACT.Abs, bias=-128.0, w=[zon], ps=["b6"])
        else:
            add("v", lambda: g.vector.tensor_tensor(T.dz[:, s], win.indirect(T.oY[:, s8]), T.zin[:, st], ALU.subtract),
                xk + ["oY" + n, "zin%d_%d" % (t, h)], ["dz" + n], (), 50 + HL * GATH)
            act(T.zout[:, st], T.dz[:, s], ACT.Abs, bias=-128.0, r=["dz" + n], w=[zon])
        if not last:
            send(nxt, T.zin[:, st.start + L:st.stop + L], T.zout[:, st], "zarr%d_%d" % (t + 1, h), [zon], 128 * 256)
        stage(t, DUE["named%d" % h] - (0.2 if h == 0 else 0))
        tt(T.msk[:, s], T.hf[:, s], T[zb][:, q1], ALU.min, ["hf" + n], ["msk" + n], [zb])
        mm(zb, T[zb][:, q3], T[Back][:], T.hit[:, s], True, False, [Back, "hit" + n])
        mm(zb, T[zb][:, q3], T.BOh[:], T.msk[:, s], False, True, ["BOh", "msk" + n])
        stage(t, DUE["named%d" % h])
        scan(T.sN[:, s], T.R2[:, q0], T[zb][:, q3], 0.0, ALU.add, ["R2"], ["sN" + n], [zb])
        ts(T.nrep[:, s], T[zb][:, q3], 256.0, None, ALU.add, w=["nrep" + n], ps=[zb])
        ts(T.oN[:, s8], T.sN[:, h * HL + 15:(h + 1) * HL:16], c("holdn"), None, ALU.subtract, r=["sN" + n, "holdn"],
           w=["oN" + n])
        act(T.tf[:, s], T.C[:, 0:CW].indirect(T.oN[:, s8]), ACT.Relu, bias=1.0 if last else ONE, scale=-2.0,
            r=["C", "oN" + n], w=["tf" + n], cost=65 + HL * GATH)
        if h in S_DZ:
            act(T.yf[:, s], T.dz[:, s], bias=-127.75, r=["dz" + n], w=["yf" + n])
        elif h in P_YF:
            mm("b6", T.b6[:, q1], T.I[:], T.zin[:, st], True, False, ["I", "zin%d_%d" % (t, h)])
            mm("b6", T.b6[:, q1], T.I[:], T.dz[:, s], False, True, ["I", "dz" + n])
            act(T.yf[:, s], T.b6[:, q1], bias=-127.75, w=["yf" + n], ps=["b6"])
        else:
            act(T.yf[:, s], win.indirect(T.oY[:, s8]), bias=-127.75, r=xk + ["oY" + n], w=["yf" + n], cost=65 + HL * GATH)
        mm(db, T[db][:, q3], T.I[:], T.Cm0[:, q0], True, False, ["I", "Cm0"])
        mm(db, T[db][:, q3], T[Back][:], T.hit[:, s], False, False, [Back, "hit" + n])
        mm(db, T[db][:, q3], T.BOh[:], T.msk[:, s], False, False, ["BOh", "msk" + n])
        cs = "Cs1" if last else "Cs"
        matches(h, T.nrep, "nrep" + n, "holdn", lambda j: T.sN[:, 16 * j + 15:16 * j + 16], "sN" + n, "E", db, 3 * HL, True,
                lambda: mm(db, T[db][:, q3], T[cs][:], T.tf[:, s], False, False, [cs, "tf" + n], True))
        scan(T.sV[:, s], T.RF[:, s], T[db][:, q3], BIG, ALU.min, ["RF"], ["sV" + n], [db])
        cp(T.oX[:, s8], T.sV[:, h * HL + 15:(h + 1) * HL:16], ["sV" + n], ["oX" + n])

    def roots(t):
        for h in (1, 0) if R_HALF else ():
            s, s8, n = half(h)
            stage(t, DUE["roots%d" % h])
            for j in range(16):
                mm("b7", T.b7[:, L:L + 8], T.SK[:, 15 - j:143 - j], T.pb[:, h * HL + j:(h + 1) * HL:16], j == 0, j == 15,
                   ["SK", "pb" + n])
            if S_PT:
                act(T.pT[:, s8], T.b7[:, L:L + 8], w=["pT" + n], ps=["b7"])
            else:
                cp(T.pT[:, s8], T.b7[:, L:L + 8], (), ["pT" + n], ["b7"])
            stage(t, DUE["twins%d" % h])
            o = slice(h * HL, (h + 1) * HL)
            mm("b7", T.b7[:, o], T.I[:], T.Cm1[:, s], True, False, ["I", "Cm1"])
            mm("b7", T.b7[:, o], T.R15[:], T.hf[:, s], False, False, ["R15", "hf" + n])
            matches(h, T.pb, "pb" + n, None, lambda j: T.pT[:, j:j + 1], "pT" + n, "E2", "b7", h * HL, True)
            if h == 0:
                scan(T.sU[:], T.RF[:], T.b7[:, 0:L], BIG, ALU.min, ["RF"], ["sU"], ["b7"])
                cp(T.oR[:], T.sU[:, 15:L:16], ["sU"], ["oR"])
        if R_HALF:
            return
        stage(t, DUE["roots"])
        for j in range(16):
            mm("b7", T.b7[:, L:L + 16], T.SK[:, 15 - j:143 - j], T.pb[:, j:L:16], j == 0, j == 15, ["SK"] + both("pb"))
        if S_PT:
            act(T.pT[:], T.b7[:, L:L + 16], w=["pT"], ps=["b7"])
        else:
            cp(T.pT[:], T.b7[:, L:L + 16], (), ["pT"], ["b7"])
        stage(t, DUE["twins"])
        mm("b7", T.b7[:, 0:L], T.I[:], T.Cm1[:], True, False, ["I", "Cm1"])
        mm("b7", T.b7[:, 0:L], T.R15[:], T.hf[:], False, False, ["R15"] + both("hf"))
        for h in (1, 0):
            matches(h, T.pb, "pb_%d" % h, None, lambda j: T.pT[:, j:j + 1], "pT", "E2", "b7", h * HL, h == 0)
        scan(T.sU[:], T.RF[:], T.b7[:, 0:L], BIG, ALU.min, ["RF"], ["sU"], ["b7"])
        cp(T.oR[:], T.sU[:, 15:L:16], ["sU"], ["oR"])

    def means(t, xk):
        stage(t, DUE["means"])
        mm("b6", T.b6[:, L:2 * L], T.H[:], T.xk[:, 15:W:16], True, False, ["H"] + xk)
        mm("b6", T.b6[:, L:2 * L], T.H[:], T.zin[:, t * L:(t + 1) * L], False, True, ["H"] + both("zin%d" % t))
        act(T.af[:], T.b6[:, L:2 * L], bias=-64.1, w=["af"], ps=["b6"])

    stage(-1, DUE["paths1"])
    paths(0, 1)
    for t in range(STEPS):
        last = t == STEPS - 1
        zt = slice(t * L, (t + 1) * L)
        stage(t, DUE["paths0"])
        paths(t, 0)
        xk1 = records(t, 1)
        answers(t, 1, xk1)
        xk0 = records(t, 0)
        answers(t, 0, xk0)
        means(t, xk0 + xk1)
        roots(t)
        stage(t, DUE["home"])
        if t in (1, 2):
            send((rank - D * t) % N, T.zhome[:, (t - 1) * L:t * L], T.zout[:, zt], "harr%d" % t, both("zout%d" % t), 128 * 512)
            arrival("zhome%d" % t, "harr%d" % t, len(topo.engines(T.cores[(rank + D * t) % N], core)))
            dma("y", T.zs[:, zt], T.zhome[:, (t - 1) * L:t * L], ["zhome%d" % t], (), "out")
        if t == 0 or last:
            dma("y", T.zs[:, zt], T.zout[:, zt], both("zout%d" % t), (), "out")
        if last:
            dma("y", T.zs[:, 3 * L:4 * L], T.zin[:, zt], both("zin%d" % t), (), "out")
        else:
            stage(t, DUE["bound"])
            mm("b4", T.b4[:, HL:HL + 2], T.sel14[:], T.acc[:, 0:2], True, True, ["sel14"] + both("acc"), True)
            ts(T.ai[:, 0:1], T.b4[:, HL:HL + 1], T.b4[:, HL + 1:HL + 2], None, ALU.add, w=["ai0"], ps=["b4"])
            ts(T.ai[:, 1:2], T.ai[:, 0:1], 15, None, ALU.bitwise_and, r=["ai0"], w=["ai1"])
            ts(c("M"), T.ai[:, 1:2], c("th"), None, ALU.add, r=["ai1", "th"], w=["M"])
        stage(t, DUE["write"])
        for h in (1, 0):
            s, s8, n = half(h)
            scatter(T.X[:, 0:XW], T.oX[:, s8], T.yf[:, s], HL, ["oX" + n, "yf" + n], ["X"])
        for h in (1, 0):
            s, s8, n = half(h)
            scatter(T.X[:, 0:CW], T.oR[:, s8], T.af[:, s], HL, ["oR", "af"], ["X"])
        stage(t, DUE["counters"])
        ts(T.tt[:, 0:16], T.sV[:, 15:L:16], CW - 0.5, -float(AWAY), ALU.is_gt, ALU.mult, r=both("sV"), w=["tt0"])
        tt(T.tt[:, 16:32], T.tt[:, 0:16], T.sV[:, 15:L:16], ALU.add, both("sV") + ["tt0"], ["tt1"])
        cp(T.oC[:], T.tt[:, 16:32], ["tt1"], ["oC"])
        stage(t, DUE["count"])
        for h in (1, 0):
            s, s8, n = half(h)
            if last:
                add("v", lambda s=s, s8=s8: g.vector.tensor_copy(T.C2[:, 0:CW].indirect(T.oC[:, s8]), T.tf[:, s]),
                    ["oC", "tf" + n], ["C2"], (), 50 + HL * SCAT)
            else:
                scatter(T.C[:, 0:CW], T.oC[:, s8], T.tf[:, s], HL, ["oC", "tf" + n], ["C"])
        if t == STEPS - 2:
            dma("g", T.Cb[0:128:16, :], T.C[0:128:16, BASE:CW], ["C"], ["Cb"], "lb", 8 * W * 4)
            dma("g", T.C2[0:128:16, BASE:CW], T.Cb[0:128:16, :], ["Cb"], ["C2"], "l2", 8 * W * 4)
        if not last:
            stage(t, DUE["paths1"])
            paths(t + 1, 1)

    stage(STEPS - 1, DUE["sums"])
    dma("y", T.cs[:, 0:TURN], T.C2[0:128:16, CW - TURN:CW], ["C2"], (), "out", 8 * W * 4)
    dma("y", T.cs[:, TURN:W], T.C2[0:128:16, BASE:CW - TURN], ["C2"], (), "out", 8 * W * 4)
    for i in range(W // L):
        cuts = [i * L] + ([TURN] if TURN // L == i else []) + [(i + 1) * L]
        names = []
        for a, b in zip(cuts, cuts[1:]):
            p = BASE + (a - TURN) % W
            names.append("xe%d" % a)
            if i % 2:
                ts(T.xb[:, a:b], T.X[:, p:p + b - a], 128.0, None, ALU.add, r=["X"], w=names[-1:])
            else:
                act(T.xb[:, a:b], T.X[:, p:p + b - a], bias=128.0, r=["X"], w=names[-1:])
        h, b = i // 8, ("b7", "b5")[i // 8]
        for j in (2 * i % 16, 2 * i % 16 + 1):
            a = h * W // 2 + j * HL
            mm(b, T[b][:, q0], T.SA[:, 15 - j:143 - j], T.xb[:, a:a + HL], j == 0, j == 15, ["SA"] + names)
        if i % 8 == 7:
            s, _, n = half(h)
            if h:
                ts(T.xo[:, s], T[b][:, q0], 4.0, c("asum"), ALU.mult, ALU.add, r=["asum"], w=["xo" + n], ps=[b])
            else:
                act(T.xo[:, s], T[b][:, q0], bias=c("asum"), scale=4.0, r=["asum"], w=["xo" + n], ps=[b])
            dma("y", T.xs[:, h * W // 2:(h + 1) * W // 2], T.xo[:, s], ["xo" + n], (), "out")

    if not ORDER:
        ORDER.extend(put_in_order(ops))
    order = ORDER
    place = {i: p for p, i in enumerate(order)}
    needed = set()
    for o in ops:
        best = {}
        for j in o["deps"]:
            if ops[j]["sem"] is None and place[j] > place.get(best.get(ops[j]["q"]), -1):
                best[ops[j]["q"]] = j
        needed.update(best.values())
    count, total = {}, {}
    for i in order:
        o = ops[i]
        s = o["sem"] if o["sem"] is not None else "q" + o["q"]
        if o["sem"] is not None or i in needed:
            total[s] = total.get(s, 0) + (o["inc"] if o["sem"] is not None else 1)
        count[i] = (s, total.get(s, 0))
    seen, most = {}, {}
    for i in order:
        o = ops[i]
        q = o["q"]
        if q is None:
            continue
        want = {}
        for j in o["deps"]:
            if ops[j]["sem"] is None and j not in needed:
                continue
            s, n = count[j]
            want[s] = max(want.get(s, 0), n)
        for s in sorted(want):
            if want[s] > seen.get((q, s), 0):
                Q[q].wait_ge(T.sem[s], want[s])
                seen[(q, s)] = want[s]
                most[s] = max(most.get(s, 0), want[s])
        ins = o["fn"]()
        if o["sem"] == "-":
            continue
        if o["sem"] is not None:
            ins.then_inc(T.sem[o["sem"]], o["inc"])
        elif i in needed:
            ins.then_inc(T.sem["q" + q], 1)
    g.wait_ge(T.sem.sent, nsent[0])
    for s in sorted(total):
        if s not in ("-", "out") and most.get(s, 0) < total[s]:
            g.wait_ge(T.sem[s], total[s])
    g.wait_ge(T.sem.out, total["out"])
